import numpy as np, ml_dtypes
CORES = [35,38,43,46]
N = 4
import mx_ref
BF = ml_dtypes.bfloat16
def entries(a):
    return np.ascontiguousarray(a.T).reshape(-1)
def table(e):
    return np.ascontiguousarray(np.reshape(e, (-1, 16)).T).astype(np.int32)
def cols(t, e):
    v = np.concatenate([t.reshape(128, -1, 4), np.zeros((128, 1, 4), BF)], axis=1)
    return np.ascontiguousarray(v[:, e]).reshape(128, -1)
def f(rng, *shape):
    return mx_ref.flush((rng.standard_normal(shape, dtype=np.float32) * np.exp2(rng.integers(-2, 3, shape[:-1] + (1,)))).astype(BF))
def wide(rng, *shape, cols=0):
    v = rng.standard_normal(shape, dtype=np.float32) * np.exp2(rng.integers(-12, 13, shape)).astype(np.float32)
    if cols: v *= np.repeat(np.exp2(rng.integers(-cols, cols + 1, shape[:-2] + (1, shape[-1] // 4))) * (rng.random(shape[:-2] + (1, shape[-1] // 4)) > 0.0625), 4, axis=-1).astype(np.float32)
    return mx_ref.flush(v.astype(BF))
T, S, O, CAPP = 512, 768, 2, (256, 480)
B = len(CAPP)
def wanters(q, b):
    return sum(1 << e for e in range(N) if (e ^ q ^ (1 << b)) % (2 << b) == 0)
def holders(q, b):
    return (q >> b) << b, ((q >> b) + 1) << b
def limit(rng, m, keep, lo, hi, s, most):
    v = m.reshape(-1)
    e = np.flatnonzero(v[lo * T:hi * T] & s) + lo * T
    e = e[np.argsort(rng.random(len(e)) - ((keep.reshape(-1)[e] & s) != 0))][most:]
    v[e] &= ~s
def masks(rng, keep=None, off=None, share=0.55):
    keep = np.zeros((N, T), int) if keep is None else keep
    off = np.zeros((N, T), bool) if off is None else off
    for r in range(N):
        if not ((keep >> r) & 1).any(): keep[r, rng.choice(np.flatnonzero(~off[r]))] |= 1 << r
    n = rng.integers(1, 4, (N, T)) * (rng.random((N, T)) < share)
    m = ((np.argsort(rng.random((N, T, N)), axis=2) < n[:, :, None]) * (1 << np.arange(N))).sum(axis=2)
    m = np.ascontiguousarray(np.where(off, 0, m) | keep)
    for b in range(B):
        for q in range(N): limit(rng, m, keep, *holders(q, b), wanters(q, b), CAPP[b])
    for r in range(N): limit(rng, m, keep, 0, N, 1 << r, S)
    return {"dm": np.stack([table(v) for v in m])}
def setup_inputs(rng):
    return {"x": f(rng, N, 128, 4 * T), **masks(rng), "w": f(rng, N, 128, 512 * O)}
def setup_inputs_comb(rng):
    k = np.zeros((N, T), int); c = np.arange(T); s = int(rng.integers(0, 16)); p = int(rng.integers(0, N)); g = p ^ (N >> 1)
    for e in range(N): k[:, (c - e - s) % 4 == 0] |= 1 << e
    lo, hi = holders(p, B - 1)
    k[lo:hi] &= ~(1 << g)
    k[p, c % 16 != s] |= 1 << g
    assert not check_inputs({"dm": np.stack([table(v) for v in k])})
    return {**setup_inputs(rng), **masks(rng, k)}
def setup_inputs_turn(rng):
    k = np.zeros((N, T), int); g = int(rng.integers(0, N))
    k[g ^ 1, rng.permutation(T)[:CAPP[0]]] |= 1 << g
    k[g ^ 3, rng.permutation(T)[:CAPP[0]]] |= 1 << g
    h = rng.permutation(T)
    k[g, h[:CAPP[0]]] |= 1 << (g ^ 3)
    k[g, h[CAPP[0]:2 * CAPP[0]]] |= 1 << (g ^ 2)
    if N == 8: k[g ^ 6, rng.permutation(T)[:CAPP[1]]] |= 1 << (g ^ 4)
    return {**setup_inputs(rng), **masks(rng, k)}
def setup_inputs_none(rng):
    z = np.zeros((N, T), bool); k = np.zeros((N, T), int); p = int(rng.integers(0, N))
    for r in range(N): z[r, rng.permutation(T)[:T // 2]] = True
    k[p ^ 1, rng.choice(np.flatnonzero(~z[p ^ 1]))] |= 1 << p
    d = {**setup_inputs(rng), **masks(rng, k, off=z, share=1)}
    d["dm"][p] = 0
    return d
def setup_inputs_full(rng):
    k = np.zeros((N, T), int); g = int(rng.integers(0, N)); s = int(rng.integers(0, T))
    k[g ^ 1, (np.arange(CAPP[0]) + s) % T] |= 1 << (g ^ 2)
    k[g, (np.arange(S - sum(CAPP[1:])) + s) % T] |= 1 << g
    for b in range(1, B):
        for r in range(N):
            if r >> b == (g >> b) ^ 1: k[r, (np.arange(CAPP[b] >> b) + s) % T] |= 1 << g
    assert not check_inputs({"dm": np.stack([table(v) for v in k])})
    return {**setup_inputs(rng), **masks(rng, k, share=1)}
def setup_inputs_spread(rng):
    d = setup_inputs(rng); d["x"] = wide(rng, N, 128, 4 * T, cols=8); return d
def check_inputs(d):
    bad = []
    m = np.stack([entries(v) for v in d["dm"]]).astype(np.int64)
    if m.min() < 0 or m.max() >= 1 << N: bad.append("dm")
    for r in range(N):
        if ((m >> r) & 1).sum() > S: bad.append("arrivals")
    for b in range(B):
        for q in range(N):
            lo, hi = holders(q, b)
            if ((m[lo:hi] & wanters(q, b)) != 0).sum() > CAPP[b]: bad.append("CAPP_" + str(b))
    return bad
def reference(x, dm, w):
    m = np.stack([entries(v) for v in dm])
    every = np.concatenate(list(x), axis=1)
    y = np.zeros((N, 128, O * S), np.float32); ln = np.zeros((N, 1, 2), np.float32)
    for r in range(N):
        e = np.flatnonzero((m.reshape(-1) >> r) & 1); n = len(e)
        k = np.full(S, -1); k[:n] = e
        a = mx_ref.quantize(cols(every, k))
        for o in range(O):
            y[r][:, S * o:S * o + n] = mx_ref.matmul(mx_ref.quantize(np.ascontiguousarray(w[r][:, 512 * o:512 * o + 512])), a)[:, :n]
        ln[r, 0, 0] = n; ln[r, 0, 1] = np.count_nonzero((m[r] >> r) & 1)
    return {"y": y, "ln": ln}

@@ -1,0 +1,430 @@
+import numpy as np
+from concourse.bass import DstId, RemoteDMATransfer
+from concourse.mybir import dt, AluOpType, AxisListType, ActivationFunctionType
+
+T_, S_, C0, C1 = 512, 768, 256, 480
+EARLY = C1 - C0
+BIG = 32768.0
+RW = T_ + C0 + C1 + 32
+ZC = T_ + C0 + C1
+
+F32, I32, U16, BF = "float32", "int32", "uint16", "bfloat16"
+Q4, U8 = "float8_e4m3fn_x4", "uint8"
+
+
+def sb(n, d):
+    return ("sbuf", [128, n], d)
+
+
+SCRATCH = {
+    "dmt": sb(40, I32), "dmp": sb(40, I32),
+    "xt": sb(2048, BF), "wt": sb(1024, BF),
+    "xq": sb(512, Q4), "xs": sb(512, U8), "wq": sb(256, Q4), "ws": sb(256, U8),
+    "xwq": sb(768, Q4), "xws": sb(768, U8),
+    "p0q": sb(256, Q4), "p0s": sb(256, U8),
+    "peq": sb(EARLY, Q4), "pes": sb(EARLY, U8), "plq": sb(256, Q4), "pls": sb(256, U8),
+    "leq": sb(EARLY, Q4), "les": sb(EARLY, U8), "llq": sb(256, Q4), "lls": sb(256, U8),
+    "zero": sb(512, F32), "one": sb(96, F32), "rst": sb(96, F32),
+    "pi": sb(2, I32), "pint": sb(8, I32), "pf": sb(8, F32),
+    "val0": sb(256, F32), "val": sb(256, F32), "tb0": sb(32, F32), "i480": sb(48, F32), "i48": sb(48, F32),
+    "d0": sb(32, F32), "du": sb(32, F32), "df": sb(64, F32),
+    "ta": sb(16, I32), "tb": sb(16, I32), "tc": sb(48, I32),
+    "z1": sb(160, F32), "zt1": sb(128, F32), "car1": sb(2, F32), "pt1": sb(64, F32), "m1": sb(64, F32), "a1": sb(64, F32),
+    "ab1": sb(32, I32), "an1": sb(32, I32), "f1": sb(32, F32), "g1": sb(32, F32), "h1": sb(32, F32), "o1": sb(32, U16),
+    "win0": sb(768, F32), "t0": sb(512, F32), "y0": sb(32, F32), "yt0": sb(32, F32), "yu0": sb(32, F32), "off0": sb(16, U16),
+    "slu": sb(32, U16), "slin": sb(32, U16), "slf": sb(32, F32), "vp": sb(256, F32),
+    "z2": sb(224, F32), "zt2": sb(192, F32), "car2": sb(4, F32), "pt2": sb(96, F32), "m2": sb(96, F32),
+    "au": sb(32, I32), "anu": sb(32, I32), "fu": sb(32, F32), "gu": sb(32, F32), "hu": sb(32, F32), "ou": sb(32, U16),
+    "winu": sb(1216, F32), "tu": sb(960, F32), "yu": sb(32, F32), "ytu": sb(32, F32), "yuu": sb(32, F32), "offu": sb(32, U16),
+    "rsum": sb(32, F32), "rst_t": sb(32, F32), "rtot": sb(1, F32), "rexp": sb(32, F32), "tot": sb(32, F32),
+    "cf": sb(4, F32), "cg": sb(4, F32), "ocol": sb(2, F32),
+    "la": sb(16, F32), "lm": sb(16, F32), "lb": sb(16, F32), "lc": sb(16, F32), "offl": sb(16, U16),
+    "sc": sb(32, F32), "lnt": sb(2, F32),
+    "xf": sb(64, F32), "af": sb(64, I32), "lof": sb(64, I32), "hif": sb(64, I32), "lo48": sb(64, F32), "plf": sb(64, F32),
+    "mlf": sb(64, F32), "tf": sb(64, F32), "of": sb(64, U16), "winf": sb(1024, F32), "off2": sb(96, F32),
+    "fx": sb(48, F32), "fy": sb(48, F32), "fz": sb(48, F32), "fin": sb(48, F32), "fr": sb(48, F32), "fe": sb(48, F32),
+    "fs": sb(48, F32), "fl": sb(48, F32), "fl2": sb(48, F32), "offf": sb(48, U16),
+    "res0": sb(RW, F32), "res1": sb(RW, F32), "yt_0": sb(768, F32), "yt_1": sb(768, F32),
+    "ps": ("psum", [128, 4096], F32),
+}
+SEMAPHORES = ["sv", "sa", "st", "sg", "dml", "xl0", "xl1", "wl", "xw", "vps", "wr", "yst",
+              "aDM", "aS0", "aSL", "aCNT", "aE", "aL", "loc"]
+
+
+def rank_program(g, core, T, topo):
+    q = T.rank_of(core)
+    if q is None:
+        return
+    A = AluOpType
+    AF = ActivationFunctionType
+    X = AxisListType.X
+    rp, rf, rg = q ^ 1, q ^ 2, q ^ 3
+    cp, cf_, cg_ = T.cores[rp], T.cores[rf], T.cores[rg]
+    P, Fb, G, Qb = 1 << rp, 1 << rf, 1 << rg, 1 << q
+    s = T.sem
+    cnt = {"sv": 0, "sa": 0, "st": 0, "sg": 0, "loc": 0}
+    seen = {}
+
+    def wait(name, eng, sem, n):
+        if n > 0 and seen.get((name, sem), 0) < n:
+            seen[(name, sem)] = n
+            eng.wait_ge(s[sem], n)
+
+    def V(ins, par=False):
+        if not par:
+            wait("v", g.vector, "sv", cnt["sv"])
+        r = ins()
+        cnt["sv"] += 1
+        r.then_inc(s.sv, 1)
+        return cnt["sv"]
+
+    def SA(ins):
+        wait("a", g.scalar, "sa", cnt["sa"])
+        r = ins()
+        cnt["sa"] += 1
+        r.then_inc(s.sa, 1)
+        return cnt["sa"]
+
+    def ts(out, in0, s1, s2, op0, op1=None, par=False):
+        if op1 is None:
+            return V(lambda: g.vector.tensor_scalar(out, in0, s1, s2, op0), par)
+        return V(lambda: g.vector.tensor_scalar(out, in0, s1, s2, op0, op1), par)
+
+    def tt(out, a, b, op, par=False):
+        return V(lambda: g.vector.tensor_tensor(out, a, b, op), par)
+
+    def cpy(out, in_, par=False):
+        return V(lambda: g.vector.tensor_copy(out, in_), par)
+
+    def tr(out, in_, par=False):
+        return V(lambda: g.vector.transpose(out, in_), par)
+
+    def red(out, in_, par=False):
+        return V(lambda: g.vector.tensor_reduce(out, in_, X, A.add), par)
+
+    def scan(out, d0, d1, init, par=False):
+        return V(lambda: g.vector.tensor_tensor_scan(out, d0, d1, init, A.mult, A.add), par)
+
+    def fill(ap, c, par=True):
+        return V(lambda: g.vector.memset(ap, c), par)
+
+    def act(out, in_, scale=1.0, bias=0.0):
+        if scale == 1.0 and bias == 0.0:
+            return SA(lambda: g.scalar.activation(out, in_, AF.Copy))
+        return SA(lambda: g.scalar.activation(out, in_, AF.Copy, bias=bias, scale=scale))
+
+    def send(dst, out, in_, rsem):
+        rid, pid, _se = topo.addr(dst)
+        g.remote_dma(out_ap=out, in_ap=in_, remote_sem=s[rsem], local_sem=s.loc, pid=pid, routing_id=rid,
+                     dma_engine_mask=topo.mask(core, dst))
+        cnt["loc"] += len(topo.engines(core, dst))
+
+    ncp, nmf = len(topo.engines(core, cp)), len(topo.engines(core, cf_))
+
+    def b8(ap):
+        return ap.bitcast(dt.uint8)
+
+    def b32(ap):
+        return ap.bitcast(dt.uint32)
+
+    for k in range(8):
+        e = g.sync if k % 2 == 0 else g.scalar
+        o = 1 - k % 2
+        e.dma_start(T.dmt[16 * k:16 * k + 16, o:o + 32], T.dm[:, :]).then_inc(s.dml, 16)
+    g.sync.dma_start(T.xt[:, 0:1024], T.x[:, 0:1024]).then_inc(s.xl0, 16)
+    g.scalar.dma_start(T.xt[:, 1024:2048], T.x[:, 1024:2048]).then_inc(s.xl1, 16)
+    g.scalar.dma_start(T.wt[:], T.w[:]).then_inc(s.wl, 16)
+
+    def I(ins):
+        ins().then_inc(s.sg, 1)
+        cnt["sg"] += 1
+    I(lambda: g.iota(T.pi[:, 0:1], [[1, 1]], 0, 1))
+    I(lambda: g.iota(T.tb0[:], [[0, 2], [1, 16]], 0, 0, allow_small_or_imprecise_dtypes=True))
+    I(lambda: g.iota(T.val0[:], [[32, 16], [1, 16]], 0, 0, allow_small_or_imprecise_dtypes=True))
+    I(lambda: g.iota(T.i480[:], [[16, 48]], 0, 0, allow_small_or_imprecise_dtypes=True))
+    g.wait_ge(s.dml, 128)
+    send(cp, T.dmp[:, 1:32], T.dmt[:, 1:32], "aDM")
+
+    nz = fill(T.zero[:], 0.0)
+    fill(T.z1[:], 0.0)
+    fill(T.z2[:], 0.0)
+    fill(T.one[:], 1.0)
+    fill(T.rst[:], 1.0)
+    fill(T.y0[:], 0.0)
+    fill(T.yu[:], 0.0)
+    fill(T.rsum[:], 0.0)
+    fill(T.win0[:, 0:512], 0.0)
+    nfill = fill(T.z1[:, 31:32], -1.0 / 32, par=False)
+    fill(T.z1[:, 63:64], C0 / 32.0)
+    for c in (31, 63, 95):
+        fill(T.z2[:, c:c + 1], -1.0 / 32)
+    fill(T.rst[:, 32:33], 0.0)
+    fill(T.rst[:, 64:65], 0.0)
+    fill(T.vp[:], 0.0)
+    fill(T.res0[:, ZC:RW], 0.0)
+    fill(T.res1[:, ZC:RW], 0.0)
+    g.vector.wait_ge(s.sg, 4)
+    ts(T.pint[:, 0:1], T.pi[:, 0:1], 16, None, A.bitwise_and, par=True)
+    ts(T.pint[:, 1:2], T.pi[:, 0:1], 31, None, A.bitwise_and, par=True)
+    ts(T.pint[:, 2:3], T.pi[:, 0:1], 15, None, A.bitwise_and, par=True)
+    ts(T.pf[:, 0:1], T.pint[:, 0:1], 1.0, None, A.mult)
+    ts(T.pf[:, 1:2], T.pint[:, 1:2], 16.0, None, A.mult, par=True)
+    ts(T.pf[:, 2:3], T.pint[:, 2:3], 1.0, None, A.mult, par=True)
+    ts(T.d0[:], T.tb0[:], T.pf[:, 1:2], 512.0, A.add, A.add)
+    ts(T.du[:], T.tb0[:], T.pf[:, 1:2], 960.0, A.add, A.add, par=True)
+    ts(T.df[:, 0:32], T.tb0[:], T.pf[:, 1:2], 768.0, A.add, A.add, par=True)
+    ts(T.df[:, 32:64], T.tb0[:], T.pf[:, 1:2], 768.0, A.add, A.add, par=True)
+    ts(T.val[:], T.val0[:], T.pf[:, 0:1], None, A.add, par=True)
+    ts(T.i48[:], T.i480[:], T.pf[:, 2:3], None, A.add, par=True)
+
+    wait("a", g.scalar, "sv", cnt["sv"])
+    act(T.winu[:, 0:512], T.zero[:, 0:512])
+    act(T.winu[:, 512:960], T.zero[:, 0:448])
+    act(T.winf[:, 0:512], T.zero[:, 0:512])
+    nwin = act(T.winf[:, 512:768], T.zero[:, 0:256])
+
+    g.vector.wait_ge(s.dml, 128)
+    dv = T.dmt[:, 1:33:2]
+    ts(T.ta[:], dv, G, None, A.bitwise_and, par=True)
+    ts(T.tb[:], dv, P | G, None, A.bitwise_and, par=True)
+    ts(T.z1[:, 32:48], T.ta[:], 0.0, None, A.is_gt)
+    ts(T.z1[:, 64:80], T.tb[:], float(P), -1.0, A.is_equal, A.mult, par=True)
+    scan(T.z1[:, 96:144], T.rst[:, 0:48], T.z1[:, 31:79], 0.0)
+    ntr = tr(T.zt1[:], T.z1[:, 32:160])
+    wait("a", g.scalar, "sv", ntr)
+    act(T.m1[:, 0:32], T.zt1[:, 0:32], -BIG, BIG)
+    nm1 = act(T.m1[:, 32:64], T.zt1[:, 32:64], BIG, BIG)
+    red(T.car1[:, 0:1], T.zt1[:, 64:96])
+    red(T.car1[:, 1:2], T.zt1[:, 96:128], par=True)
+    scan(T.pt1[:, 0:32], T.one[:, 0:32], T.zt1[:, 0:32], T.car1[:, 0:1])
+    scan(T.pt1[:, 32:64], T.one[:, 0:32], T.zt1[:, 32:64], T.car1[:, 1:2], par=True)
+    wait("v", g.vector, "sa", nm1)
+    tt(T.a1[:], T.pt1[:], T.m1[:], A.max)
+    tt(T.ab1[:], T.a1[:, 0:32], T.a1[:, 32:64], A.min)
+    ts(T.an1[:], T.ab1[:], 65520, None, A.bitwise_and)
+    tt(T.f1[:], T.ab1[:], T.an1[:], A.add)
+    tt(T.g1[:], T.f1[:], T.d0[:], A.min)
+    tr(T.h1[:], T.g1[:])
+    cpy(T.o1[:], T.h1[:])
+    cpy(T.win0[:, 0:768].indirect(T.o1[:, 0:16]), T.val[:])
+    tr(T.t0[:], T.win0[:, 0:512])
+    tt(T.y0[:, 0:16], T.t0[:, 0:512:32], T.t0[:, 16:512:32], A.add)
+    tr(T.yt0[:], T.y0[:])
+    cpy(T.yt0[:, 16:32], T.yt0[:, 0:16])
+    tr(T.yu0[:], T.yt0[:])
+    cpy(T.off0[:], T.yu0[:, 0:16])
+    g.vector.wait_ge(s.xl0, 16)
+    V(lambda: g.vector.quantize_mx(T.xq[:, 0:256], T.xs[:, 0:256], T.xt[:, 0:1024]), True)
+    g.vector.wait_ge(s.xl1, 16)
+    nxq = V(lambda: g.vector.quantize_mx(T.xq[:, 256:512], T.xs[:, 256:512], T.xt[:, 1024:2048]), True)
+    nq0 = cpy(b32(T.p0q[:]), b32(T.xq[:]).indirect(T.off0[:]))
+    wait("a", g.scalar, "sv", nxq)
+    na0 = SA(lambda: g.scalar.activation(T.p0s[:], T.xs[:].indirect(T.off0[:]), AF.Copy))
+    wait("s", g.sync, "sv", nxq)
+    g.sync.dma_start(b8(T.xwq[:, 0:512]), b8(T.xq[:, 0:512])).then_inc(s.xw, 16)
+    g.sync.dma_start(T.xws[:, 0:512], T.xs[:, 0:512]).then_inc(s.xw, 16)
+    wait("g", g, "sv", nq0)
+    send(cp, b8(T.xwq[:, 512:768]), b8(T.p0q[:]), "aS0")
+    wait("g", g, "sa", na0)
+    send(cp, T.xws[:, 512:768], T.p0s[:], "aS0")
+
+    ts(T.tc[:, 0:16], dv, Fb, None, A.bitwise_and)
+    ts(T.tc[:, 16:32], dv, Qb, None, A.bitwise_and, par=True)
+    g.vector.wait_ge(s.aDM, ncp)
+    ts(T.tc[:, 32:48], T.dmp[:, 1:33:2], Qb, None, A.bitwise_and, par=True)
+    for k in range(3):
+        ts(T.z2[:, 32 + 32 * k:48 + 32 * k], T.tc[:, 16 * k:16 * k + 16], 0.0, None, A.is_gt, par=k > 0)
+    scan(T.z2[:, 128:208], T.rst[:, 0:80], T.z2[:, 31:111], 0.0)
+    ntr2 = tr(T.zt2[:], T.z2[:, 32:224])
+    wait("a", g.scalar, "sv", ntr2)
+    nm2 = act(T.m2[:], T.zt2[:, 0:96], -BIG, BIG)
+    for k in range(3):
+        red(T.car2[:, k:k + 1], T.zt2[:, 96 + 32 * k:128 + 32 * k], par=k > 0)
+    for k in range(3):
+        scan(T.pt2[:, 32 * k:32 * k + 32], T.one[:, 0:32], T.zt2[:, 32 * k:32 * k + 32], T.car2[:, k:k + 1], par=k > 0)
+    wait("v", g.vector, "sa", nm2)
+    tt(T.au[:], T.pt2[:, 0:32], T.m2[:, 0:32], A.max)
+    ts(T.anu[:], T.au[:], 65520, None, A.bitwise_and)
+    tt(T.fu[:], T.au[:], T.anu[:], A.add)
+    tt(T.gu[:], T.fu[:], T.du[:], A.min)
+    tr(T.hu[:], T.gu[:])
+    cpy(T.ou[:], T.hu[:])
+    cpy(T.winu[:, 0:1216].indirect(T.ou[:, 0:16]), T.val[:])
+    tr(T.tu[:], T.winu[:, 0:960])
+    tt(T.yu[:, 0:30], T.tu[:, 0:960:32], T.tu[:, 16:960:32], A.add)
+    tr(T.ytu[:], T.yu[:])
+    cpy(T.ytu[:, 16:32], T.ytu[:, 0:16])
+    tr(T.yuu[:], T.ytu[:])
+    noffu = cpy(T.offu[:], T.yuu[:])
+    npe = cpy(b32(T.peq[:]), b32(T.xq[:]).indirect(T.offu[:, 0:14]))
+    wait("a", g.scalar, "sv", noffu)
+    nae = SA(lambda: g.scalar.activation(T.pes[:], T.xs[:].indirect(T.offu[:, 0:14]), AF.Copy))
+    nsl = cpy(T.slu[:], T.ab1[:], par=True)
+    red(T.rsum[:, 0:1], T.z2[:, 32:48])
+    red(T.rsum[:, 1:2], T.z1[:, 32:48], par=True)
+    red(T.rsum[:, 2:3], T.z2[:, 64:80], par=True)
+    red(T.rsum[:, 3:4], T.z2[:, 96:112], par=True)
+    tr(T.rst_t[:], T.rsum[:])
+    red(T.rtot[:], T.rst_t[:])
+    ts(T.rexp[:], T.zero[:, 0:32], T.rtot[:], None, A.add)
+    ntot = tr(T.tot[:], T.rexp[:])
+    ts(T.ocol[:, 0:1], T.tot[:, 0:1], -float(EARLY), 0.0, A.add, A.max)
+    ts(T.la[:], T.i48[:, 0:16], T.ocol[:, 0:1], float(T_), A.subtract, A.add)
+    ts(T.lm[:], T.i48[:, 0:16], T.ocol[:, 0:1], None, A.is_ge, par=True)
+    tt(T.lb[:], T.la[:], T.lm[:], A.mult)
+    tt(T.lc[:], T.lb[:], T.yuu[:, 14:30], A.add)
+    noffl = cpy(T.offl[:], T.lc[:])
+    g.vector.wait_ge(s.xw, 32)
+    g.vector.wait_ge(s.aS0, 2 * ncp)
+    npl = cpy(b32(T.plq[:]), b32(T.xwq[:]).indirect(T.offl[:]))
+    wait("a", g.scalar, "sv", noffl)
+    g.scalar.wait_ge(s.xw, 32)
+    g.scalar.wait_ge(s.aS0, 2 * ncp)
+    nal = SA(lambda: g.scalar.activation(T.pls[:], T.xws[:].indirect(T.offl[:]), AF.Copy))
+
+    wait("g", g, "sv", npe)
+    send(cf_, b8(T.leq[:]), b8(T.peq[:]), "aE")
+    wait("g", g, "sa", nae)
+    send(cf_, T.les[:], T.pes[:], "aE")
+    wait("g", g, "sv", nsl)
+    send(cp, T.slin[:], T.slu[:], "aSL")
+    wait("g", g, "sv", ntot)
+    send(cf_, T.cf[:], T.tot[:, 0:4], "aCNT")
+    send(cg_, T.cg[:], T.tot[:, 0:4], "aCNT")
+    wait("g", g, "sv", npl)
+    send(cf_, b8(T.llq[:]), b8(T.plq[:]), "aL")
+    wait("g", g, "sa", nal)
+    send(cf_, T.lls[:], T.pls[:], "aL")
+
+    g.vector.wait_ge(s.wl, 16)
+    nwq = V(lambda: g.vector.quantize_mx(T.wq[:], T.ws[:], T.wt[:]), True)
+    g.vector.wait_ge(s.aSL, ncp)
+    nslf = ts(T.slf[:], T.slin[:], float(T_), None, A.add, par=True)
+    wait("s", g.sync, "sv", nslf)
+    for k in range(8):
+        a, h = k // 2, k % 2
+        g.sync.dma_start(T.vp[16 * k:16 * k + 1, :], T.slf[32 * a:32 * a + 16, 16 * h:16 * h + 16]).then_inc(s.vps, 16)
+    g.vector.wait_ge(s.aCNT, 2 * nmf)
+    u, v, nq, npq = T.cf[:, 0:1], T.cg[:, 1:2], T.tot[:, 2:3], T.tot[:, 3:4]
+    col = [0]
+
+    def c1():
+        col[0] += 1
+        return T.sc[:, col[0] - 1:col[0]]
+    nl, nf, na_ = c1(), c1(), T.lnt[:, 0:1]
+    tt(nl, nq, npq, A.add)
+    tt(nf, u, v, A.add, par=True)
+    cpy(T.lnt[:, 1:2], nq, par=True)
+    nln = tt(na_, nl, nf, A.add)
+    local_first = q < rf
+    own_first = q < rp
+    if local_first:
+        b_own = None if own_first else npq
+        b_p = nq if own_first else None
+    else:
+        sh = c1()
+        tt(sh, nf, nq if own_first else npq, A.add, par=True)
+        b_own, b_p = (nf, sh) if own_first else (sh, nf)
+    for k, b in ((0, b_own), (1, b_p)):
+        o = T.xf[:, 32 * k:32 * k + 32]
+        i = T.pt2[:, 32 + 32 * k:64 + 32 * k]
+        if b is None:
+            cpy(o, i, par=k > 0)
+        else:
+            ts(o, i, b, None, A.add, par=k > 0)
+    tt(T.af[:], T.xf[:], T.m2[:, 32:96], A.max)
+    ts(T.lof[:], T.af[:], 15, None, A.bitwise_and)
+    ts(T.hif[:], T.af[:], 4, None, A.arith_shift_right, par=True)
+    ts(T.lo48[:], T.lof[:], 48.0, None, A.mult)
+    tt(T.plf[:], T.lo48[:], T.hif[:], A.add)
+    tt(T.mlf[:], T.plf[:], T.df[:], A.min)
+    tr(T.tf[:], T.mlf[:])
+    cpy(T.of[:], T.tf[:])
+    wait("v", g.vector, "sa", nwin)
+    cpy(T.winf[:].indirect(T.of[:, 0:16]), T.val[:])
+    g.vector.wait_ge(s.vps, 128)
+    nwf = cpy(T.winf[:].indirect(T.of[:, 32:48]), T.vp[:])
+    wait("s", g.sync, "sv", nwf)
+    g.sync.dma_start(T.off2[0:128, 0:48], T.winf[0:128:16, 0:768]).then_inc(s.wr, 16)
+    g.sync.dma_start(T.off2[0:112, 48:96], T.winf[16:128:16, 0:768]).then_inc(s.wr, 16)
+    g.sync.dma_start(T.off2[112:128, 48:96], T.winf[0:1, 0:768]).then_inc(s.wr, 16)
+    ca, cb, cs = c1(), c1(), c1()
+    e0, e1 = c1(), c1()
+    EB, LB = float(T_ + C0), float(T_ + C0 + EARLY)
+    if rf < rg:
+        ts(e0, u, float(EARLY), None, A.min)
+        ts(cb, e0, -1.0, float(EARLY), A.mult, A.add)
+        if local_first:
+            ts(ca, nl, -1.0, EB, A.mult, A.add, par=True)
+            tt(cs, nl, e0, A.add, par=True)
+        else:
+            ts(ca, e0, 0.0, EB, A.mult, A.add, par=True)
+            cpy(cs, e0, par=True)
+    else:
+        ts(e0, u, -float(EARLY), 0.0, A.add, A.max)
+        tt(e1, e0, v, A.add)
+        if local_first:
+            e2 = c1()
+            tt(e2, e0, nl, A.subtract, par=True)
+            ts(ca, e2, LB, None, A.add)
+            tt(cs, nl, v, A.add, par=True)
+        else:
+            ts(ca, e0, LB, None, A.add, par=True)
+            cpy(cs, v, par=True)
+        ts(cb, e1, -1.0, -float(EARLY), A.mult, A.add)
+    ii = T.i48[:]
+    ts(T.fx[:], ii, cs, cb, A.is_ge, A.mult)
+    ts(T.fy[:], ii, ca, None, A.add, par=True)
+    if local_first:
+        ts(T.fin[:], ii, nl, None, A.is_ge, par=True)
+    else:
+        ts(T.fin[:], ii, nf, None, A.is_lt, par=True)
+    ts(T.fe[:], ii, na_, 4096.0, A.is_ge, A.mult, par=True)
+    tt(T.fz[:], T.fx[:], T.fy[:], A.add)
+    tt(T.fr[:], T.fz[:], T.fin[:], A.mult)
+    tt(T.fs[:], T.fr[:], T.fe[:], A.add)
+    g.vector.wait_ge(s.wr, 48)
+    tt(T.fl[:], T.off2[:, 0:48], T.off2[:, 48:96], A.add)
+    tt(T.fl2[:], T.fl[:], T.fs[:], A.add)
+    noff = ts(T.offf[:], T.fl2[:], float(ZC), None, A.min)
+
+    def mm(bank, o, qb, sbuf, a, n):
+        g.tensor.matmul_mx(T.ps[:, 512 * bank:512 * bank + n], T.wq[:, 128 * o:128 * o + 128], T.ws[:, 128 * o:128 * o + 128],
+                           qb[:, a:a + n], sbuf[:, a:a + n], True, True).then_inc(s.st, 1)
+        cnt["st"] += 1
+    g.tensor.wait_ge(s.sv, nwq)
+    for bank, (qb, sbuf, a, n, sem, k) in enumerate(((T.xq, T.xs, 0, 512, None, 0), (T.xwq, T.xws, 512, 256, "aS0", 2 * ncp),
+                                                     (T.leq, T.les, 0, EARLY, "aE", 2 * nmf), (T.llq, T.lls, 0, 256, "aL", 2 * nmf))):
+        if sem:
+            g.tensor.wait_ge(s[sem], k)
+        for o in range(2):
+            if cnt["st"]:
+                g.tensor.wait_ge(s.st, cnt["st"])
+            mm(2 * bank + o, o, qb, sbuf, a, n)
+    res = (T.res0, T.res1)
+    base = (0, T_, T_ + C0, T_ + C0 + EARLY)
+    width = (512, 256, EARLY, 256)
+    for b in range(3):
+        for o in range(2):
+            wait("a", g.scalar, "st", 2 * b + o + 1)
+            ncop = act(res[o][:, base[b]:base[b] + width[b]], T.ps[:, 512 * (2 * b + o):512 * (2 * b + o) + width[b]])
+    wait("a", g.scalar, "st", 8)
+    act(res[1][:, base[3]:base[3] + 256], T.ps[:, 512 * 7:512 * 7 + 256])
+    wait("v", g.vector, "st", 7)
+    cpy(res[0][:, base[3]:base[3] + 256], T.ps[:, 512 * 6:512 * 6 + 256])
+    wait("v", g.vector, "sa", ncop)
+    wait("a", g.scalar, "sv", noff)
+    for k in range(3):
+        r = slice(256 * k, 256 * k + 256)
+        of = T.offf[:, 16 * k:16 * k + 16]
+        n0 = cpy(T.yt_0[:, r], T.res0[:].indirect(of), par=k > 0)
+        n1 = SA(lambda: g.scalar.activation(T.yt_1[:, r], T.res1[:].indirect(of), AF.Copy))
+        if k == 0:
+            wait("s", g.sync, "sv", nln)
+            g.sync.dma_start(T.ln[:, :], T.lnt[0:1, :]).then_inc(s.yst, 16)
+        wait("s", g.sync, "sv", n0)
+        g.sync.dma_start(T.y[:, 256 * k:256 * k + 256], T.yt_0[:, r]).then_inc(s.yst, 16)
+        wait("s", g.sync, "sa", n1)
+        g.sync.dma_start(T.y[:, S_ + 256 * k:S_ + 256 * k + 256], T.yt_1[:, r]).then_inc(s.yst, 16)
+    g.sync.wait_ge(s.yst, 16 * 7)
+    g.wait_ge(s.loc, cnt["loc"])

@@ -24,24 +24,25 @@ SCRATCH = {
     "p0q": sb(256, Q4), "p0s": sb(256, U8),
     "peq": sb(EARLY, Q4), "pes": sb(EARLY, U8), "plq": sb(256, Q4), "pls": sb(256, U8),
     "leq": sb(EARLY, Q4), "les": sb(EARLY, U8), "llq": sb(256, Q4), "lls": sb(256, U8),
-    "zero": sb(512, F32), "one": sb(96, F32), "rst": sb(96, F32),
+    "zero": sb(512, F32), "one": sb(32, F32), "rst": sb(48, F32),
     "pi": sb(2, I32), "pint": sb(8, I32), "pf": sb(8, F32),
-    "val0": sb(256, F32), "val": sb(256, F32), "tb0": sb(32, F32), "i480": sb(48, F32), "i48": sb(48, F32),
-    "d0": sb(32, F32), "du": sb(32, F32), "df": sb(64, F32),
+    "val0": sb(256, F32), "valb": sb(256, BF), "valx": sb(256, F32), "tb0": sb(32, F32), "i480": sb(48, F32), "i48": sb(48, F32),
+    "d0": sb(32, F32), "du": sb(32, F32), "df": sb(32, F32), "bcol": sb(1, F32), "nfc": sb(1, F32),
     "ta": sb(16, I32), "tb": sb(16, I32), "tc": sb(48, I32),
     "z1": sb(160, F32), "zt1": sb(128, F32), "car1": sb(2, F32), "pt1": sb(64, F32), "m1": sb(64, F32), "a1": sb(64, F32),
     "ab1": sb(32, I32), "an1": sb(32, I32), "f1": sb(32, F32), "g1": sb(32, F32), "h1": sb(32, F32), "o1": sb(32, U16),
-    "win0": sb(768, F32), "t0": sb(512, F32), "y0": sb(32, F32), "yt0": sb(32, F32), "yu0": sb(32, F32), "off0": sb(16, U16),
-    "slu": sb(32, U16), "slin": sb(32, U16), "slf": sb(32, F32), "vp": sb(256, F32),
-    "z2": sb(224, F32), "zt2": sb(192, F32), "car2": sb(4, F32), "pt2": sb(96, F32), "m2": sb(96, F32),
+    "win0": sb(768, BF), "t0": sb(512, BF), "y0": sb(32, F32), "yt0": sb(32, F32), "yu0": sb(32, F32), "off0": sb(16, U16),
+    "slu": sb(32, U16), "slin": sb(32, U16), "slf": sb(32, F32),
+    "z2": sb(128, F32), "zt2": sb(96, F32), "car2": sb(2, F32), "pt2": sb(32, F32), "m2": sb(32, F32),
+    "z3": sb(96, F32), "zt3": sb(64, F32), "pt3": sb(32, F32), "m3": sb(32, F32),
     "au": sb(32, I32), "anu": sb(32, I32), "fu": sb(32, F32), "gu": sb(32, F32), "hu": sb(32, F32), "ou": sb(32, U16),
-    "winu": sb(1216, F32), "tu": sb(960, F32), "yu": sb(32, F32), "ytu": sb(32, F32), "yuu": sb(32, F32), "offu": sb(32, U16),
+    "winu": sb(1216, BF), "tu": sb(960, BF), "yu": sb(32, F32), "ytu": sb(32, F32), "yuu": sb(32, F32), "offu": sb(32, U16),
     "rsum": sb(32, F32), "rst_t": sb(32, F32), "rtot": sb(1, F32), "rexp": sb(32, F32), "tot": sb(32, F32),
     "cf": sb(4, F32), "cg": sb(4, F32), "ocol": sb(2, F32),
     "la": sb(16, F32), "lm": sb(16, F32), "lb": sb(16, F32), "lc": sb(16, F32), "offl": sb(16, U16),
     "sc": sb(32, F32), "lnt": sb(2, F32),
-    "xf": sb(64, F32), "af": sb(64, I32), "lof": sb(64, I32), "hif": sb(64, I32), "lo48": sb(64, F32), "plf": sb(64, F32),
-    "mlf": sb(64, F32), "tf": sb(64, F32), "of": sb(64, U16), "winf": sb(1024, F32), "off2": sb(96, F32),
+    "xf": sb(32, F32), "af": sb(32, I32), "lof": sb(32, I32), "hif": sb(32, I32), "lo48": sb(32, F32), "plf": sb(32, F32),
+    "mlf": sb(32, F32), "tf": sb(32, F32), "of": sb(32, U16), "winf": sb(1024, F32), "off2": sb(192, F32), "fq": sb(96, F32),
     "fx": sb(48, F32), "fy": sb(48, F32), "fz": sb(48, F32), "fin": sb(48, F32), "fr": sb(48, F32), "fe": sb(48, F32),
     "fs": sb(48, F32), "fl": sb(48, F32), "fl2": sb(48, F32), "offf": sb(48, U16),
     "res0": sb(RW, F32), "res1": sb(RW, F32), "yt_0": sb(768, F32), "yt_1": sb(768, F32),
@@ -145,24 +146,16 @@ def rank_program(g, core, T, topo):
     g.wait_ge(s.dml, 128)
     send(cp, T.dmp[:, 1:32], T.dmt[:, 1:32], "aDM")
 
-    nz = fill(T.zero[:], 0.0)
+    fill(T.zero[:], 0.0)
     fill(T.z1[:], 0.0)
-    fill(T.z2[:], 0.0)
     fill(T.one[:], 1.0)
     fill(T.rst[:], 1.0)
     fill(T.y0[:], 0.0)
-    fill(T.yu[:], 0.0)
-    fill(T.rsum[:], 0.0)
     fill(T.win0[:, 0:512], 0.0)
-    nfill = fill(T.z1[:, 31:32], -1.0 / 32, par=False)
+    fill(T.z1[:, 31:32], -1.0 / 32, par=False)
     fill(T.z1[:, 63:64], C0 / 32.0)
-    for c in (31, 63, 95):
-        fill(T.z2[:, c:c + 1], -1.0 / 32)
     fill(T.rst[:, 32:33], 0.0)
-    fill(T.rst[:, 64:65], 0.0)
-    fill(T.vp[:], 0.0)
-    fill(T.res0[:, ZC:RW], 0.0)
-    fill(T.res1[:, ZC:RW], 0.0)
+    fill(T.bcol[:], 0.0)
     g.vector.wait_ge(s.sg, 4)
     ts(T.pint[:, 0:1], T.pi[:, 0:1], 16, None, A.bitwise_and, par=True)
     ts(T.pint[:, 1:2], T.pi[:, 0:1], 31, None, A.bitwise_and, par=True)
@@ -171,17 +164,7 @@ def rank_program(g, core, T, topo):
     ts(T.pf[:, 1:2], T.pint[:, 1:2], 16.0, None, A.mult, par=True)
     ts(T.pf[:, 2:3], T.pint[:, 2:3], 1.0, None, A.mult, par=True)
     ts(T.d0[:], T.tb0[:], T.pf[:, 1:2], 512.0, A.add, A.add)
-    ts(T.du[:], T.tb0[:], T.pf[:, 1:2], 960.0, A.add, A.add, par=True)
-    ts(T.df[:, 0:32], T.tb0[:], T.pf[:, 1:2], 768.0, A.add, A.add, par=True)
-    ts(T.df[:, 32:64], T.tb0[:], T.pf[:, 1:2], 768.0, A.add, A.add, par=True)
-    ts(T.val[:], T.val0[:], T.pf[:, 0:1], None, A.add, par=True)
-    ts(T.i48[:], T.i480[:], T.pf[:, 2:3], None, A.add, par=True)
-
-    wait("a", g.scalar, "sv", cnt["sv"])
-    act(T.winu[:, 0:512], T.zero[:, 0:512])
-    act(T.winu[:, 512:960], T.zero[:, 0:448])
-    act(T.winf[:, 0:512], T.zero[:, 0:512])
-    nwin = act(T.winf[:, 512:768], T.zero[:, 0:256])
+    ts(T.valb[:], T.val0[:], T.pf[:, 0:1], -256.0, A.add, A.add, par=True)
 
     g.vector.wait_ge(s.dml, 128)
     dv = T.dmt[:, 1:33:2]
@@ -189,15 +172,15 @@ def rank_program(g, core, T, topo):
     ts(T.tb[:], dv, P | G, None, A.bitwise_and, par=True)
     ts(T.z1[:, 32:48], T.ta[:], 0.0, None, A.is_gt)
     ts(T.z1[:, 64:80], T.tb[:], float(P), -1.0, A.is_equal, A.mult, par=True)
-    scan(T.z1[:, 96:144], T.rst[:, 0:48], T.z1[:, 31:79], 0.0)
+    scan(T.z1[:, 96:144], T.rst[:], T.z1[:, 31:79], 0.0)
     ntr = tr(T.zt1[:], T.z1[:, 32:160])
     wait("a", g.scalar, "sv", ntr)
     act(T.m1[:, 0:32], T.zt1[:, 0:32], -BIG, BIG)
     nm1 = act(T.m1[:, 32:64], T.zt1[:, 32:64], BIG, BIG)
     red(T.car1[:, 0:1], T.zt1[:, 64:96])
     red(T.car1[:, 1:2], T.zt1[:, 96:128], par=True)
-    scan(T.pt1[:, 0:32], T.one[:, 0:32], T.zt1[:, 0:32], T.car1[:, 0:1])
-    scan(T.pt1[:, 32:64], T.one[:, 0:32], T.zt1[:, 32:64], T.car1[:, 1:2], par=True)
+    scan(T.pt1[:, 0:32], T.one[:], T.zt1[:, 0:32], T.car1[:, 0:1])
+    scan(T.pt1[:, 32:64], T.one[:], T.zt1[:, 32:64], T.car1[:, 1:2], par=True)
     wait("v", g.vector, "sa", nm1)
     tt(T.a1[:], T.pt1[:], T.m1[:], A.max)
     tt(T.ab1[:], T.a1[:, 0:32], T.a1[:, 32:64], A.min)
@@ -206,18 +189,22 @@ def rank_program(g, core, T, topo):
     tt(T.g1[:], T.f1[:], T.d0[:], A.min)
     tr(T.h1[:], T.g1[:])
     cpy(T.o1[:], T.h1[:])
-    cpy(T.win0[:, 0:768].indirect(T.o1[:, 0:16]), T.val[:])
+    cpy(T.win0[:, 0:768].indirect(T.o1[:, 0:16]), T.valb[:])
     tr(T.t0[:], T.win0[:, 0:512])
     tt(T.y0[:, 0:16], T.t0[:, 0:512:32], T.t0[:, 16:512:32], A.add)
     tr(T.yt0[:], T.y0[:])
     cpy(T.yt0[:, 16:32], T.yt0[:, 0:16])
     tr(T.yu0[:], T.yt0[:])
-    cpy(T.off0[:], T.yu0[:, 0:16])
+    ts(T.off0[:], T.yu0[:, 0:16], 256.0, None, A.add)
     g.vector.wait_ge(s.xl0, 16)
     V(lambda: g.vector.quantize_mx(T.xq[:, 0:256], T.xs[:, 0:256], T.xt[:, 0:1024]), True)
     g.vector.wait_ge(s.xl1, 16)
     nxq = V(lambda: g.vector.quantize_mx(T.xq[:, 256:512], T.xs[:, 256:512], T.xt[:, 1024:2048]), True)
     nq0 = cpy(b32(T.p0q[:]), b32(T.xq[:]).indirect(T.off0[:]))
+    for o_, n in ((T.z2[:], 128), (T.z3[:], 96), (T.rsum[:], 32), (T.yu[:], 32), (T.winu[:, 0:512], 512), (T.winu[:, 512:960], 448)):
+        act(o_, T.zero[:, 0:n])
+    act(T.z2[:, 31:32], T.zero[:, 0:1], 1.0, -1.0 / 32)
+    nz2 = act(T.z3[:, 31:32], T.zero[:, 0:1], 1.0, -1.0 / 32)
     wait("a", g.scalar, "sv", nxq)
     na0 = SA(lambda: g.scalar.activation(T.p0s[:], T.xs[:].indirect(T.off0[:]), AF.Copy))
     wait("s", g.sync, "sv", nxq)
@@ -228,83 +215,103 @@ def rank_program(g, core, T, topo):
     wait("g", g, "sa", na0)
     send(cp, T.xws[:, 512:768], T.p0s[:], "aS0")
 
+    wait("v", g.vector, "sa", nz2)
     ts(T.tc[:, 0:16], dv, Fb, None, A.bitwise_and)
     ts(T.tc[:, 16:32], dv, Qb, None, A.bitwise_and, par=True)
     g.vector.wait_ge(s.aDM, ncp)
     ts(T.tc[:, 32:48], T.dmp[:, 1:33:2], Qb, None, A.bitwise_and, par=True)
-    for k in range(3):
-        ts(T.z2[:, 32 + 32 * k:48 + 32 * k], T.tc[:, 16 * k:16 * k + 16], 0.0, None, A.is_gt, par=k > 0)
-    scan(T.z2[:, 128:208], T.rst[:, 0:80], T.z2[:, 31:111], 0.0)
-    ntr2 = tr(T.zt2[:], T.z2[:, 32:224])
-    wait("a", g.scalar, "sv", ntr2)
-    nm2 = act(T.m2[:], T.zt2[:, 0:96], -BIG, BIG)
-    for k in range(3):
-        red(T.car2[:, k:k + 1], T.zt2[:, 96 + 32 * k:128 + 32 * k], par=k > 0)
-    for k in range(3):
-        scan(T.pt2[:, 32 * k:32 * k + 32], T.one[:, 0:32], T.zt2[:, 32 * k:32 * k + 32], T.car2[:, k:k + 1], par=k > 0)
+    nsl = cpy(T.slu[:], T.ab1[:], par=True)
+    ts(T.z2[:, 32:80], T.tc[:], 0.0, None, A.is_gt)
+    scan(T.z2[:, 96:112], T.one[:, 0:16], T.z2[:, 31:47], 0.0)
+    red(T.rsum[:, 0:1], T.z2[:, 32:48], par=True)
+    red(T.rsum[:, 1:2], T.z1[:, 32:48], par=True)
+    red(T.rsum[:, 2:3], T.z2[:, 48:64], par=True)
+    red(T.rsum[:, 3:4], T.z2[:, 64:80], par=True)
+    cpy(T.z3[0:64, 32:48], T.z2[0:64, 48:64], par=True)
+    cpy(T.z3[64:128, 32:48], T.z2[64:128, 64:80], par=True)
+    tr(T.zt2[:], T.z2[:, 32:128])
+    tr(T.rst_t[:], T.rsum[:], par=True)
+    n = scan(T.z3[:, 64:80], T.one[:, 0:16], T.z3[:, 31:47], 0.0, par=True)
+    wait("a", g.scalar, "sv", n)
+    nm2 = act(T.m2[:], T.zt2[:, 0:32], -BIG, BIG)
+    red(T.car2[:, 0:1], T.zt2[:, 64:96])
+    red(T.rtot[:], T.rst_t[:], par=True)
+    n = tr(T.zt3[:], T.z3[:, 32:96], par=True)
+    wait("a", g.scalar, "sv", n)
+    act(T.m3[:], T.zt3[:, 0:32], -BIG, BIG)
+    scan(T.pt2[:], T.one[:], T.zt2[:, 0:32], T.car2[:, 0:1])
+    ts(T.rexp[:], T.zero[:, 0:32], T.rtot[:], None, A.add, par=True)
+    red(T.car2[:, 1:2], T.zt3[:, 32:64], par=True)
     wait("v", g.vector, "sa", nm2)
-    tt(T.au[:], T.pt2[:, 0:32], T.m2[:, 0:32], A.max)
+    tt(T.au[:], T.pt2[:], T.m2[:], A.max)
+    tr(T.tot[:], T.rexp[:], par=True)
+    ntot = scan(T.pt3[:], T.one[:], T.zt3[:, 0:32], T.car2[:, 1:2], par=True)
     ts(T.anu[:], T.au[:], 65520, None, A.bitwise_and)
+    ts(T.du[:], T.tb0[:], T.pf[:, 1:2], 960.0, A.add, A.add, par=True)
+    ts(T.i48[:], T.i480[:], T.pf[:, 2:3], None, A.add, par=True)
+    ts(T.ocol[:, 0:1], T.tot[:, 0:1], -float(EARLY), 0.0, A.add, A.max, par=True)
     tt(T.fu[:], T.au[:], T.anu[:], A.add)
+    ts(T.la[:], T.i48[:, 0:16], T.ocol[:, 0:1], float(T_ - 256), A.subtract, A.add, par=True)
+    ts(T.lm[:], T.i48[:, 0:16], T.ocol[:, 0:1], None, A.is_ge, par=True)
     tt(T.gu[:], T.fu[:], T.du[:], A.min)
+    tt(T.lb[:], T.la[:], T.lm[:], A.mult, par=True)
     tr(T.hu[:], T.gu[:])
     cpy(T.ou[:], T.hu[:])
-    cpy(T.winu[:, 0:1216].indirect(T.ou[:, 0:16]), T.val[:])
+    cpy(T.winu[:, 0:1216].indirect(T.ou[:, 0:16]), T.valb[:])
     tr(T.tu[:], T.winu[:, 0:960])
     tt(T.yu[:, 0:30], T.tu[:, 0:960:32], T.tu[:, 16:960:32], A.add)
     tr(T.ytu[:], T.yu[:])
     cpy(T.ytu[:, 16:32], T.ytu[:, 0:16])
     tr(T.yuu[:], T.ytu[:])
-    noffu = cpy(T.offu[:], T.yuu[:])
-    npe = cpy(b32(T.peq[:]), b32(T.xq[:]).indirect(T.offu[:, 0:14]))
+    ts(T.offu[:], T.yuu[:], 256.0, None, A.add)
+    noffu = tt(T.lc[:], T.lb[:], T.yuu[:, 14:30], A.add, par=True)
+    ts(T.offl[:], T.lc[:], 256.0, None, A.add)
+    npe = cpy(b32(T.peq[:]), b32(T.xq[:]).indirect(T.offu[:, 0:14]), par=True)
+    for o_, n in ((T.winf[:, 0:512], 512), (T.winf[:, 512:768], 256), (T.res0[:, ZC:RW], 32), (T.res1[:, ZC:RW], 32), (T.valx[64:128, :], 256)):
+        nwin = act(o_, T.zero[0:o_.shape[0], 0:n])
     wait("a", g.scalar, "sv", noffu)
     nae = SA(lambda: g.scalar.activation(T.pes[:], T.xs[:].indirect(T.offu[:, 0:14]), AF.Copy))
-    nsl = cpy(T.slu[:], T.ab1[:], par=True)
-    red(T.rsum[:, 0:1], T.z2[:, 32:48])
-    red(T.rsum[:, 1:2], T.z1[:, 32:48], par=True)
-    red(T.rsum[:, 2:3], T.z2[:, 64:80], par=True)
-    red(T.rsum[:, 3:4], T.z2[:, 96:112], par=True)
-    tr(T.rst_t[:], T.rsum[:])
-    red(T.rtot[:], T.rst_t[:])
-    ts(T.rexp[:], T.zero[:, 0:32], T.rtot[:], None, A.add)
-    ntot = tr(T.tot[:], T.rexp[:])
-    ts(T.ocol[:, 0:1], T.tot[:, 0:1], -float(EARLY), 0.0, A.add, A.max)
-    ts(T.la[:], T.i48[:, 0:16], T.ocol[:, 0:1], float(T_), A.subtract, A.add)
-    ts(T.lm[:], T.i48[:, 0:16], T.ocol[:, 0:1], None, A.is_ge, par=True)
-    tt(T.lb[:], T.la[:], T.lm[:], A.mult)
-    tt(T.lc[:], T.lb[:], T.yuu[:, 14:30], A.add)
-    noffl = cpy(T.offl[:], T.lc[:])
     g.vector.wait_ge(s.xw, 32)
     g.vector.wait_ge(s.aS0, 2 * ncp)
     npl = cpy(b32(T.plq[:]), b32(T.xwq[:]).indirect(T.offl[:]))
-    wait("a", g.scalar, "sv", noffl)
+    wait("a", g.scalar, "sv", npe)
     g.scalar.wait_ge(s.xw, 32)
     g.scalar.wait_ge(s.aS0, 2 * ncp)
     nal = SA(lambda: g.scalar.activation(T.pls[:], T.xws[:].indirect(T.offl[:]), AF.Copy))
 
+    wait("g", g, "sv", nsl)
+    send(cp, T.slin[:], T.slu[:], "aSL")
+    wait("g", g, "sv", ntot)
+    trs = []
+    for dst, land, h in ((cf_, T.cf, 0), (cg_, T.cg, 1)):
+        en = topo.engines(core, dst)
+        en = en[:len(en) // 2] if h == 0 else en[len(en) // 2:]
+        rid, pid, _se = topo.addr(dst)
+        trs.append(RemoteDMATransfer(dst_ids=[DstId(rid=rid, pnc=pid)], dma_engine_mask=sum(1 << e for e in en),
+                                     remote_sem=s.aCNT, src=T.tot[:, 0:4], dst=land[:]))
+        cnt["loc"] += len(en)
+    g.remote_dma_fused(trs, local_sem=s.loc)
     wait("g", g, "sv", npe)
     send(cf_, b8(T.leq[:]), b8(T.peq[:]), "aE")
     wait("g", g, "sa", nae)
     send(cf_, T.les[:], T.pes[:], "aE")
-    wait("g", g, "sv", nsl)
-    send(cp, T.slin[:], T.slu[:], "aSL")
-    wait("g", g, "sv", ntot)
-    send(cf_, T.cf[:], T.tot[:, 0:4], "aCNT")
-    send(cg_, T.cg[:], T.tot[:, 0:4], "aCNT")
     wait("g", g, "sv", npl)
     send(cf_, b8(T.llq[:]), b8(T.plq[:]), "aL")
     wait("g", g, "sa", nal)
     send(cf_, T.lls[:], T.pls[:], "aL")
 
     g.vector.wait_ge(s.wl, 16)
-    nwq = V(lambda: g.vector.quantize_mx(T.wq[:], T.ws[:], T.wt[:]), True)
+    nwq = V(lambda: g.vector.quantize_mx(T.wq[:], T.ws[:], T.wt[:]))
+    ts(T.valx[0:64, :], T.val0[0:64, :], T.pf[0:64, 0:1], None, A.add, par=True)
+    ts(T.df[:], T.tb0[:], T.pf[:, 1:2], 768.0, A.add, A.add, par=True)
     g.vector.wait_ge(s.aSL, ncp)
     nslf = ts(T.slf[:], T.slin[:], float(T_), None, A.add, par=True)
     wait("s", g.sync, "sv", nslf)
-    for k in range(8):
+    wait("s", g.sync, "sa", nwin)
+    for k in range(4, 8):
         a, h = k // 2, k % 2
-        g.sync.dma_start(T.vp[16 * k:16 * k + 1, :], T.slf[32 * a:32 * a + 16, 16 * h:16 * h + 16]).then_inc(s.vps, 16)
-    g.vector.wait_ge(s.aCNT, 2 * nmf)
+        g.sync.dma_start(T.valx[16 * k:16 * k + 1, :], T.slf[32 * a:32 * a + 16, 16 * h:16 * h + 16]).then_inc(s.vps, 16)
+    local_first, own_first = q < rf, q < rp
     u, v, nq, npq = T.cf[:, 0:1], T.cg[:, 1:2], T.tot[:, 2:3], T.tot[:, 3:4]
     col = [0]
 
@@ -312,27 +319,18 @@ def rank_program(g, core, T, topo):
         col[0] += 1
         return T.sc[:, col[0] - 1:col[0]]
     nl, nf, na_ = c1(), c1(), T.lnt[:, 0:1]
-    tt(nl, nq, npq, A.add)
-    tt(nf, u, v, A.add, par=True)
-    cpy(T.lnt[:, 1:2], nq, par=True)
-    nln = tt(na_, nl, nf, A.add)
-    local_first = q < rf
-    own_first = q < rp
+    first, second = (slice(0, 64), slice(64, 128)) if own_first else (slice(64, 128), slice(0, 64))
+    n2 = T.tot[second, 2:3] if own_first else T.tot[second, 3:4]
     if local_first:
-        b_own = None if own_first else npq
-        b_p = nq if own_first else None
+        cpy(T.bcol[second, :], n2)
     else:
-        sh = c1()
-        tt(sh, nf, nq if own_first else npq, A.add, par=True)
-        b_own, b_p = (nf, sh) if own_first else (sh, nf)
-    for k, b in ((0, b_own), (1, b_p)):
-        o = T.xf[:, 32 * k:32 * k + 32]
-        i = T.pt2[:, 32 + 32 * k:64 + 32 * k]
-        if b is None:
-            cpy(o, i, par=k > 0)
-        else:
-            ts(o, i, b, None, A.add, par=k > 0)
-    tt(T.af[:], T.xf[:], T.m2[:, 32:96], A.max)
+        g.vector.wait_ge(s.aCNT, nmf)
+        tt(T.nfc[:], u, v, A.add)
+        cpy(T.bcol[first, :], T.nfc[first, :])
+        tt(T.bcol[second, :], T.nfc[second, :], n2, A.add, par=True)
+    ts(T.xf[:], T.pt3[:], T.bcol[:], None, A.add)
+    wait("v", g.vector, "sa", nwin)
+    tt(T.af[:], T.xf[:], T.m3[:], A.max)
     ts(T.lof[:], T.af[:], 15, None, A.bitwise_and)
     ts(T.hif[:], T.af[:], 4, None, A.arith_shift_right, par=True)
     ts(T.lo48[:], T.lof[:], 48.0, None, A.mult)
@@ -340,38 +338,48 @@ def rank_program(g, core, T, topo):
     tt(T.mlf[:], T.plf[:], T.df[:], A.min)
     tr(T.tf[:], T.mlf[:])
     cpy(T.of[:], T.tf[:])
-    wait("v", g.vector, "sa", nwin)
-    cpy(T.winf[:].indirect(T.of[:, 0:16]), T.val[:])
-    g.vector.wait_ge(s.vps, 128)
-    nwf = cpy(T.winf[:].indirect(T.of[:, 32:48]), T.vp[:])
+    g.vector.wait_ge(s.vps, 64)
+    nwf = cpy(T.winf[:].indirect(T.of[:, 0:16]), T.valx[:])
     wait("s", g.sync, "sv", nwf)
-    g.sync.dma_start(T.off2[0:128, 0:48], T.winf[0:128:16, 0:768]).then_inc(s.wr, 16)
-    g.sync.dma_start(T.off2[0:112, 48:96], T.winf[16:128:16, 0:768]).then_inc(s.wr, 16)
-    g.sync.dma_start(T.off2[112:128, 48:96], T.winf[0:1, 0:768]).then_inc(s.wr, 16)
+    nwr = 0
+    for j, d in enumerate((0, 1, 4, 5)):
+        k = 16 * (8 - d)
+        g.sync.dma_start(T.off2[0:k, 48 * j:48 * j + 48], T.winf[16 * d:128:16, 0:768]).then_inc(s.wr, 16)
+        nwr += 16
+        if d:
+            g.sync.dma_start(T.off2[k:128, 48 * j:48 * j + 48], T.winf[0:16 * d:16, 0:768]).then_inc(s.wr, 16)
+            nwr += 16
+    if local_first:
+        g.vector.wait_ge(s.aCNT, nmf)
     ca, cb, cs = c1(), c1(), c1()
     e0, e1 = c1(), c1()
     EB, LB = float(T_ + C0), float(T_ + C0 + EARLY)
+    tt(nl, nq, npq, A.add)
+    tt(nf, u, v, A.add, par=True)
+    cpy(T.lnt[:, 1:2], nq, par=True)
     if rf < rg:
-        ts(e0, u, float(EARLY), None, A.min)
-        ts(cb, e0, -1.0, float(EARLY), A.mult, A.add)
+        ts(e0, u, float(EARLY), None, A.min, par=True)
+        tt(na_, nl, nf, A.add)
+        ts(cb, e0, -1.0, float(EARLY), A.mult, A.add, par=True)
         if local_first:
             ts(ca, nl, -1.0, EB, A.mult, A.add, par=True)
-            tt(cs, nl, e0, A.add, par=True)
+            nln = tt(cs, nl, e0, A.add, par=True)
         else:
             ts(ca, e0, 0.0, EB, A.mult, A.add, par=True)
-            cpy(cs, e0, par=True)
+            nln = cpy(cs, e0, par=True)
     else:
-        ts(e0, u, -float(EARLY), 0.0, A.add, A.max)
-        tt(e1, e0, v, A.add)
+        ts(e0, u, -float(EARLY), 0.0, A.add, A.max, par=True)
+        tt(na_, nl, nf, A.add)
+        tt(e1, e0, v, A.add, par=True)
         if local_first:
             e2 = c1()
             tt(e2, e0, nl, A.subtract, par=True)
-            ts(ca, e2, LB, None, A.add)
             tt(cs, nl, v, A.add, par=True)
+            ts(ca, e2, LB, None, A.add)
         else:
             ts(ca, e0, LB, None, A.add, par=True)
-            cpy(cs, v, par=True)
-        ts(cb, e1, -1.0, -float(EARLY), A.mult, A.add)
+            cpy(cs, v)
+        nln = ts(cb, e1, -1.0, -float(EARLY), A.mult, A.add, par=True)
     ii = T.i48[:]
     ts(T.fx[:], ii, cs, cb, A.is_ge, A.mult)
     ts(T.fy[:], ii, ca, None, A.add, par=True)
@@ -383,8 +391,9 @@ def rank_program(g, core, T, topo):
     tt(T.fz[:], T.fx[:], T.fy[:], A.add)
     tt(T.fr[:], T.fz[:], T.fin[:], A.mult)
     tt(T.fs[:], T.fr[:], T.fe[:], A.add)
-    g.vector.wait_ge(s.wr, 48)
-    tt(T.fl[:], T.off2[:, 0:48], T.off2[:, 48:96], A.add)
+    g.vector.wait_ge(s.wr, nwr)
+    tt(T.fq[:], T.off2[:, 0:96], T.off2[:, 96:192], A.add)
+    tt(T.fl[:], T.fq[:, 0:48], T.fq[:, 48:96], A.add)
     tt(T.fl2[:], T.fl[:], T.fs[:], A.add)
     noff = ts(T.offf[:], T.fl2[:], float(ZC), None, A.min)
 

@@ -7,6 +7,7 @@ EARLY = C1 - C0
 BIG = 32768.0
 RW = T_ + C0 + C1 + 32
 ZC = T_ + C0 + C1
+CUTS = (0, 256, 768)
 
 F32, I32, U16, BF = "float32", "int32", "uint16", "bfloat16"
 Q4, U8 = "float8_e4m3fn_x4", "uint8"
@@ -24,18 +25,16 @@ SCRATCH = {
     "p0q": sb(256, Q4), "p0s": sb(256, U8),
     "peq": sb(EARLY, Q4), "pes": sb(EARLY, U8), "plq": sb(256, Q4), "pls": sb(256, U8),
     "leq": sb(EARLY, Q4), "les": sb(EARLY, U8), "llq": sb(256, Q4), "lls": sb(256, U8),
-    "zero": sb(512, F32), "one": sb(32, F32), "rst": sb(48, F32),
+    "zero": sb(512, F32), "one": sb(32, F32), "rst": sb(80, F32),
     "pi": sb(2, I32), "pint": sb(8, I32), "pf": sb(8, F32),
-    "val0": sb(256, F32), "valb": sb(256, BF), "valx": sb(256, F32), "tb0": sb(32, F32), "i480": sb(48, F32), "i48": sb(48, F32),
-    "d0": sb(32, F32), "du": sb(32, F32), "df": sb(32, F32), "bcol": sb(1, F32), "nfc": sb(1, F32),
-    "ta": sb(16, I32), "tb": sb(16, I32), "tc": sb(48, I32),
-    "z1": sb(160, F32), "zt1": sb(128, F32), "car1": sb(2, F32), "pt1": sb(64, F32), "m1": sb(64, F32), "a1": sb(64, F32),
-    "ab1": sb(32, I32), "an1": sb(32, I32), "f1": sb(32, F32), "g1": sb(32, F32), "h1": sb(32, F32), "o1": sb(32, U16),
+    "val0": sb(256, F32), "valb": sb(256, BF), "valx": sb(256, U16), "tb0": sb(32, F32), "i480": sb(48, F32), "i48": sb(48, F32),
+    "d0": sb(64, F32), "df": sb(32, F32), "bcol": sb(1, F32), "nfc": sb(1, F32),
+    "ta": sb(16, I32), "tb": sb(16, I32), "tc": sb(16, I32), "td": sb(32, I32),
+    "z1": sb(224, F32), "zt1": sb(192, F32), "car1": sb(3, F32), "pt1": sb(96, F32), "m1": sb(96, F32), "a1": sb(96, F32),
+    "ab1": sb(64, I32), "an1": sb(64, I32), "f1": sb(64, F32), "g1": sb(64, F32), "h1": sb(64, F32), "o1": sb(64, U16),
     "win0": sb(768, BF), "t0": sb(512, BF), "y0": sb(32, F32), "yt0": sb(32, F32), "yu0": sb(32, F32), "off0": sb(16, U16),
-    "slu": sb(32, U16), "slin": sb(32, U16), "slf": sb(32, F32),
-    "z2": sb(128, F32), "zt2": sb(96, F32), "car2": sb(2, F32), "pt2": sb(32, F32), "m2": sb(32, F32),
-    "z3": sb(96, F32), "zt3": sb(64, F32), "pt3": sb(32, F32), "m3": sb(32, F32),
-    "au": sb(32, I32), "anu": sb(32, I32), "fu": sb(32, F32), "gu": sb(32, F32), "hu": sb(32, F32), "ou": sb(32, U16),
+    "slu": sb(32, U16), "slin": sb(32, U16), "w2": sb(32, F32),
+    "z3": sb(96, F32), "zt3": sb(64, F32), "car3": sb(1, F32), "pt3": sb(32, F32), "m3": sb(32, F32),
     "winu": sb(1216, BF), "tu": sb(960, BF), "yu": sb(32, F32), "ytu": sb(32, F32), "yuu": sb(32, F32), "offu": sb(32, U16),
     "rsum": sb(32, F32), "rst_t": sb(32, F32), "rtot": sb(1, F32), "rexp": sb(32, F32), "tot": sb(32, F32),
     "cf": sb(4, F32), "cg": sb(4, F32), "ocol": sb(2, F32),
@@ -63,7 +62,7 @@ def rank_program(g, core, T, topo):
     cp, cf_, cg_ = T.cores[rp], T.cores[rf], T.cores[rg]
     P, Fb, G, Qb = 1 << rp, 1 << rf, 1 << rg, 1 << q
     s = T.sem
-    cnt = {"sv": 0, "sa": 0, "st": 0, "sg": 0, "loc": 0}
+    cnt = {"sv": 0, "sa": 0, "st": 0, "loc": 0}
     seen = {}
 
     def wait(name, eng, sem, n):
@@ -136,13 +135,10 @@ def rank_program(g, core, T, topo):
     g.scalar.dma_start(T.xt[:, 1024:2048], T.x[:, 1024:2048]).then_inc(s.xl1, 16)
     g.scalar.dma_start(T.wt[:], T.w[:]).then_inc(s.wl, 16)
 
-    def I(ins):
-        ins().then_inc(s.sg, 1)
-        cnt["sg"] += 1
-    I(lambda: g.iota(T.pi[:, 0:1], [[1, 1]], 0, 1))
-    I(lambda: g.iota(T.tb0[:], [[0, 2], [1, 16]], 0, 0, allow_small_or_imprecise_dtypes=True))
-    I(lambda: g.iota(T.val0[:], [[32, 16], [1, 16]], 0, 0, allow_small_or_imprecise_dtypes=True))
-    I(lambda: g.iota(T.i480[:], [[16, 48]], 0, 0, allow_small_or_imprecise_dtypes=True))
+    g.iota(T.pi[:, 0:1], [[1, 1]], 0, 1).then_inc(s.sg, 1)
+    g.iota(T.tb0[:], [[0, 2], [1, 16]], 0, 0, allow_small_or_imprecise_dtypes=True).then_inc(s.sg, 1)
+    g.iota(T.val0[:], [[32, 16], [1, 16]], 0, 0, allow_small_or_imprecise_dtypes=True).then_inc(s.sg, 1)
+    g.iota(T.i480[:], [[16, 48]], 0, 0, allow_small_or_imprecise_dtypes=True).then_inc(s.sg, 1)
     g.wait_ge(s.dml, 128)
     send(cp, T.dmp[:, 1:32], T.dmt[:, 1:32], "aDM")
 
@@ -153,8 +149,10 @@ def rank_program(g, core, T, topo):
     fill(T.y0[:], 0.0)
     fill(T.win0[:, 0:512], 0.0)
     fill(T.z1[:, 31:32], -1.0 / 32, par=False)
-    fill(T.z1[:, 63:64], C0 / 32.0)
+    fill(T.z1[:, 63:64], -1.0 / 32)
+    fill(T.z1[:, 95:96], C0 / 32.0)
     fill(T.rst[:, 32:33], 0.0)
+    fill(T.rst[:, 64:65], 0.0)
     fill(T.bcol[:], 0.0)
     g.vector.wait_ge(s.sg, 4)
     ts(T.pint[:, 0:1], T.pi[:, 0:1], 16, None, A.bitwise_and, par=True)
@@ -163,121 +161,117 @@ def rank_program(g, core, T, topo):
     ts(T.pf[:, 0:1], T.pint[:, 0:1], 1.0, None, A.mult)
     ts(T.pf[:, 1:2], T.pint[:, 1:2], 16.0, None, A.mult, par=True)
     ts(T.pf[:, 2:3], T.pint[:, 2:3], 1.0, None, A.mult, par=True)
-    ts(T.d0[:], T.tb0[:], T.pf[:, 1:2], 512.0, A.add, A.add)
+    ts(T.d0[:, 0:32], T.tb0[:], T.pf[:, 1:2], 512.0, A.add, A.add)
+    ts(T.d0[:, 32:64], T.tb0[:], T.pf[:, 1:2], 960.0, A.add, A.add, par=True)
     ts(T.valb[:], T.val0[:], T.pf[:, 0:1], -256.0, A.add, A.add, par=True)
 
     g.vector.wait_ge(s.dml, 128)
     dv = T.dmt[:, 1:33:2]
     ts(T.ta[:], dv, G, None, A.bitwise_and, par=True)
     ts(T.tb[:], dv, P | G, None, A.bitwise_and, par=True)
+    ts(T.tc[:], dv, Fb, None, A.bitwise_and, par=True)
     ts(T.z1[:, 32:48], T.ta[:], 0.0, None, A.is_gt)
-    ts(T.z1[:, 64:80], T.tb[:], float(P), -1.0, A.is_equal, A.mult, par=True)
-    scan(T.z1[:, 96:144], T.rst[:], T.z1[:, 31:79], 0.0)
-    ntr = tr(T.zt1[:], T.z1[:, 32:160])
+    ts(T.z1[:, 96:112], T.tb[:], float(P), -1.0, A.is_equal, A.mult, par=True)
+    ts(T.z1[:, 64:80], T.tc[:], 0.0, None, A.is_gt, par=True)
+    scan(T.z1[:, 128:208], T.rst[:], T.z1[:, 31:111], 0.0)
+    ntr = tr(T.zt1[:], T.z1[:, 32:224])
     wait("a", g.scalar, "sv", ntr)
-    act(T.m1[:, 0:32], T.zt1[:, 0:32], -BIG, BIG)
-    nm1 = act(T.m1[:, 32:64], T.zt1[:, 32:64], BIG, BIG)
-    red(T.car1[:, 0:1], T.zt1[:, 64:96])
-    red(T.car1[:, 1:2], T.zt1[:, 96:128], par=True)
-    scan(T.pt1[:, 0:32], T.one[:], T.zt1[:, 0:32], T.car1[:, 0:1])
-    scan(T.pt1[:, 32:64], T.one[:], T.zt1[:, 32:64], T.car1[:, 1:2], par=True)
+    act(T.m1[:, 0:64], T.zt1[:, 0:64], -BIG, BIG)
+    nm1 = act(T.m1[:, 64:96], T.zt1[:, 64:96], BIG, BIG)
+    for k in range(3):
+        red(T.car1[:, k:k + 1], T.zt1[:, 96 + 32 * k:128 + 32 * k], par=k > 0)
+    for k in range(3):
+        scan(T.pt1[:, 32 * k:32 * k + 32], T.one[:], T.zt1[:, 32 * k:32 * k + 32], T.car1[:, k:k + 1], par=k > 0)
     wait("v", g.vector, "sa", nm1)
     tt(T.a1[:], T.pt1[:], T.m1[:], A.max)
-    tt(T.ab1[:], T.a1[:, 0:32], T.a1[:, 32:64], A.min)
+    tt(T.ab1[:, 0:32], T.a1[:, 0:32], T.a1[:, 64:96], A.min)
+    cpy(T.ab1[:, 32:64], T.a1[:, 32:64], par=True)
     ts(T.an1[:], T.ab1[:], 65520, None, A.bitwise_and)
     tt(T.f1[:], T.ab1[:], T.an1[:], A.add)
     tt(T.g1[:], T.f1[:], T.d0[:], A.min)
     tr(T.h1[:], T.g1[:])
     cpy(T.o1[:], T.h1[:])
-    cpy(T.win0[:, 0:768].indirect(T.o1[:, 0:16]), T.valb[:])
+    cpy(T.win0[:].indirect(T.o1[:, 0:16]), T.valb[:])
+    g.vector.wait_ge(s.xl0, 16)
+    nxq0 = V(lambda: g.vector.quantize_mx(T.xq[:, 0:256], T.xs[:, 0:256], T.xt[:, 0:1024]), True)
     tr(T.t0[:], T.win0[:, 0:512])
     tt(T.y0[:, 0:16], T.t0[:, 0:512:32], T.t0[:, 16:512:32], A.add)
     tr(T.yt0[:], T.y0[:])
     cpy(T.yt0[:, 16:32], T.yt0[:, 0:16])
     tr(T.yu0[:], T.yt0[:])
     ts(T.off0[:], T.yu0[:, 0:16], 256.0, None, A.add)
-    g.vector.wait_ge(s.xl0, 16)
-    V(lambda: g.vector.quantize_mx(T.xq[:, 0:256], T.xs[:, 0:256], T.xt[:, 0:1024]), True)
     g.vector.wait_ge(s.xl1, 16)
     nxq = V(lambda: g.vector.quantize_mx(T.xq[:, 256:512], T.xs[:, 256:512], T.xt[:, 1024:2048]), True)
     nq0 = cpy(b32(T.p0q[:]), b32(T.xq[:]).indirect(T.off0[:]))
-    for o_, n in ((T.z2[:], 128), (T.z3[:], 96), (T.rsum[:], 32), (T.yu[:], 32), (T.winu[:, 0:512], 512), (T.winu[:, 512:960], 448)):
+    for o_, n in ((T.winu[:, 0:512], 512), (T.winu[:, 512:960], 448), (T.yu[:], 32), (T.z3[:], 96), (T.rsum[:], 32)):
         act(o_, T.zero[:, 0:n])
-    act(T.z2[:, 31:32], T.zero[:, 0:1], 1.0, -1.0 / 32)
-    nz2 = act(T.z3[:, 31:32], T.zero[:, 0:1], 1.0, -1.0 / 32)
+    nz3 = act(T.z3[:, 31:32], T.zero[:, 0:1], 1.0, -1.0 / 32)
     wait("a", g.scalar, "sv", nxq)
     na0 = SA(lambda: g.scalar.activation(T.p0s[:], T.xs[:].indirect(T.off0[:]), AF.Copy))
-    wait("s", g.sync, "sv", nxq)
-    g.sync.dma_start(b8(T.xwq[:, 0:512]), b8(T.xq[:, 0:512])).then_inc(s.xw, 16)
-    g.sync.dma_start(T.xws[:, 0:512], T.xs[:, 0:512]).then_inc(s.xw, 16)
+    for n, r in ((nxq0, slice(0, 256)), (nxq, slice(256, 512))):
+        wait("s", g.sync, "sv", n)
+        g.sync.dma_start(b8(T.xwq[:, r]), b8(T.xq[:, r])).then_inc(s.xw, 16)
+        g.sync.dma_start(T.xws[:, r], T.xs[:, r]).then_inc(s.xw, 16)
     wait("g", g, "sv", nq0)
     send(cp, b8(T.xwq[:, 512:768]), b8(T.p0q[:]), "aS0")
     wait("g", g, "sa", na0)
     send(cp, T.xws[:, 512:768], T.p0s[:], "aS0")
 
-    wait("v", g.vector, "sa", nz2)
-    ts(T.tc[:, 0:16], dv, Fb, None, A.bitwise_and)
-    ts(T.tc[:, 16:32], dv, Qb, None, A.bitwise_and, par=True)
+    ts(T.td[:, 0:16], dv, Qb, None, A.bitwise_and)
     g.vector.wait_ge(s.aDM, ncp)
-    ts(T.tc[:, 32:48], T.dmp[:, 1:33:2], Qb, None, A.bitwise_and, par=True)
-    nsl = cpy(T.slu[:], T.ab1[:], par=True)
-    ts(T.z2[:, 32:80], T.tc[:], 0.0, None, A.is_gt)
-    scan(T.z2[:, 96:112], T.one[:, 0:16], T.z2[:, 31:47], 0.0)
-    red(T.rsum[:, 0:1], T.z2[:, 32:48], par=True)
+    ts(T.td[:, 16:32], T.dmp[:, 1:33:2], Qb, None, A.bitwise_and, par=True)
+    nsl = ts(T.slu[:], T.ab1[:, 0:32], float(T_), None, A.add, par=True)
+    wait("v", g.vector, "sa", nz3)
+    ts(T.w2[:], T.td[:], 0.0, None, A.is_gt)
+    cpy(T.winu[:].indirect(T.o1[:, 32:48]), T.valb[:], par=True)
+    tr(T.tu[:], T.winu[:, 0:960])
+    red(T.rsum[:, 0:1], T.z1[:, 64:80], par=True)
     red(T.rsum[:, 1:2], T.z1[:, 32:48], par=True)
-    red(T.rsum[:, 2:3], T.z2[:, 48:64], par=True)
-    red(T.rsum[:, 3:4], T.z2[:, 64:80], par=True)
-    cpy(T.z3[0:64, 32:48], T.z2[0:64, 48:64], par=True)
-    cpy(T.z3[64:128, 32:48], T.z2[64:128, 64:80], par=True)
-    tr(T.zt2[:], T.z2[:, 32:128])
+    red(T.rsum[:, 2:3], T.w2[:, 0:16], par=True)
+    red(T.rsum[:, 3:4], T.w2[:, 16:32], par=True)
+    cpy(T.z3[0:64, 32:48], T.w2[0:64, 0:16], par=True)
+    cpy(T.z3[64:128, 32:48], T.w2[64:128, 16:32], par=True)
+    tt(T.yu[:, 0:30], T.tu[:, 0:960:32], T.tu[:, 16:960:32], A.add)
     tr(T.rst_t[:], T.rsum[:], par=True)
-    n = scan(T.z3[:, 64:80], T.one[:, 0:16], T.z3[:, 31:47], 0.0, par=True)
-    wait("a", g.scalar, "sv", n)
-    nm2 = act(T.m2[:], T.zt2[:, 0:32], -BIG, BIG)
-    red(T.car2[:, 0:1], T.zt2[:, 64:96])
+    scan(T.z3[:, 64:80], T.one[:, 0:16], T.z3[:, 31:47], 0.0, par=True)
+    ts(T.i48[:], T.i480[:], T.pf[:, 2:3], None, A.add, par=True)
+    tr(T.ytu[:], T.yu[:])
     red(T.rtot[:], T.rst_t[:], par=True)
     n = tr(T.zt3[:], T.z3[:, 32:96], par=True)
     wait("a", g.scalar, "sv", n)
-    act(T.m3[:], T.zt3[:, 0:32], -BIG, BIG)
-    scan(T.pt2[:], T.one[:], T.zt2[:, 0:32], T.car2[:, 0:1])
-    ts(T.rexp[:], T.zero[:, 0:32], T.rtot[:], None, A.add, par=True)
-    red(T.car2[:, 1:2], T.zt3[:, 32:64], par=True)
-    wait("v", g.vector, "sa", nm2)
-    tt(T.au[:], T.pt2[:], T.m2[:], A.max)
-    tr(T.tot[:], T.rexp[:], par=True)
-    ntot = scan(T.pt3[:], T.one[:], T.zt3[:, 0:32], T.car2[:, 1:2], par=True)
-    ts(T.anu[:], T.au[:], 65520, None, A.bitwise_and)
-    ts(T.du[:], T.tb0[:], T.pf[:, 1:2], 960.0, A.add, A.add, par=True)
-    ts(T.i48[:], T.i480[:], T.pf[:, 2:3], None, A.add, par=True)
-    ts(T.ocol[:, 0:1], T.tot[:, 0:1], -float(EARLY), 0.0, A.add, A.max, par=True)
-    tt(T.fu[:], T.au[:], T.anu[:], A.add)
-    ts(T.la[:], T.i48[:, 0:16], T.ocol[:, 0:1], float(T_ - 256), A.subtract, A.add, par=True)
-    ts(T.lm[:], T.i48[:, 0:16], T.ocol[:, 0:1], None, A.is_ge, par=True)
-    tt(T.gu[:], T.fu[:], T.du[:], A.min)
-    tt(T.lb[:], T.la[:], T.lm[:], A.mult, par=True)
-    tr(T.hu[:], T.gu[:])
-    cpy(T.ou[:], T.hu[:])
-    cpy(T.winu[:, 0:1216].indirect(T.ou[:, 0:16]), T.valb[:])
-    tr(T.tu[:], T.winu[:, 0:960])
-    tt(T.yu[:, 0:30], T.tu[:, 0:960:32], T.tu[:, 16:960:32], A.add)
-    tr(T.ytu[:], T.yu[:])
+    nm3 = act(T.m3[:], T.zt3[:, 0:32], -BIG, BIG)
     cpy(T.ytu[:, 16:32], T.ytu[:, 0:16])
+    ts(T.rexp[:], T.zero[:, 0:32], T.rtot[:], None, A.add, par=True)
+    red(T.car3[:], T.zt3[:, 32:64], par=True)
     tr(T.yuu[:], T.ytu[:])
+    tr(T.tot[:], T.rexp[:], par=True)
+    ntot = scan(T.pt3[:], T.one[:], T.zt3[:, 0:32], T.car3[:], par=True)
     ts(T.offu[:], T.yuu[:], 256.0, None, A.add)
-    noffu = tt(T.lc[:], T.lb[:], T.yuu[:, 14:30], A.add, par=True)
-    ts(T.offl[:], T.lc[:], 256.0, None, A.add)
+    noffu = ts(T.ocol[:, 0:1], T.tot[:, 0:1], -float(EARLY), 0.0, A.add, A.max, par=True)
+    ts(T.la[:], T.i48[:, 0:16], T.ocol[:, 0:1], float(T_ - 256), A.subtract, A.add)
+    ts(T.lm[:], T.i48[:, 0:16], T.ocol[:, 0:1], None, A.is_ge, par=True)
     npe = cpy(b32(T.peq[:]), b32(T.xq[:]).indirect(T.offu[:, 0:14]), par=True)
-    for o_, n in ((T.winf[:, 0:512], 512), (T.winf[:, 512:768], 256), (T.res0[:, ZC:RW], 32), (T.res1[:, ZC:RW], 32), (T.valx[64:128, :], 256)):
-        nwin = act(o_, T.zero[0:o_.shape[0], 0:n])
+    tt(T.lb[:], T.la[:], T.lm[:], A.mult)
+    fill(T.valx[64:128, :], 0)
+    tt(T.lc[:], T.lb[:], T.yuu[:, 14:30], A.add)
+    ts(T.valx[0:64, :], T.val0[0:64, :], T.pf[0:64, 0:1], None, A.add, par=True)
+    noffl = ts(T.offl[:], T.lc[:], 256.0, None, A.add)
     wait("a", g.scalar, "sv", noffu)
     nae = SA(lambda: g.scalar.activation(T.pes[:], T.xs[:].indirect(T.offu[:, 0:14]), AF.Copy))
-    g.vector.wait_ge(s.xw, 32)
+    g.vector.wait_ge(s.xw, 64)
     g.vector.wait_ge(s.aS0, 2 * ncp)
     npl = cpy(b32(T.plq[:]), b32(T.xwq[:]).indirect(T.offl[:]))
-    wait("a", g.scalar, "sv", npe)
-    g.scalar.wait_ge(s.xw, 32)
+    wait("a", g.scalar, "sv", noffl)
+    g.scalar.wait_ge(s.xw, 64)
     g.scalar.wait_ge(s.aS0, 2 * ncp)
     nal = SA(lambda: g.scalar.activation(T.pls[:], T.xws[:].indirect(T.offl[:]), AF.Copy))
+    for o_, n in ((T.winf[:, 0:512], 512), (T.winf[:, 512:768], 256), (T.res0[:, ZC:RW], 32), (T.res1[:, ZC:RW], 32)):
+        nwin = act(o_, T.zero[:, 0:n])
+    wait("s", g.sync, "sv", noffl)
+    g.sync.wait_ge(s.aSL, ncp)
+    for k in range(4, 8):
+        a, h = k // 2, k % 2
+        g.sync.dma_start(T.valx[16 * k:16 * k + 1, :], T.slin[32 * a:32 * a + 16, 16 * h:16 * h + 16]).then_inc(s.vps, 16)
 
     wait("g", g, "sv", nsl)
     send(cp, T.slin[:], T.slu[:], "aSL")
@@ -302,15 +296,7 @@ def rank_program(g, core, T, topo):
 
     g.vector.wait_ge(s.wl, 16)
     nwq = V(lambda: g.vector.quantize_mx(T.wq[:], T.ws[:], T.wt[:]))
-    ts(T.valx[0:64, :], T.val0[0:64, :], T.pf[0:64, 0:1], None, A.add, par=True)
     ts(T.df[:], T.tb0[:], T.pf[:, 1:2], 768.0, A.add, A.add, par=True)
-    g.vector.wait_ge(s.aSL, ncp)
-    nslf = ts(T.slf[:], T.slin[:], float(T_), None, A.add, par=True)
-    wait("s", g.sync, "sv", nslf)
-    wait("s", g.sync, "sa", nwin)
-    for k in range(4, 8):
-        a, h = k // 2, k % 2
-        g.sync.dma_start(T.valx[16 * k:16 * k + 1, :], T.slf[32 * a:32 * a + 16, 16 * h:16 * h + 16]).then_inc(s.vps, 16)
     local_first, own_first = q < rf, q < rp
     u, v, nq, npq = T.cf[:, 0:1], T.cg[:, 1:2], T.tot[:, 2:3], T.tot[:, 3:4]
     col = [0]
@@ -322,14 +308,14 @@ def rank_program(g, core, T, topo):
     first, second = (slice(0, 64), slice(64, 128)) if own_first else (slice(64, 128), slice(0, 64))
     n2 = T.tot[second, 2:3] if own_first else T.tot[second, 3:4]
     if local_first:
-        cpy(T.bcol[second, :], n2)
+        cpy(T.bcol[second, :], n2, par=True)
     else:
         g.vector.wait_ge(s.aCNT, nmf)
-        tt(T.nfc[:], u, v, A.add)
+        tt(T.nfc[:], u, v, A.add, par=True)
         cpy(T.bcol[first, :], T.nfc[first, :])
         tt(T.bcol[second, :], T.nfc[second, :], n2, A.add, par=True)
     ts(T.xf[:], T.pt3[:], T.bcol[:], None, A.add)
-    wait("v", g.vector, "sa", nwin)
+    wait("v", g.vector, "sa", nm3)
     tt(T.af[:], T.xf[:], T.m3[:], A.max)
     ts(T.lof[:], T.af[:], 15, None, A.bitwise_and)
     ts(T.hif[:], T.af[:], 4, None, A.arith_shift_right, par=True)
@@ -338,6 +324,7 @@ def rank_program(g, core, T, topo):
     tt(T.mlf[:], T.plf[:], T.df[:], A.min)
     tr(T.tf[:], T.mlf[:])
     cpy(T.of[:], T.tf[:])
+    wait("v", g.vector, "sa", nwin)
     g.vector.wait_ge(s.vps, 64)
     nwf = cpy(T.winf[:].indirect(T.of[:, 0:16]), T.valx[:])
     wait("s", g.sync, "sv", nwf)
@@ -423,17 +410,17 @@ def rank_program(g, core, T, topo):
     cpy(res[0][:, base[3]:base[3] + 256], T.ps[:, 512 * 6:512 * 6 + 256])
     wait("v", g.vector, "sa", ncop)
     wait("a", g.scalar, "sv", noff)
-    for k in range(3):
-        r = slice(256 * k, 256 * k + 256)
-        of = T.offf[:, 16 * k:16 * k + 16]
-        n0 = cpy(T.yt_0[:, r], T.res0[:].indirect(of), par=k > 0)
-        n1 = SA(lambda: g.scalar.activation(T.yt_1[:, r], T.res1[:].indirect(of), AF.Copy))
+    for k in range(len(CUTS) - 1):
+        a, b = CUTS[k], CUTS[k + 1]
+        of = T.offf[:, a // 16:b // 16]
+        n0 = cpy(T.yt_0[:, a:b], T.res0[:].indirect(of), par=k > 0)
+        n1 = SA(lambda: g.scalar.activation(T.yt_1[:, a:b], T.res1[:].indirect(of), AF.Copy))
         if k == 0:
             wait("s", g.sync, "sv", nln)
             g.sync.dma_start(T.ln[:, :], T.lnt[0:1, :]).then_inc(s.yst, 16)
         wait("s", g.sync, "sv", n0)
-        g.sync.dma_start(T.y[:, 256 * k:256 * k + 256], T.yt_0[:, r]).then_inc(s.yst, 16)
+        g.sync.dma_start(T.y[:, a:b], T.yt_0[:, a:b]).then_inc(s.yst, 16)
         wait("s", g.sync, "sa", n1)
-        g.sync.dma_start(T.y[:, S_ + 256 * k:S_ + 256 * k + 256], T.yt_1[:, r]).then_inc(s.yst, 16)
-    g.sync.wait_ge(s.yst, 16 * 7)
+        g.sync.dma_start(T.y[:, S_ + a:S_ + b], T.yt_1[:, a:b]).then_inc(s.yst, 16)
+    g.sync.wait_ge(s.yst, 16 * (2 * len(CUTS) - 1))
     g.wait_ge(s.loc, cnt["loc"])

@@ -4,10 +4,10 @@ from concourse.mybir import dt, AluOpType, AxisListType, ActivationFunctionType
 
 T_, S_, C0, C1 = 512, 768, 256, 480
 EARLY = C1 - C0
-BIG = 32768.0
 RW = T_ + C0 + C1 + 32
 ZC = T_ + C0 + C1
 CUTS = (0, 256, 768)
+FAR = 16 * 127 + 16
 
 F32, I32, U16, BF = "float32", "int32", "uint16", "bfloat16"
 Q4, U8 = "float8_e4m3fn_x4", "uint8"
@@ -18,36 +18,37 @@ def sb(n, d):
 
 
 SCRATCH = {
-    "dmt": sb(40, I32), "dmp": sb(40, I32),
+    "dmt": sb(68, I32),
     "xt": sb(2048, BF), "wt": sb(1024, BF),
     "xq": sb(512, Q4), "xs": sb(512, U8), "wq": sb(256, Q4), "ws": sb(256, U8),
     "xwq": sb(768, Q4), "xws": sb(768, U8),
     "p0q": sb(256, Q4), "p0s": sb(256, U8),
     "peq": sb(EARLY, Q4), "pes": sb(EARLY, U8), "plq": sb(256, Q4), "pls": sb(256, U8),
     "leq": sb(EARLY, Q4), "les": sb(EARLY, U8), "llq": sb(256, Q4), "lls": sb(256, U8),
-    "zero": sb(512, F32), "one": sb(32, F32), "rst": sb(80, F32),
+    "zero": sb(512, BF), "one": sb(32, F32), "half": sb(32, F32), "hb": sb(1, F32),
     "pi": sb(2, I32), "pint": sb(8, I32), "pf": sb(8, F32),
-    "val0": sb(256, F32), "valb": sb(256, BF), "valx": sb(256, U16), "tb0": sb(32, F32), "i480": sb(48, F32), "i48": sb(48, F32),
-    "d0": sb(64, F32), "df": sb(32, F32), "bcol": sb(1, F32), "nfc": sb(1, F32),
+    "val0": sb(256, F32), "valb": sb(256, BF), "valx": sb(256, BF), "dd": sb(96, F32), "i480": sb(48, F32), "i48": sb(48, F32),
     "ta": sb(16, I32), "tb": sb(16, I32), "tc": sb(16, I32), "td": sb(32, I32),
-    "z1": sb(224, F32), "zt1": sb(192, F32), "car1": sb(3, F32), "pt1": sb(96, F32), "m1": sb(96, F32), "a1": sb(96, F32),
-    "ab1": sb(64, I32), "an1": sb(64, I32), "f1": sb(64, F32), "g1": sb(64, F32), "h1": sb(64, F32), "o1": sb(64, U16),
-    "win0": sb(768, BF), "t0": sb(512, BF), "y0": sb(32, F32), "yt0": sb(32, F32), "yu0": sb(32, F32), "off0": sb(16, U16),
-    "slu": sb(32, U16), "slin": sb(32, U16), "w2": sb(32, F32),
-    "z3": sb(96, F32), "zt3": sb(64, F32), "car3": sb(1, F32), "pt3": sb(32, F32), "m3": sb(32, F32),
-    "winu": sb(1216, BF), "tu": sb(960, BF), "yu": sb(32, F32), "ytu": sb(32, F32), "yuu": sb(32, F32), "offu": sb(32, U16),
-    "rsum": sb(32, F32), "rst_t": sb(32, F32), "rtot": sb(1, F32), "rexp": sb(32, F32), "tot": sb(32, F32),
-    "cf": sb(4, F32), "cg": sb(4, F32), "ocol": sb(2, F32),
+    "z0": sb(96, F32), "zt0": sb(64, F32), "car0": sb(1, F32), "pt0": sb(32, F32), "zb0": sb(32, F32), "m0": sb(32, F32),
+    "a0": sb(32, F32), "h0": sb(32, F32), "hm": sb(32, F32), "o0": sb(16, U16), "slt": sb(32, F32),
+    "zf": sb(96, F32), "ztf": sb(64, F32), "carf": sb(1, F32), "ptf": sb(32, F32), "zbf": sb(32, F32), "mf": sb(32, F32),
+    "af": sb(32, F32), "hf": sb(32, F32), "of": sb(16, U16),
+    "z3": sb(96, F32), "zt3": sb(64, F32), "car3": sb(1, F32), "pt3": sb(32, F32), "zb3": sb(32, F32), "m3": sb(32, F32),
+    "x3": sb(32, F32), "a3": sb(32, F32), "h3": sb(32, F32), "o3": sb(16, U16),
+    "win0": sb(512 + FAR, BF), "t0": sb(512, BF), "y0": sb(64, F32), "yt0": sb(64, F32), "yu0": sb(32, F32), "off0": sb(16, U16),
+    "winu": sb(1024 + FAR, BF), "tu": sb(960, BF), "yu": sb(64, F32), "ytu": sb(64, F32), "yuu": sb(32, F32), "offu": sb(32, U16),
+    "winf": sb(1536 + FAR, BF), "tf": sb(1536, BF), "yf": sb(128, F32), "ytf": sb(128, F32), "yff": sb(64, F32), "sw": sb(48, F32),
+    "slu": sb(32, BF), "slin": sb(32, BF),
+    "rexp": sb(64, F32), "ct": sb(64, F32), "rexp3": sb(32, F32), "ct3": sb(32, F32),
+    "cf": sb(4, F32), "cg": sb(4, F32), "ocol": sb(1, F32), "nf2": sb(1, F32),
     "la": sb(16, F32), "lm": sb(16, F32), "lb": sb(16, F32), "lc": sb(16, F32), "offl": sb(16, U16),
-    "sc": sb(32, F32), "lnt": sb(2, F32),
-    "xf": sb(32, F32), "af": sb(32, I32), "lof": sb(32, I32), "hif": sb(32, I32), "lo48": sb(32, F32), "plf": sb(32, F32),
-    "mlf": sb(32, F32), "tf": sb(32, F32), "of": sb(32, U16), "winf": sb(1024, F32), "off2": sb(192, F32), "fq": sb(96, F32),
+    "sc": sb(16, F32), "lnt": sb(2, F32),
     "fx": sb(48, F32), "fy": sb(48, F32), "fz": sb(48, F32), "fin": sb(48, F32), "fr": sb(48, F32), "fe": sb(48, F32),
     "fs": sb(48, F32), "fl": sb(48, F32), "fl2": sb(48, F32), "offf": sb(48, U16),
     "res0": sb(RW, F32), "res1": sb(RW, F32), "yt_0": sb(768, F32), "yt_1": sb(768, F32),
     "ps": ("psum", [128, 4096], F32),
 }
-SEMAPHORES = ["sv", "sa", "st", "sg", "dml", "xl0", "xl1", "wl", "xw", "vps", "wr", "yst",
+SEMAPHORES = ["sv", "sa", "st", "sg", "dml", "xl0", "xl1", "wl", "xw", "wf", "vps", "yst",
               "aDM", "aS0", "aSL", "aCNT", "aE", "aL", "loc"]
 
 
@@ -70,48 +71,54 @@ def rank_program(g, core, T, topo):
             seen[(name, sem)] = n
             eng.wait_ge(s[sem], n)
 
-    def V(ins, par=False):
-        if not par:
-            wait("v", g.vector, "sv", cnt["sv"])
+    def V(ins, d=0):
+        wait("v", g.vector, "sv", d)
         r = ins()
         cnt["sv"] += 1
         r.then_inc(s.sv, 1)
         return cnt["sv"]
 
-    def SA(ins):
-        wait("a", g.scalar, "sa", cnt["sa"])
+    def SA(ins, v=0, a=0):
+        wait("a", g.scalar, "sv", v)
+        wait("a", g.scalar, "sa", a)
         r = ins()
         cnt["sa"] += 1
         r.then_inc(s.sa, 1)
         return cnt["sa"]
 
-    def ts(out, in0, s1, s2, op0, op1=None, par=False):
+    def vsa(n):
+        wait("v", g.vector, "sa", n)
+
+    def ts(out, in0, s1, s2, op0, op1=None, d=0):
         if op1 is None:
-            return V(lambda: g.vector.tensor_scalar(out, in0, s1, s2, op0), par)
-        return V(lambda: g.vector.tensor_scalar(out, in0, s1, s2, op0, op1), par)
+            return V(lambda: g.vector.tensor_scalar(out, in0, s1, s2, op0), d)
+        return V(lambda: g.vector.tensor_scalar(out, in0, s1, s2, op0, op1), d)
 
-    def tt(out, a, b, op, par=False):
-        return V(lambda: g.vector.tensor_tensor(out, a, b, op), par)
+    def tt(out, a, b, op, d=0):
+        return V(lambda: g.vector.tensor_tensor(out, a, b, op), d)
 
-    def cpy(out, in_, par=False):
-        return V(lambda: g.vector.tensor_copy(out, in_), par)
+    def cpy(out, in_, d=0):
+        return V(lambda: g.vector.tensor_copy(out, in_), d)
 
-    def tr(out, in_, par=False):
-        return V(lambda: g.vector.transpose(out, in_), par)
+    def tr(out, in_, d=0):
+        return V(lambda: g.vector.transpose(out, in_), d)
 
-    def red(out, in_, par=False):
-        return V(lambda: g.vector.tensor_reduce(out, in_, X, A.add), par)
+    def red(out, in_, d=0):
+        return V(lambda: g.vector.tensor_reduce(out, in_, X, A.add), d)
 
-    def scan(out, d0, d1, init, par=False):
-        return V(lambda: g.vector.tensor_tensor_scan(out, d0, d1, init, A.mult, A.add), par)
+    def scan(out, d1, init, d=0):
+        return V(lambda: g.vector.tensor_tensor_scan(out, T.one[:], d1, init, A.mult, A.add), d)
 
-    def fill(ap, c, par=True):
-        return V(lambda: g.vector.memset(ap, c), par)
+    def fill(ap, c, d=0):
+        return V(lambda: g.vector.memset(ap, c), d)
 
-    def act(out, in_, scale=1.0, bias=0.0):
-        if scale == 1.0 and bias == 0.0:
-            return SA(lambda: g.scalar.activation(out, in_, AF.Copy))
-        return SA(lambda: g.scalar.activation(out, in_, AF.Copy, bias=bias, scale=scale))
+    def act(out, in_, v=0, a=0, f=AF.Copy, scale=None, bias=None):
+        kw = {}
+        if scale is not None:
+            kw["scale"] = scale
+        if bias is not None:
+            kw["bias"] = bias
+        return SA(lambda: g.scalar.activation(out, in_, f, **kw), v, a)
 
     def send(dst, out, in_, rsem):
         rid, pid, _se = topo.addr(dst)
@@ -127,164 +134,183 @@ def rank_program(g, core, T, topo):
     def b32(ap):
         return ap.bitcast(dt.uint32)
 
+    even = q < rp
+    ob = 4 if even else 36
     for k in range(8):
         e = g.sync if k % 2 == 0 else g.scalar
-        o = 1 - k % 2
+        o = ob - k % 2
         e.dma_start(T.dmt[16 * k:16 * k + 16, o:o + 32], T.dm[:, :]).then_inc(s.dml, 16)
     g.sync.dma_start(T.xt[:, 0:1024], T.x[:, 0:1024]).then_inc(s.xl0, 16)
     g.scalar.dma_start(T.xt[:, 1024:2048], T.x[:, 1024:2048]).then_inc(s.xl1, 16)
     g.scalar.dma_start(T.wt[:], T.w[:]).then_inc(s.wl, 16)
 
+    FL = {"allow_small_or_imprecise_dtypes": True}
     g.iota(T.pi[:, 0:1], [[1, 1]], 0, 1).then_inc(s.sg, 1)
-    g.iota(T.tb0[:], [[0, 2], [1, 16]], 0, 0, allow_small_or_imprecise_dtypes=True).then_inc(s.sg, 1)
-    g.iota(T.val0[:], [[32, 16], [1, 16]], 0, 0, allow_small_or_imprecise_dtypes=True).then_inc(s.sg, 1)
-    g.iota(T.i480[:], [[16, 48]], 0, 0, allow_small_or_imprecise_dtypes=True).then_inc(s.sg, 1)
+    g.iota(T.dd[:], [[512, 3], [0, 2], [1, 16]], 512, 16, **FL).then_inc(s.sg, 1)
+    g.iota(T.val0[:], [[32, 16], [1, 16]], -256, 0, **FL).then_inc(s.sg, 1)
     g.wait_ge(s.dml, 128)
-    send(cp, T.dmp[:, 1:32], T.dmt[:, 1:32], "aDM")
+    send(cp, T.dmt[:, ob:ob + 31], T.dmt[:, ob:ob + 31], "aDM")
+    g.iota(T.i480[:], [[16, 48]], 0, 0, **FL).then_inc(s.sg, 1)
 
-    fill(T.zero[:], 0.0)
-    fill(T.z1[:], 0.0)
+    nzero = fill(T.zero[:], 0.0)
+    n = fill(T.zf[:], 0.0)
     fill(T.one[:], 1.0)
-    fill(T.rst[:], 1.0)
+    fill(T.z0[:, 31:32], -2.0 / 32)
+    fill(T.zf[:, 31:32], -2.0 / 32, n)
+    fill(T.half[:], 0.5)
     fill(T.y0[:], 0.0)
-    fill(T.win0[:, 0:512], 0.0)
-    fill(T.z1[:, 31:32], -1.0 / 32, par=False)
-    fill(T.z1[:, 63:64], -1.0 / 32)
-    fill(T.z1[:, 95:96], C0 / 32.0)
-    fill(T.rst[:, 32:33], 0.0)
-    fill(T.rst[:, 64:65], 0.0)
-    fill(T.bcol[:], 0.0)
-    g.vector.wait_ge(s.sg, 4)
-    ts(T.pint[:, 0:1], T.pi[:, 0:1], 16, None, A.bitwise_and, par=True)
-    ts(T.pint[:, 1:2], T.pi[:, 0:1], 31, None, A.bitwise_and, par=True)
-    ts(T.pint[:, 2:3], T.pi[:, 0:1], 15, None, A.bitwise_and, par=True)
-    ts(T.pf[:, 0:1], T.pint[:, 0:1], 1.0, None, A.mult)
-    ts(T.pf[:, 1:2], T.pint[:, 1:2], 16.0, None, A.mult, par=True)
-    ts(T.pf[:, 2:3], T.pint[:, 2:3], 1.0, None, A.mult, par=True)
-    ts(T.d0[:, 0:32], T.tb0[:], T.pf[:, 1:2], 512.0, A.add, A.add)
-    ts(T.d0[:, 32:64], T.tb0[:], T.pf[:, 1:2], 960.0, A.add, A.add, par=True)
-    ts(T.valb[:], T.val0[:], T.pf[:, 0:1], -256.0, A.add, A.add, par=True)
+    fill(T.hm[:], 0.0)
+    g.vector.wait_ge(s.sg, 1)
+    ts(T.pint[:, 0:1], T.pi[:, 0:1], 16, None, A.bitwise_and)
+    n = ts(T.pint[:, 1:2], T.pi[:, 0:1], 15, None, A.bitwise_and)
+    fill(T.z3[:, 31:32], -2.0 / 32)
+    npf = cpy(T.pf[:, 0:2], T.pint[:, 0:2], n)
+    fill(T.hb[0:64, :], 256.0)
+    nhb = fill(T.hb[64:128, :], 0.0)
+    g.vector.wait_ge(s.sg, 3)
+    nvalb = ts(T.valb[:], T.val0[:], T.pf[:, 0:1], None, A.add, d=npf)
+
+    nw0 = act(T.win0[:, 0:512], T.zero[:], nzero)
+    act(T.winu[:, 0:512], T.zero[:])
+    nwu = act(T.winu[:, 512:960], T.zero[:, 0:448])
+    nyu = act(T.yu[:], T.zero[:, 0:64])
 
     g.vector.wait_ge(s.dml, 128)
-    dv = T.dmt[:, 1:33:2]
-    ts(T.ta[:], dv, G, None, A.bitwise_and, par=True)
-    ts(T.tb[:], dv, P | G, None, A.bitwise_and, par=True)
-    ts(T.tc[:], dv, Fb, None, A.bitwise_and, par=True)
-    ts(T.z1[:, 32:48], T.ta[:], 0.0, None, A.is_gt)
-    ts(T.z1[:, 96:112], T.tb[:], float(P), -1.0, A.is_equal, A.mult, par=True)
-    ts(T.z1[:, 64:80], T.tc[:], 0.0, None, A.is_gt, par=True)
-    scan(T.z1[:, 128:208], T.rst[:], T.z1[:, 31:111], 0.0)
-    ntr = tr(T.zt1[:], T.z1[:, 32:224])
-    wait("a", g.scalar, "sv", ntr)
-    act(T.m1[:, 0:64], T.zt1[:, 0:64], -BIG, BIG)
-    nm1 = act(T.m1[:, 64:96], T.zt1[:, 64:96], BIG, BIG)
-    for k in range(3):
-        red(T.car1[:, k:k + 1], T.zt1[:, 96 + 32 * k:128 + 32 * k], par=k > 0)
-    for k in range(3):
-        scan(T.pt1[:, 32 * k:32 * k + 32], T.one[:], T.zt1[:, 32 * k:32 * k + 32], T.car1[:, k:k + 1], par=k > 0)
-    wait("v", g.vector, "sa", nm1)
-    tt(T.a1[:], T.pt1[:], T.m1[:], A.max)
-    tt(T.ab1[:, 0:32], T.a1[:, 0:32], T.a1[:, 64:96], A.min)
-    cpy(T.ab1[:, 32:64], T.a1[:, 32:64], par=True)
-    ts(T.an1[:], T.ab1[:], 65520, None, A.bitwise_and)
-    tt(T.f1[:], T.ab1[:], T.an1[:], A.add)
-    tt(T.g1[:], T.f1[:], T.d0[:], A.min)
-    tr(T.h1[:], T.g1[:])
-    cpy(T.o1[:], T.h1[:])
-    cpy(T.win0[:].indirect(T.o1[:, 0:16]), T.valb[:])
+    dv = T.dmt[:, ob:ob + 31:2]
+    na = ts(T.ta[:], dv, G, None, A.bitwise_and)
+    nb = ts(T.tb[:], dv, P | G, None, A.bitwise_and)
+    nc = ts(T.tc[:], dv, Fb, None, A.bitwise_and)
+    ts(T.z0[:, 32:48], T.ta[:], 0.0, 2.0, A.is_gt, A.mult, d=na)
+    n = ts(T.z0[:, 48:64], T.tb[:], float(P), 2.0, A.is_equal, A.mult, d=nb)
+    nc = ts(T.zf[:, 32:48], T.tc[:], 0.0, 2.0, A.is_gt, A.mult, d=nc)
+    n = scan(T.z0[:, 64:96], T.z0[:, 31:63], 0.0, n)
+    nc = scan(T.zf[:, 64:96], T.zf[:, 31:63], 0.0, nc)
+    n = tr(T.zt0[:], T.z0[:, 32:96], n)
+    nzb = act(T.zb0[:], T.zt0[:, 0:32], n, f=AF.Square, scale=128.0)
+    nc = tr(T.ztf[:], T.zf[:, 32:96], nc)
+    nzbf = act(T.zbf[:], T.ztf[:, 0:32], nc, f=AF.Square, scale=128.0)
+    n = red(T.car0[:], T.zt0[:, 32:64], n)
+    nc = red(T.carf[:], T.ztf[:, 32:64], nc)
+    np0 = scan(T.pt0[:], T.zt0[:, 0:32], T.car0[:], n)
+    npf_ = scan(T.ptf[:], T.ztf[:, 0:32], T.carf[:], nc)
+    vsa(nzb)
+    n = tt(T.m0[:], T.dd[:, 0:32], T.zb0[:], A.subtract)
+    n = tt(T.a0[:], T.pt0[:], T.m0[:], A.max, n)
+    vsa(nzbf)
+    nc = tt(T.mf[:], T.dd[:, 32:64], T.zbf[:], A.subtract)
+    n = tr(T.h0[:], T.a0[:], n)
+    nc = tt(T.af[:], T.ptf[:], T.mf[:], A.max, nc)
+    nhm = tt(T.hm[:, 0:16], T.h0[:, 0:16], T.h0[:, 16:32], A.min, n)
+    nc = tr(T.hf[:], T.af[:], nc)
+    n = cpy(T.o0[:], T.hm[:, 0:16], nhm)
+    vsa(nw0)
+    n = cpy(T.win0[:].indirect(T.o0[:]), T.valb[:], n)
+    nof = cpy(T.of[:], T.hf[:, 0:16], nc)
+    nslt = tr(T.slt[:], T.hm[:], nhm)
+    act(T.rexp[:, 0:32], T.half[:], np0, scale=T.pt0[:, 31:32], bias=1.0)
+    nrx = act(T.rexp[:, 32:64], T.half[:], npf_, scale=T.ptf[:, 31:32], bias=1.0)
+    nwf = act(T.winf[:, 0:512], T.zero[:], nhb, f=AF.Identity, bias=T.hb[:])
+    nslu = act(T.slu[:], T.slt[:], nslt, scale=0.5)
+    act(T.valx[0:64, :], T.valb[0:64, :], nvalb)
+    nvx = act(T.valx[64:128, :], T.zero[64:128, 0:256])
     g.vector.wait_ge(s.xl0, 16)
-    nxq0 = V(lambda: g.vector.quantize_mx(T.xq[:, 0:256], T.xs[:, 0:256], T.xt[:, 0:1024]), True)
-    tr(T.t0[:], T.win0[:, 0:512])
-    tt(T.y0[:, 0:16], T.t0[:, 0:512:32], T.t0[:, 16:512:32], A.add)
-    tr(T.yt0[:], T.y0[:])
-    cpy(T.yt0[:, 16:32], T.yt0[:, 0:16])
-    tr(T.yu0[:], T.yt0[:])
-    ts(T.off0[:], T.yu0[:, 0:16], 256.0, None, A.add)
+    nxq0 = V(lambda: g.vector.quantize_mx(T.xq[:, 0:256], T.xs[:, 0:256], T.xt[:, 0:1024]))
+    n = tr(T.t0[:], T.win0[:, 0:512], n)
+    tt(T.y0[:, 0:16], T.t0[:, 0:512:32], T.t0[:, 16:512:32], A.add, n)
+    n = tt(T.y0[:, 32:48], T.t0[:, 0:512:32], T.t0[:, 16:512:32], A.add)
+    vsa(nrx)
+    nct = tr(T.ct[:], T.rexp[:])
+    n = tr(T.yt0[:], T.y0[:], n)
+    n = tr(T.yu0[:], T.yt0[:, 0:64:2], n)
+    n = ts(T.off0[:], T.yu0[:, 0:16], 256.0, None, A.add, d=n)
     g.vector.wait_ge(s.xl1, 16)
-    nxq = V(lambda: g.vector.quantize_mx(T.xq[:, 256:512], T.xs[:, 256:512], T.xt[:, 1024:2048]), True)
-    nq0 = cpy(b32(T.p0q[:]), b32(T.xq[:]).indirect(T.off0[:]))
-    for o_, n in ((T.winu[:, 0:512], 512), (T.winu[:, 512:960], 448), (T.yu[:], 32), (T.z3[:], 96), (T.rsum[:], 32)):
-        act(o_, T.zero[:, 0:n])
-    nz3 = act(T.z3[:, 31:32], T.zero[:, 0:1], 1.0, -1.0 / 32)
-    wait("a", g.scalar, "sv", nxq)
-    na0 = SA(lambda: g.scalar.activation(T.p0s[:], T.xs[:].indirect(T.off0[:]), AF.Copy))
+    nxq = V(lambda: g.vector.quantize_mx(T.xq[:, 256:512], T.xs[:, 256:512], T.xt[:, 1024:2048]))
+    nq0 = cpy(b32(T.p0q[:]), b32(T.xq[:]).indirect(T.off0[:]), nxq)
+    na0 = SA(lambda: g.scalar.activation(T.p0s[:], T.xs[:].indirect(T.off0[:]), AF.Copy), nxq)
+
+    wait("s", g.sync, "sa", nwf)
+    g.sync.dma_start(T.winf[:, 512:1024], T.winf[:, 0:512]).then_inc(s.wf, 16)
+    g.sync.dma_start(T.winf[:, 1024:1536], T.winf[:, 0:512]).then_inc(s.wf, 16)
     for n, r in ((nxq0, slice(0, 256)), (nxq, slice(256, 512))):
         wait("s", g.sync, "sv", n)
         g.sync.dma_start(b8(T.xwq[:, r]), b8(T.xq[:, r])).then_inc(s.xw, 16)
         g.sync.dma_start(T.xws[:, r], T.xs[:, r]).then_inc(s.xw, 16)
+
+    wait("g", g, "sa", nslu)
+    send(cp, T.slin[:], T.slu[:], "aSL")
+    wait("g", g, "sv", nct)
+    trs = []
+    for dst, land, c, h in ((cf_, T.cf, 47, 0), (cg_, T.cg, 15, 1)):
+        en = topo.engines(core, dst)
+        en = en[:len(en) // 2] if h == 0 else en[len(en) // 2:]
+        rid, pid, _se = topo.addr(dst)
+        trs.append(RemoteDMATransfer(dst_ids=[DstId(rid=rid, pnc=pid)], dma_engine_mask=sum(1 << e for e in en),
+                                     remote_sem=s.aCNT, src=T.ct[:, c:c + 4], dst=land[:]))
+        cnt["loc"] += len(en)
+    g.remote_dma_fused(trs, local_sem=s.loc)
     wait("g", g, "sv", nq0)
     send(cp, b8(T.xwq[:, 512:768]), b8(T.p0q[:]), "aS0")
     wait("g", g, "sa", na0)
     send(cp, T.xws[:, 512:768], T.p0s[:], "aS0")
 
-    ts(T.td[:, 0:16], dv, Qb, None, A.bitwise_and)
+    vsa(nwu)
+    nc = cpy(T.winu[:].indirect(T.of[:]), T.valb[:], nof)
+    nc = tr(T.tu[:], T.winu[:, 0:960], nc)
     g.vector.wait_ge(s.aDM, ncp)
-    ts(T.td[:, 16:32], T.dmp[:, 1:33:2], Qb, None, A.bitwise_and, par=True)
-    nsl = ts(T.slu[:], T.ab1[:, 0:32], float(T_), None, A.add, par=True)
-    wait("v", g.vector, "sa", nz3)
-    ts(T.w2[:], T.td[:], 0.0, None, A.is_gt)
-    cpy(T.winu[:].indirect(T.o1[:, 32:48]), T.valb[:], par=True)
-    tr(T.tu[:], T.winu[:, 0:960])
-    red(T.rsum[:, 0:1], T.z1[:, 64:80], par=True)
-    red(T.rsum[:, 1:2], T.z1[:, 32:48], par=True)
-    red(T.rsum[:, 2:3], T.w2[:, 0:16], par=True)
-    red(T.rsum[:, 3:4], T.w2[:, 16:32], par=True)
-    cpy(T.z3[0:64, 32:48], T.w2[0:64, 0:16], par=True)
-    cpy(T.z3[64:128, 32:48], T.w2[64:128, 16:32], par=True)
-    tt(T.yu[:, 0:30], T.tu[:, 0:960:32], T.tu[:, 16:960:32], A.add)
-    tr(T.rst_t[:], T.rsum[:], par=True)
-    scan(T.z3[:, 64:80], T.one[:, 0:16], T.z3[:, 31:47], 0.0, par=True)
-    ts(T.i48[:], T.i480[:], T.pf[:, 2:3], None, A.add, par=True)
-    tr(T.ytu[:], T.yu[:])
-    red(T.rtot[:], T.rst_t[:], par=True)
-    n = tr(T.zt3[:], T.z3[:, 32:96], par=True)
-    wait("a", g.scalar, "sv", n)
-    nm3 = act(T.m3[:], T.zt3[:, 0:32], -BIG, BIG)
-    cpy(T.ytu[:, 16:32], T.ytu[:, 0:16])
-    ts(T.rexp[:], T.zero[:, 0:32], T.rtot[:], None, A.add, par=True)
-    red(T.car3[:], T.zt3[:, 32:64], par=True)
-    tr(T.yuu[:], T.ytu[:])
-    tr(T.tot[:], T.rexp[:], par=True)
-    ntot = scan(T.pt3[:], T.one[:], T.zt3[:, 0:32], T.car3[:], par=True)
-    ts(T.offu[:], T.yuu[:], 256.0, None, A.add)
-    noffu = ts(T.ocol[:, 0:1], T.tot[:, 0:1], -float(EARLY), 0.0, A.add, A.max, par=True)
-    ts(T.la[:], T.i48[:, 0:16], T.ocol[:, 0:1], float(T_ - 256), A.subtract, A.add)
-    ts(T.lm[:], T.i48[:, 0:16], T.ocol[:, 0:1], None, A.is_ge, par=True)
-    npe = cpy(b32(T.peq[:]), b32(T.xq[:]).indirect(T.offu[:, 0:14]), par=True)
-    tt(T.lb[:], T.la[:], T.lm[:], A.mult)
-    fill(T.valx[64:128, :], 0)
-    tt(T.lc[:], T.lb[:], T.yuu[:, 14:30], A.add)
-    ts(T.valx[0:64, :], T.val0[0:64, :], T.pf[0:64, 0:1], None, A.add, par=True)
-    noffl = ts(T.offl[:], T.lc[:], 256.0, None, A.add)
-    wait("a", g.scalar, "sv", noffu)
-    nae = SA(lambda: g.scalar.activation(T.pes[:], T.xs[:].indirect(T.offu[:, 0:14]), AF.Copy))
+    n = ts(T.td[:], T.dmt[:, 4:67:2], Qb, None, A.bitwise_and)
+    g.vector.wait_ge(s.sg, 4)
+    ts(T.i48[:], T.i480[:], T.pf[:, 1:2], None, A.add)
+    vsa(nyu)
+    tt(T.yu[:, 0:30], T.tu[:, 0:960:32], T.tu[:, 16:960:32], A.add, nc)
+    nc = tt(T.yu[:, 32:62], T.tu[:, 0:960:32], T.tu[:, 16:960:32], A.add)
+    n = ts(T.z3[:, 32:64], T.td[:], 0.0, 2.0, A.is_gt, A.mult, d=n)
+    noc = ts(T.ocol[:], T.ct[:, 47:48], -float(EARLY), 0.0, A.add, A.max, d=nct)
+    nc = tr(T.ytu[:], T.yu[:], nc)
+    n = scan(T.z3[:, 64:96], T.z3[:, 31:63], 0.0, n)
+    ts(T.la[:], T.i48[:, 0:16], T.ocol[:], float(T_ - 256), A.subtract, A.add, d=noc)
+    nc = tr(T.yuu[:], T.ytu[:, 0:64:2], nc)
+    nlm = ts(T.lm[:], T.i48[:, 0:16], T.ocol[:], None, A.is_ge)
+    n = tr(T.zt3[:], T.z3[:, 32:96], n)
+    nzb3 = act(T.zb3[:], T.zt3[:, 0:32], n, f=AF.Square, scale=128.0)
+    noffu = ts(T.offu[:], T.yuu[:], 256.0, None, A.add, d=nc)
+    nlb = tt(T.lb[:], T.la[:], T.lm[:], A.mult, nlm)
+    n = red(T.car3[:], T.zt3[:, 32:64], n)
+    npe = cpy(b32(T.peq[:]), b32(T.xq[:]).indirect(T.offu[:, 0:14]), noffu)
+    nc = tt(T.lc[:], T.lb[:], T.yuu[:, 14:30], A.add, nlb)
+    np3 = scan(T.pt3[:], T.zt3[:, 0:32], T.car3[:], n)
+    noffl = ts(T.offl[:], T.lc[:], 256.0, None, A.add, d=nc)
+    nrx3 = act(T.rexp3[:], T.half[:], np3, scale=T.pt3[:, 31:32], bias=1.0)
+    vsa(nzb3)
+    nm3 = tt(T.m3[:], T.dd[:, 64:96], T.zb3[:], A.subtract)
+
+    nae = SA(lambda: g.scalar.activation(T.pes[:], T.xs[:].indirect(T.offu[:, 0:14]), AF.Copy), noffu)
+    u, v = T.cf[:, 0:1], T.cg[:, 0:1]
+    local_first = q < rf
+
+    def places(pt, n):
+        n = tt(T.a3[:], pt, T.m3[:], A.max, n)
+        n = tr(T.h3[:], T.a3[:], n)
+        lo, hi = (slice(0, 16), slice(16, 32)) if even else (slice(16, 32), slice(0, 16))
+        cpy(T.o3[0:64, :], T.h3[0:64, lo], n)
+        return cpy(T.o3[64:128, :], T.h3[64:128, hi])
+    if local_first:
+        no3 = places(T.pt3[:], max(np3, nm3))
     g.vector.wait_ge(s.xw, 64)
     g.vector.wait_ge(s.aS0, 2 * ncp)
-    npl = cpy(b32(T.plq[:]), b32(T.xwq[:]).indirect(T.offl[:]))
+    npl = cpy(b32(T.plq[:]), b32(T.xwq[:]).indirect(T.offl[:]), noffl)
     wait("a", g.scalar, "sv", noffl)
     g.scalar.wait_ge(s.xw, 64)
     g.scalar.wait_ge(s.aS0, 2 * ncp)
     nal = SA(lambda: g.scalar.activation(T.pls[:], T.xws[:].indirect(T.offl[:]), AF.Copy))
-    for o_, n in ((T.winf[:, 0:512], 512), (T.winf[:, 512:768], 256), (T.res0[:, ZC:RW], 32), (T.res1[:, ZC:RW], 32)):
-        nwin = act(o_, T.zero[:, 0:n])
-    wait("s", g.sync, "sv", noffl)
+    nyf = act(T.yf[:], T.zero[:, 0:128])
+    act(T.res0[:, ZC:RW], T.zero[:, 0:32])
+    nres = act(T.res1[:, ZC:RW], T.zero[:, 0:32])
+    wait("s", g.sync, "sa", nvx)
     g.sync.wait_ge(s.aSL, ncp)
     for k in range(4, 8):
         a, h = k // 2, k % 2
         g.sync.dma_start(T.valx[16 * k:16 * k + 1, :], T.slin[32 * a:32 * a + 16, 16 * h:16 * h + 16]).then_inc(s.vps, 16)
 
-    wait("g", g, "sv", nsl)
-    send(cp, T.slin[:], T.slu[:], "aSL")
-    wait("g", g, "sv", ntot)
-    trs = []
-    for dst, land, h in ((cf_, T.cf, 0), (cg_, T.cg, 1)):
-        en = topo.engines(core, dst)
-        en = en[:len(en) // 2] if h == 0 else en[len(en) // 2:]
-        rid, pid, _se = topo.addr(dst)
-        trs.append(RemoteDMATransfer(dst_ids=[DstId(rid=rid, pnc=pid)], dma_engine_mask=sum(1 << e for e in en),
-                                     remote_sem=s.aCNT, src=T.tot[:, 0:4], dst=land[:]))
-        cnt["loc"] += len(en)
-    g.remote_dma_fused(trs, local_sem=s.loc)
     wait("g", g, "sv", npe)
     send(cf_, b8(T.leq[:]), b8(T.peq[:]), "aE")
     wait("g", g, "sa", nae)
@@ -296,93 +322,81 @@ def rank_program(g, core, T, topo):
 
     g.vector.wait_ge(s.wl, 16)
     nwq = V(lambda: g.vector.quantize_mx(T.wq[:], T.ws[:], T.wt[:]))
-    ts(T.df[:], T.tb0[:], T.pf[:, 1:2], 768.0, A.add, A.add, par=True)
-    local_first, own_first = q < rf, q < rp
-    u, v, nq, npq = T.cf[:, 0:1], T.cg[:, 1:2], T.tot[:, 2:3], T.tot[:, 3:4]
+    if not local_first:
+        g.vector.wait_ge(s.aCNT, nmf)
+        n = ts(T.nf2[:], u, v, 2.0, A.add, A.mult)
+        n = ts(T.x3[:], T.pt3[:], T.nf2[:], None, A.add, d=max(n, np3))
+        no3 = places(T.x3[:], max(n, nm3))
+    vsa(nvx)
+    g.vector.wait_ge(s.vps, 64)
+    g.vector.wait_ge(s.wf, 32)
+    n = cpy(T.winf[:].indirect(T.o3[:]), T.valx[:], no3)
+    vsa(nrx3)
+    nc3 = tr(T.ct3[:], T.rexp3[:])
+    nw = tr(T.tf[:], T.winf[:, 0:1536], n)
+    vsa(nyf)
+    for o in (0, 32):
+        tt(T.yf[:, o:o + 32], T.tf[:, 0:1024:32], T.tf[:, 16:1024:32], A.add, nw)
+    for o in (64, 96):
+        nyl = tt(T.yf[:, o:o + 16], T.tf[:, 1024:1536:32], T.tf[:, 1040:1536:32], A.add)
+    if local_first:
+        g.vector.wait_ge(s.aCNT, nmf)
     col = [0]
 
     def c1():
         col[0] += 1
         return T.sc[:, col[0] - 1:col[0]]
-    nl, nf, na_ = c1(), c1(), T.lnt[:, 0:1]
-    first, second = (slice(0, 64), slice(64, 128)) if own_first else (slice(64, 128), slice(0, 64))
-    n2 = T.tot[second, 2:3] if own_first else T.tot[second, 3:4]
-    if local_first:
-        cpy(T.bcol[second, :], n2, par=True)
-    else:
-        g.vector.wait_ge(s.aCNT, nmf)
-        tt(T.nfc[:], u, v, A.add, par=True)
-        cpy(T.bcol[first, :], T.nfc[first, :])
-        tt(T.bcol[second, :], T.nfc[second, :], n2, A.add, par=True)
-    ts(T.xf[:], T.pt3[:], T.bcol[:], None, A.add)
-    wait("v", g.vector, "sa", nm3)
-    tt(T.af[:], T.xf[:], T.m3[:], A.max)
-    ts(T.lof[:], T.af[:], 15, None, A.bitwise_and)
-    ts(T.hif[:], T.af[:], 4, None, A.arith_shift_right, par=True)
-    ts(T.lo48[:], T.lof[:], 48.0, None, A.mult)
-    tt(T.plf[:], T.lo48[:], T.hif[:], A.add)
-    tt(T.mlf[:], T.plf[:], T.df[:], A.min)
-    tr(T.tf[:], T.mlf[:])
-    cpy(T.of[:], T.tf[:])
-    wait("v", g.vector, "sa", nwin)
-    g.vector.wait_ge(s.vps, 64)
-    nwf = cpy(T.winf[:].indirect(T.of[:, 0:16]), T.valx[:])
-    wait("s", g.sync, "sv", nwf)
-    nwr = 0
-    for j, d in enumerate((0, 1, 4, 5)):
-        k = 16 * (8 - d)
-        g.sync.dma_start(T.off2[0:k, 48 * j:48 * j + 48], T.winf[16 * d:128:16, 0:768]).then_inc(s.wr, 16)
-        nwr += 16
-        if d:
-            g.sync.dma_start(T.off2[k:128, 48 * j:48 * j + 48], T.winf[0:16 * d:16, 0:768]).then_inc(s.wr, 16)
-            nwr += 16
-    if local_first:
-        g.vector.wait_ge(s.aCNT, nmf)
-    ca, cb, cs = c1(), c1(), c1()
-    e0, e1 = c1(), c1()
+    nf, ca, cb, cs, e0, e1, e2 = c1(), c1(), c1(), c1(), c1(), c1(), c1()
+    nl, fst = T.ct3[:, 31:32], T.ct3[:, 15:16]
+    na_, nq = T.lnt[:, 0:1], T.lnt[:, 1:2]
     EB, LB = float(T_ + C0), float(T_ + C0 + EARLY)
-    tt(nl, nq, npq, A.add)
-    tt(nf, u, v, A.add, par=True)
-    cpy(T.lnt[:, 1:2], nq, par=True)
+    nw = tr(T.ytf[:], T.yf[:], nyl)
+    nnf = tt(nf, u, v, A.add)
+    if even:
+        nln = cpy(nq, fst, nc3)
+    else:
+        nln = tt(nq, nl, fst, A.subtract, nc3)
     if rf < rg:
-        ts(e0, u, float(EARLY), None, A.min, par=True)
-        tt(na_, nl, nf, A.add)
-        ts(cb, e0, -1.0, float(EARLY), A.mult, A.add, par=True)
+        n = ts(e0, u, float(EARLY), None, A.min)
+        nna = tt(na_, nl, nf, A.add, nnf)
+        ts(cb, e0, -1.0, float(EARLY), A.mult, A.add, d=n)
         if local_first:
-            ts(ca, nl, -1.0, EB, A.mult, A.add, par=True)
-            nln = tt(cs, nl, e0, A.add, par=True)
+            ts(ca, nl, -1.0, EB - 512.0, A.mult, A.add)
+            n = tt(cs, nl, e0, A.add)
         else:
-            ts(ca, e0, 0.0, EB, A.mult, A.add, par=True)
-            nln = cpy(cs, e0, par=True)
+            ts(ca, e0, 0.0, EB - 512.0, A.mult, A.add)
+            n = cpy(cs, e0)
     else:
-        ts(e0, u, -float(EARLY), 0.0, A.add, A.max, par=True)
-        tt(na_, nl, nf, A.add)
-        tt(e1, e0, v, A.add, par=True)
+        n = ts(e0, u, -float(EARLY), 0.0, A.add, A.max)
+        nna = tt(na_, nl, nf, A.add, nnf)
+        n1 = tt(e1, e0, v, A.add, n)
         if local_first:
-            e2 = c1()
-            tt(e2, e0, nl, A.subtract, par=True)
-            tt(cs, nl, v, A.add, par=True)
-            ts(ca, e2, LB, None, A.add)
+            n = tt(e2, e0, nl, A.subtract)
+            tt(cs, nl, v, A.add)
+            ts(cb, e1, -1.0, -float(EARLY), A.mult, A.add, d=n1)
+            n = ts(ca, e2, LB - 512.0, None, A.add, d=n)
         else:
-            ts(ca, e0, LB, None, A.add, par=True)
             cpy(cs, v)
-        nln = ts(cb, e1, -1.0, -float(EARLY), A.mult, A.add, par=True)
+            ts(ca, e0, LB - 512.0, None, A.add)
+            n = ts(cb, e1, -1.0, -float(EARLY), A.mult, A.add, d=n1)
+    nln = max(nln, nna)
+    nw = tr(T.yff[:], T.ytf[:, 0:128:2], nw)
     ii = T.i48[:]
-    ts(T.fx[:], ii, cs, cb, A.is_ge, A.mult)
-    ts(T.fy[:], ii, ca, None, A.add, par=True)
+    ts(T.fx[:], ii, cs, cb, A.is_ge, A.mult, d=n)
+    ny = ts(T.fy[:], ii, ca, None, A.add)
+    cpy(T.sw[0:64, :], T.yff[64:128, 0:48], nw)
+    nsw = cpy(T.sw[64:128, :], T.yff[0:64, 0:48])
     if local_first:
-        ts(T.fin[:], ii, nl, None, A.is_ge, par=True)
+        ts(T.fin[:], ii, nl, None, A.is_ge)
     else:
-        ts(T.fin[:], ii, nf, None, A.is_lt, par=True)
-    ts(T.fe[:], ii, na_, 4096.0, A.is_ge, A.mult, par=True)
-    tt(T.fz[:], T.fx[:], T.fy[:], A.add)
-    tt(T.fr[:], T.fz[:], T.fin[:], A.mult)
-    tt(T.fs[:], T.fr[:], T.fe[:], A.add)
-    g.vector.wait_ge(s.wr, nwr)
-    tt(T.fq[:], T.off2[:, 0:96], T.off2[:, 96:192], A.add)
-    tt(T.fl[:], T.fq[:, 0:48], T.fq[:, 48:96], A.add)
-    tt(T.fl2[:], T.fl[:], T.fs[:], A.add)
-    noff = ts(T.offf[:], T.fl2[:], float(ZC), None, A.min)
+        ts(T.fin[:], ii, nf, None, A.is_lt)
+    nz = tt(T.fz[:], T.fx[:], T.fy[:], A.add, ny)
+    nfe = ts(T.fe[:], ii, na_, 4096.0, A.is_ge, A.mult, d=nna)
+    nz = tt(T.fr[:], T.fz[:], T.fin[:], A.mult, nz)
+    n = tt(T.fl[:], T.yff[:, 0:48], T.sw[:], A.add, nsw)
+    nz = tt(T.fs[:], T.fr[:], T.fe[:], A.add, max(nz, nfe))
+    n = tt(T.fl2[:], T.fl[:], T.fs[:], A.add, nz)
+    noff = ts(T.offf[:], T.fl2[:], float(ZC), None, A.min, d=n)
 
     def mm(bank, o, qb, sbuf, a, n):
         g.tensor.matmul_mx(T.ps[:, 512 * bank:512 * bank + n], T.wq[:, 128 * o:128 * o + 128], T.ws[:, 128 * o:128 * o + 128],
@@ -394,8 +408,6 @@ def rank_program(g, core, T, topo):
         if sem:
             g.tensor.wait_ge(s[sem], k)
         for o in range(2):
-            if cnt["st"]:
-                g.tensor.wait_ge(s.st, cnt["st"])
             mm(2 * bank + o, o, qb, sbuf, a, n)
     res = (T.res0, T.res1)
     base = (0, T_, T_ + C0, T_ + C0 + EARLY)
@@ -405,16 +417,15 @@ def rank_program(g, core, T, topo):
             wait("a", g.scalar, "st", 2 * b + o + 1)
             ncop = act(res[o][:, base[b]:base[b] + width[b]], T.ps[:, 512 * (2 * b + o):512 * (2 * b + o) + width[b]])
     wait("a", g.scalar, "st", 8)
-    act(res[1][:, base[3]:base[3] + 256], T.ps[:, 512 * 7:512 * 7 + 256])
+    nlast = act(res[1][:, base[3]:base[3] + 256], T.ps[:, 512 * 7:512 * 7 + 256])
     wait("v", g.vector, "st", 7)
-    cpy(res[0][:, base[3]:base[3] + 256], T.ps[:, 512 * 6:512 * 6 + 256])
-    wait("v", g.vector, "sa", ncop)
-    wait("a", g.scalar, "sv", noff)
+    n = cpy(res[0][:, base[3]:base[3] + 256], T.ps[:, 512 * 6:512 * 6 + 256])
+    vsa(max(ncop, nres))
     for k in range(len(CUTS) - 1):
         a, b = CUTS[k], CUTS[k + 1]
         of = T.offf[:, a // 16:b // 16]
-        n0 = cpy(T.yt_0[:, a:b], T.res0[:].indirect(of), par=k > 0)
-        n1 = SA(lambda: g.scalar.activation(T.yt_1[:, a:b], T.res1[:].indirect(of), AF.Copy))
+        n0 = cpy(T.yt_0[:, a:b], T.res0[:].indirect(of), n)
+        n1 = SA(lambda: g.scalar.activation(T.yt_1[:, a:b], T.res1[:].indirect(of), AF.Copy), noff, nlast)
         if k == 0:
             wait("s", g.sync, "sv", nln)
             g.sync.dma_start(T.ln[:, :], T.lnt[0:1, :]).then_inc(s.yst, 16)

@@ -4,10 +4,13 @@ from concourse.mybir import dt, AluOpType, AxisListType, ActivationFunctionType
 
 T_, S_, C0, C1 = 512, 768, 256, 480
 EARLY = C1 - C0
-RW = T_ + C0 + C1 + 32
-ZC = T_ + C0 + C1
+FB = T_ + C0
+RW = FB + C1 + 32
+ZC = FB + C1
 CUTS = (0, 256, 768)
 FAR = 16 * 127 + 16
+PL, PH = 1280.0, 1024.0
+LOC = PL + 2 * PH - 256.0
 
 F32, I32, U16, BF = "float32", "int32", "uint16", "bfloat16"
 Q4, U8 = "float8_e4m3fn_x4", "uint8"
@@ -25,9 +28,10 @@ SCRATCH = {
     "p0q": sb(256, Q4), "p0s": sb(256, U8),
     "peq": sb(EARLY, Q4), "pes": sb(EARLY, U8), "plq": sb(256, Q4), "pls": sb(256, U8),
     "leq": sb(EARLY, Q4), "les": sb(EARLY, U8), "llq": sb(256, Q4), "lls": sb(256, U8),
-    "zero": sb(512, BF), "one": sb(32, F32), "half": sb(32, F32), "hb": sb(1, F32),
+    "zero": sb(512, BF), "one": sb(32, F32), "half": sb(32, F32), "nhalf": sb(32, F32), "hb": sb(1, F32),
     "pi": sb(2, I32), "pint": sb(8, I32), "pf": sb(8, F32),
     "val0": sb(256, F32), "valb": sb(256, BF), "valx": sb(256, BF), "dd": sb(96, F32), "i480": sb(48, F32), "i48": sb(48, F32),
+    "dfl": sb(16, F32),
     "ta": sb(16, I32), "tb": sb(16, I32), "tc": sb(16, I32), "td": sb(32, I32),
     "z0": sb(96, F32), "zt0": sb(64, F32), "car0": sb(1, F32), "pt0": sb(32, F32), "zb0": sb(32, F32), "m0": sb(32, F32),
     "a0": sb(32, F32), "h0": sb(32, F32), "hm": sb(32, F32), "o0": sb(16, U16), "slt": sb(32, F32),
@@ -40,11 +44,11 @@ SCRATCH = {
     "winf": sb(1536 + FAR, BF), "tf": sb(1536, BF), "yf": sb(128, F32), "ytf": sb(128, F32), "yff": sb(64, F32), "sw": sb(48, F32),
     "slu": sb(32, BF), "slin": sb(32, BF),
     "rexp": sb(64, F32), "ct": sb(64, F32), "rexp3": sb(32, F32), "ct3": sb(32, F32),
-    "cf": sb(4, F32), "cg": sb(4, F32), "ocol": sb(1, F32), "nf2": sb(1, F32),
-    "la": sb(16, F32), "lm": sb(16, F32), "lb": sb(16, F32), "lc": sb(16, F32), "offl": sb(16, U16),
+    "cf": sb(4, F32), "cg": sb(4, F32), "nf2": sb(1, F32),
+    "lc": sb(16, F32), "offl": sb(16, U16),
     "sc": sb(16, F32), "lnt": sb(2, F32),
-    "fx": sb(48, F32), "fy": sb(48, F32), "fz": sb(48, F32), "fin": sb(48, F32), "fr": sb(48, F32), "fe": sb(48, F32),
-    "fs": sb(48, F32), "fl": sb(48, F32), "fl2": sb(48, F32), "offf": sb(48, U16),
+    "fst": sb(48, F32), "fd": sb(48, F32), "fl1": sb(48, F32), "fz": sb(48, F32), "fsd": sb(48, F32), "ff": sb(48, F32),
+    "fm": sb(48, F32), "fl": sb(48, F32), "fl2": sb(48, F32), "offf": sb(48, U16),
     "res0": sb(RW, F32), "res1": sb(RW, F32), "yt_0": sb(768, F32), "yt_1": sb(768, F32),
     "ps": ("psum", [128, 4096], F32),
 }
@@ -146,42 +150,40 @@ def rank_program(g, core, T, topo):
 
     FL = {"allow_small_or_imprecise_dtypes": True}
     g.iota(T.pi[:, 0:1], [[1, 1]], 0, 1).then_inc(s.sg, 1)
-    g.iota(T.dd[:], [[512, 3], [0, 2], [1, 16]], 512, 16, **FL).then_inc(s.sg, 1)
     g.iota(T.val0[:], [[32, 16], [1, 16]], -256, 0, **FL).then_inc(s.sg, 1)
+    g.iota(T.dd[:], [[512, 3], [0, 2], [1, 16]], 512, 16, **FL).then_inc(s.sg, 1)
     g.wait_ge(s.dml, 128)
     send(cp, T.dmt[:, ob:ob + 31], T.dmt[:, ob:ob + 31], "aDM")
     g.iota(T.i480[:], [[16, 48]], 0, 0, **FL).then_inc(s.sg, 1)
 
     nzero = fill(T.zero[:], 0.0)
-    n = fill(T.zf[:], 0.0)
-    fill(T.one[:], 1.0)
-    fill(T.z0[:, 31:32], -2.0 / 32)
-    fill(T.zf[:, 31:32], -2.0 / 32, n)
-    fill(T.half[:], 0.5)
-    fill(T.y0[:], 0.0)
-    fill(T.hm[:], 0.0)
     g.vector.wait_ge(s.sg, 1)
     ts(T.pint[:, 0:1], T.pi[:, 0:1], 16, None, A.bitwise_and)
     n = ts(T.pint[:, 1:2], T.pi[:, 0:1], 15, None, A.bitwise_and)
-    fill(T.z3[:, 31:32], -2.0 / 32)
+    nz = fill(T.zf[:], 0.0)
     npf = cpy(T.pf[:, 0:2], T.pint[:, 0:2], n)
-    fill(T.hb[0:64, :], 256.0)
-    nhb = fill(T.hb[64:128, :], 0.0)
-    g.vector.wait_ge(s.sg, 3)
-    nvalb = ts(T.valb[:], T.val0[:], T.pf[:, 0:1], None, A.add, d=npf)
+    fill(T.one[:], 1.0)
+    fill(T.z0[:, 31:32], C0 / 16.0)
+    fill(T.zf[:, 31:32], -2.0 / 32, nz)
+    fill(T.z3[:, 31:32], -2.0 / 32)
+    fill(T.half[:], 0.5)
+    fill(T.nhalf[:], -0.5)
+    fill(T.hb[0:64, :], PL)
+    nhb = fill(T.hb[64:128, :], PH)
+    fill(T.y0[:], 0.0)
+    fill(T.hm[:], 0.0)
 
     nw0 = act(T.win0[:, 0:512], T.zero[:], nzero)
-    act(T.winu[:, 0:512], T.zero[:])
-    nwu = act(T.winu[:, 512:960], T.zero[:, 0:448])
-    nyu = act(T.yu[:], T.zero[:, 0:64])
+    g.scalar.wait_ge(s.sg, 3)
+    nvalb = act(T.valb[:], T.val0[:], npf, f=AF.Identity, bias=T.pf[:, 0:1])
 
     g.vector.wait_ge(s.dml, 128)
     dv = T.dmt[:, ob:ob + 31:2]
     na = ts(T.ta[:], dv, G, None, A.bitwise_and)
     nb = ts(T.tb[:], dv, P | G, None, A.bitwise_and)
     nc = ts(T.tc[:], dv, Fb, None, A.bitwise_and)
-    ts(T.z0[:, 32:48], T.ta[:], 0.0, 2.0, A.is_gt, A.mult, d=na)
-    n = ts(T.z0[:, 48:64], T.tb[:], float(P), 2.0, A.is_equal, A.mult, d=nb)
+    ts(T.z0[:, 32:48], T.ta[:], 0.0, -2.0, A.is_gt, A.mult, d=na)
+    n = ts(T.z0[:, 48:64], T.tb[:], float(P), -2.0, A.is_equal, A.mult, d=nb)
     nc = ts(T.zf[:, 32:48], T.tc[:], 0.0, 2.0, A.is_gt, A.mult, d=nc)
     n = scan(T.z0[:, 64:96], T.z0[:, 31:63], 0.0, n)
     nc = scan(T.zf[:, 64:96], T.zf[:, 31:63], 0.0, nc)
@@ -192,9 +194,10 @@ def rank_program(g, core, T, topo):
     n = red(T.car0[:], T.zt0[:, 32:64], n)
     nc = red(T.carf[:], T.ztf[:, 32:64], nc)
     np0 = scan(T.pt0[:], T.zt0[:, 0:32], T.car0[:], n)
-    npf_ = scan(T.ptf[:], T.ztf[:, 0:32], T.carf[:], nc)
+    g.vector.wait_ge(s.sg, 3)
     vsa(nzb)
     n = tt(T.m0[:], T.dd[:, 0:32], T.zb0[:], A.subtract)
+    npf_ = scan(T.ptf[:], T.ztf[:, 0:32], T.carf[:], nc)
     n = tt(T.a0[:], T.pt0[:], T.m0[:], A.max, n)
     vsa(nzbf)
     nc = tt(T.mf[:], T.dd[:, 32:64], T.zbf[:], A.subtract)
@@ -203,38 +206,44 @@ def rank_program(g, core, T, topo):
     nhm = tt(T.hm[:, 0:16], T.h0[:, 0:16], T.h0[:, 16:32], A.min, n)
     nc = tr(T.hf[:], T.af[:], nc)
     n = cpy(T.o0[:], T.hm[:, 0:16], nhm)
-    vsa(nw0)
+    nslt = tr(T.slt[:], T.hm[:])
+    vsa(max(nw0, nvalb))
     n = cpy(T.win0[:].indirect(T.o0[:]), T.valb[:], n)
-    nof = cpy(T.of[:], T.hf[:, 0:16], nc)
-    nslt = tr(T.slt[:], T.hm[:], nhm)
-    act(T.rexp[:, 0:32], T.half[:], np0, scale=T.pt0[:, 31:32], bias=1.0)
+    act(T.rexp[:, 0:32], T.nhalf[:], np0, scale=T.pt0[:, 31:32], bias=float(C0))
     nrx = act(T.rexp[:, 32:64], T.half[:], npf_, scale=T.ptf[:, 31:32], bias=1.0)
     nwf = act(T.winf[:, 0:512], T.zero[:], nhb, f=AF.Identity, bias=T.hb[:])
+    act(T.winu[:, 0:512], T.zero[:], bias=-4096.0)
     nslu = act(T.slu[:], T.slt[:], nslt, scale=0.5)
-    act(T.valx[0:64, :], T.valb[0:64, :], nvalb)
+    nwu = act(T.winu[:, 512:960], T.zero[:, 0:448], bias=-4096.0)
+    act(T.valx[0:64, :], T.valb[0:64, :], 0, nvalb)
     nvx = act(T.valx[64:128, :], T.zero[64:128, 0:256])
+    g.scalar.wait_ge(s.sg, 4)
+    ni48 = act(T.i48[:], T.i480[:], f=AF.Identity, bias=T.pf[:, 1:2])
+    nyu = act(T.yu[:], T.zero[:, 0:64])
+    ndfl = act(T.dfl[:], T.i48[:, 0:16], 0, ni48, bias=-float(T_))
     g.vector.wait_ge(s.xl0, 16)
     nxq0 = V(lambda: g.vector.quantize_mx(T.xq[:, 0:256], T.xs[:, 0:256], T.xt[:, 0:1024]))
     n = tr(T.t0[:], T.win0[:, 0:512], n)
+    nof = cpy(T.of[:], T.hf[:, 0:16], nc)
     tt(T.y0[:, 0:16], T.t0[:, 0:512:32], T.t0[:, 16:512:32], A.add, n)
     n = tt(T.y0[:, 32:48], T.t0[:, 0:512:32], T.t0[:, 16:512:32], A.add)
     vsa(nrx)
     nct = tr(T.ct[:], T.rexp[:])
     n = tr(T.yt0[:], T.y0[:], n)
     n = tr(T.yu0[:], T.yt0[:, 0:64:2], n)
-    n = ts(T.off0[:], T.yu0[:, 0:16], 256.0, None, A.add, d=n)
     g.vector.wait_ge(s.xl1, 16)
     nxq = V(lambda: g.vector.quantize_mx(T.xq[:, 256:512], T.xs[:, 256:512], T.xt[:, 1024:2048]))
-    nq0 = cpy(b32(T.p0q[:]), b32(T.xq[:]).indirect(T.off0[:]), nxq)
-    na0 = SA(lambda: g.scalar.activation(T.p0s[:], T.xs[:].indirect(T.off0[:]), AF.Copy), nxq)
+    noff0 = ts(T.off0[:], T.yu0[:, 0:16], 256.0, None, A.add, d=n)
+    nq0 = cpy(b32(T.p0q[:]), b32(T.xq[:]).indirect(T.off0[:]), noff0)
+    na0 = SA(lambda: g.scalar.activation(T.p0s[:], T.xs[:].indirect(T.off0[:]), AF.Copy), noff0)
 
     wait("s", g.sync, "sa", nwf)
     g.sync.dma_start(T.winf[:, 512:1024], T.winf[:, 0:512]).then_inc(s.wf, 16)
     g.sync.dma_start(T.winf[:, 1024:1536], T.winf[:, 0:512]).then_inc(s.wf, 16)
-    for n, r in ((nxq0, slice(0, 256)), (nxq, slice(256, 512))):
+    for n, a in ((nxq0, 0), (nxq, 256)):
         wait("s", g.sync, "sv", n)
-        g.sync.dma_start(b8(T.xwq[:, r]), b8(T.xq[:, r])).then_inc(s.xw, 16)
-        g.sync.dma_start(T.xws[:, r], T.xs[:, r]).then_inc(s.xw, 16)
+        g.sync.dma_start(b8(T.xwq[:, C0 + a:C0 + a + 256]), b8(T.xq[:, a:a + 256])).then_inc(s.xw, 16)
+        g.sync.dma_start(T.xws[:, C0 + a:C0 + a + 256], T.xs[:, a:a + 256]).then_inc(s.xw, 16)
 
     wait("g", g, "sa", nslu)
     send(cp, T.slin[:], T.slu[:], "aSL")
@@ -249,52 +258,38 @@ def rank_program(g, core, T, topo):
         cnt["loc"] += len(en)
     g.remote_dma_fused(trs, local_sem=s.loc)
     wait("g", g, "sv", nq0)
-    send(cp, b8(T.xwq[:, 512:768]), b8(T.p0q[:]), "aS0")
+    send(cp, b8(T.xwq[:, 0:C0]), b8(T.p0q[:]), "aS0")
     wait("g", g, "sa", na0)
-    send(cp, T.xws[:, 512:768], T.p0s[:], "aS0")
+    send(cp, T.xws[:, 0:C0], T.p0s[:], "aS0")
 
     vsa(nwu)
     nc = cpy(T.winu[:].indirect(T.of[:]), T.valb[:], nof)
-    nc = tr(T.tu[:], T.winu[:, 0:960], nc)
     g.vector.wait_ge(s.aDM, ncp)
     n = ts(T.td[:], T.dmt[:, 4:67:2], Qb, None, A.bitwise_and)
-    g.vector.wait_ge(s.sg, 4)
-    ts(T.i48[:], T.i480[:], T.pf[:, 1:2], None, A.add)
-    vsa(nyu)
-    tt(T.yu[:, 0:30], T.tu[:, 0:960:32], T.tu[:, 16:960:32], A.add, nc)
-    nc = tt(T.yu[:, 32:62], T.tu[:, 0:960:32], T.tu[:, 16:960:32], A.add)
+    nc = tr(T.tu[:], T.winu[:, 0:960], nc)
     n = ts(T.z3[:, 32:64], T.td[:], 0.0, 2.0, A.is_gt, A.mult, d=n)
-    noc = ts(T.ocol[:], T.ct[:, 47:48], -float(EARLY), 0.0, A.add, A.max, d=nct)
-    nc = tr(T.ytu[:], T.yu[:], nc)
+    vsa(nyu)
+    tt(T.yu[:, 0:30], T.tu[:, 0:960:32], T.tu[:, 16:960:32], A.max, nc)
+    nc = tt(T.yu[:, 32:62], T.tu[:, 0:960:32], T.tu[:, 16:960:32], A.max)
     n = scan(T.z3[:, 64:96], T.z3[:, 31:63], 0.0, n)
-    ts(T.la[:], T.i48[:, 0:16], T.ocol[:], float(T_ - 256), A.subtract, A.add, d=noc)
-    nc = tr(T.yuu[:], T.ytu[:, 0:64:2], nc)
-    nlm = ts(T.lm[:], T.i48[:, 0:16], T.ocol[:], None, A.is_ge)
+    nc = tr(T.ytu[:], T.yu[:], nc)
     n = tr(T.zt3[:], T.z3[:, 32:96], n)
     nzb3 = act(T.zb3[:], T.zt3[:, 0:32], n, f=AF.Square, scale=128.0)
-    noffu = ts(T.offu[:], T.yuu[:], 256.0, None, A.add, d=nc)
-    nlb = tt(T.lb[:], T.la[:], T.lm[:], A.mult, nlm)
+    nc = tr(T.yuu[:], T.ytu[:, 0:64:2], nc)
     n = red(T.car3[:], T.zt3[:, 32:64], n)
+    noffu = ts(T.offu[:], T.yuu[:], 256.0, None, A.add, d=nc)
+    vsa(ndfl)
+    nc = tt(T.lc[:], T.dfl[:], T.yuu[:, 14:30], A.max)
     npe = cpy(b32(T.peq[:]), b32(T.xq[:]).indirect(T.offu[:, 0:14]), noffu)
-    nc = tt(T.lc[:], T.lb[:], T.yuu[:, 14:30], A.add, nlb)
+    noffl = ts(T.offl[:], T.lc[:], float(T_), None, A.add, d=nc)
     np3 = scan(T.pt3[:], T.zt3[:, 0:32], T.car3[:], n)
-    noffl = ts(T.offl[:], T.lc[:], 256.0, None, A.add, d=nc)
-    nrx3 = act(T.rexp3[:], T.half[:], np3, scale=T.pt3[:, 31:32], bias=1.0)
     vsa(nzb3)
     nm3 = tt(T.m3[:], T.dd[:, 64:96], T.zb3[:], A.subtract)
 
     nae = SA(lambda: g.scalar.activation(T.pes[:], T.xs[:].indirect(T.offu[:, 0:14]), AF.Copy), noffu)
+    nrx3 = act(T.rexp3[:], T.half[:], np3, scale=T.pt3[:, 31:32], bias=1.0)
     u, v = T.cf[:, 0:1], T.cg[:, 0:1]
     local_first = q < rf
-
-    def places(pt, n):
-        n = tt(T.a3[:], pt, T.m3[:], A.max, n)
-        n = tr(T.h3[:], T.a3[:], n)
-        lo, hi = (slice(0, 16), slice(16, 32)) if even else (slice(16, 32), slice(0, 16))
-        cpy(T.o3[0:64, :], T.h3[0:64, lo], n)
-        return cpy(T.o3[64:128, :], T.h3[64:128, hi])
-    if local_first:
-        no3 = places(T.pt3[:], max(np3, nm3))
     g.vector.wait_ge(s.xw, 64)
     g.vector.wait_ge(s.aS0, 2 * ncp)
     npl = cpy(b32(T.plq[:]), b32(T.xwq[:]).indirect(T.offl[:]), noffl)
@@ -320,97 +315,82 @@ def rank_program(g, core, T, topo):
     wait("g", g, "sa", nal)
     send(cf_, T.lls[:], T.pls[:], "aL")
 
+    fline = rf < rg
+    first = u if fline else v
+    nl, fst = T.ct3[:, 31:32], T.ct3[:, 15:16]
+    na_, nq = T.lnt[:, 0:1], T.lnt[:, 1:2]
+    nf, c1, ba, cz = T.sc[:, 0:1], T.sc[:, 2:3], T.sc[:, 3:4], T.sc[:, 4:5]
+    pt, np_ = T.pt3, np3
     g.vector.wait_ge(s.wl, 16)
-    nwq = V(lambda: g.vector.quantize_mx(T.wq[:], T.ws[:], T.wt[:]))
     if not local_first:
         g.vector.wait_ge(s.aCNT, nmf)
         n = ts(T.nf2[:], u, v, 2.0, A.add, A.mult)
-        n = ts(T.x3[:], T.pt3[:], T.nf2[:], None, A.add, d=max(n, np3))
-        no3 = places(T.x3[:], max(n, nm3))
+    nwq = V(lambda: g.vector.quantize_mx(T.wq[:], T.ws[:], T.wt[:]))
+    if not local_first:
+        np_ = ts(T.x3[:], T.pt3[:], T.nf2[:], None, A.add, d=max(n, np3))
+        pt = T.x3
+    vsa(nrx3)
+    nc3 = tr(T.ct3[:], T.rexp3[:])
+    n3 = tt(T.a3[:], pt[:], T.m3[:], A.max, max(np_, nm3))
+    g.vector.wait_ge(s.aCNT, nmf)
+    nnf = tt(nf, u, v, A.add)
+    if local_first:
+        cs = T.sc[:, 1:2]
+        ncs = tt(cs, nl, first, A.add, nc3)
+    else:
+        cs, ncs = first, 0
+    n3 = tr(T.h3[:], T.a3[:], n3)
+    nna = tt(na_, nl, nf, A.add, max(nnf, nc3))
+    if local_first:
+        ts(c1, nl, -1.0 if fline else 1.0, 0.0 if fline else C1 - 1.0, A.mult, A.add)
+        n1 = ts(ba, cs, nl, C1 - 1.0, A.add, A.add, d=ncs)
+    else:
+        c1 = 0.0 if fline else C1 - 1.0
+        n1 = ts(ba, cs, C1 - 1.0, None, A.add)
+    lo, hi = (slice(0, 16), slice(16, 32)) if even else (slice(16, 32), slice(0, 16))
+    cpy(T.o3[0:64, :], T.h3[0:64, lo], n3)
+    no3 = cpy(T.o3[64:128, :], T.h3[64:128, hi])
+    ncz = ts(cz, na_, -4096.0, 4096.0, A.mult, A.add, d=nna)
+    ii = T.i48[:]
+    act(T.fl1[:], ii, n1, f=AF.Identity, scale=1.0 if fline else -1.0, bias=c1)
+    act(T.fd[:], ii, f=AF.Identity, scale=-2.0, bias=ba)
+    nfz = act(T.fz[:], ii, ncz, f=AF.Relu, scale=4096.0, bias=cz)
+    nln = max(nna, cpy(nq, fst) if even else tt(nq, nl, fst, A.subtract))
     vsa(nvx)
     g.vector.wait_ge(s.vps, 64)
     g.vector.wait_ge(s.wf, 32)
     n = cpy(T.winf[:].indirect(T.o3[:]), T.valx[:], no3)
-    vsa(nrx3)
-    nc3 = tr(T.ct3[:], T.rexp3[:])
+    nst = ts(T.fst[:], ii, cs, None, A.is_ge, d=ncs)
     nw = tr(T.tf[:], T.winf[:, 0:1536], n)
-    vsa(nyf)
+    vsa(nfz)
+    nst = tt(T.fsd[:], T.fst[:], T.fd[:], A.mult, nst)
     for o in (0, 32):
         tt(T.yf[:, o:o + 32], T.tf[:, 0:1024:32], T.tf[:, 16:1024:32], A.add, nw)
     for o in (64, 96):
-        nyl = tt(T.yf[:, o:o + 16], T.tf[:, 1024:1536:32], T.tf[:, 1040:1536:32], A.add)
-    if local_first:
-        g.vector.wait_ge(s.aCNT, nmf)
-    col = [0]
-
-    def c1():
-        col[0] += 1
-        return T.sc[:, col[0] - 1:col[0]]
-    nf, ca, cb, cs, e0, e1, e2 = c1(), c1(), c1(), c1(), c1(), c1(), c1()
-    nl, fst = T.ct3[:, 31:32], T.ct3[:, 15:16]
-    na_, nq = T.lnt[:, 0:1], T.lnt[:, 1:2]
-    EB, LB = float(T_ + C0), float(T_ + C0 + EARLY)
-    nw = tr(T.ytf[:], T.yf[:], nyl)
-    nnf = tt(nf, u, v, A.add)
-    if even:
-        nln = cpy(nq, fst, nc3)
-    else:
-        nln = tt(nq, nl, fst, A.subtract, nc3)
-    if rf < rg:
-        n = ts(e0, u, float(EARLY), None, A.min)
-        nna = tt(na_, nl, nf, A.add, nnf)
-        ts(cb, e0, -1.0, float(EARLY), A.mult, A.add, d=n)
-        if local_first:
-            ts(ca, nl, -1.0, EB - 512.0, A.mult, A.add)
-            n = tt(cs, nl, e0, A.add)
-        else:
-            ts(ca, e0, 0.0, EB - 512.0, A.mult, A.add)
-            n = cpy(cs, e0)
-    else:
-        n = ts(e0, u, -float(EARLY), 0.0, A.add, A.max)
-        nna = tt(na_, nl, nf, A.add, nnf)
-        n1 = tt(e1, e0, v, A.add, n)
-        if local_first:
-            n = tt(e2, e0, nl, A.subtract)
-            tt(cs, nl, v, A.add)
-            ts(cb, e1, -1.0, -float(EARLY), A.mult, A.add, d=n1)
-            n = ts(ca, e2, LB - 512.0, None, A.add, d=n)
-        else:
-            cpy(cs, v)
-            ts(ca, e0, LB - 512.0, None, A.add)
-            n = ts(cb, e1, -1.0, -float(EARLY), A.mult, A.add, d=n1)
-    nln = max(nln, nna)
+        nw = tt(T.yf[:, o:o + 16], T.tf[:, 1024:1536:32], T.tf[:, 1040:1536:32], A.add)
+    nst = tt(T.ff[:], T.fl1[:], T.fsd[:], A.add if fline else A.subtract, nst)
+    nw = tr(T.ytf[:], T.yf[:], nw)
+    nst = tt(T.fm[:], T.ff[:], T.fz[:], A.max, nst)
     nw = tr(T.yff[:], T.ytf[:, 0:128:2], nw)
-    ii = T.i48[:]
-    ts(T.fx[:], ii, cs, cb, A.is_ge, A.mult, d=n)
-    ny = ts(T.fy[:], ii, ca, None, A.add)
-    cpy(T.sw[0:64, :], T.yff[64:128, 0:48], nw)
-    nsw = cpy(T.sw[64:128, :], T.yff[0:64, 0:48])
-    if local_first:
-        ts(T.fin[:], ii, nl, None, A.is_ge)
-    else:
-        ts(T.fin[:], ii, nf, None, A.is_lt)
-    nz = tt(T.fz[:], T.fx[:], T.fy[:], A.add, ny)
-    nfe = ts(T.fe[:], ii, na_, 4096.0, A.is_ge, A.mult, d=nna)
-    nz = tt(T.fr[:], T.fz[:], T.fin[:], A.mult, nz)
-    n = tt(T.fl[:], T.yff[:, 0:48], T.sw[:], A.add, nsw)
-    nz = tt(T.fs[:], T.fr[:], T.fe[:], A.add, max(nz, nfe))
-    n = tt(T.fl2[:], T.fl[:], T.fs[:], A.add, nz)
-    noff = ts(T.offf[:], T.fl2[:], float(ZC), None, A.min, d=n)
+    ts(T.sw[0:64, :], T.yff[64:128, 0:48], -LOC - FB, None, A.add, d=nw)
+    n = ts(T.sw[64:128, :], T.yff[0:64, 0:48], -LOC - FB, None, A.add)
+    n = tt(T.fl[:], T.yff[:, 0:48], T.sw[:], A.add, n)
+    n = tt(T.fl2[:], T.fl[:], T.fm[:], A.min, max(n, nst))
+    noff = ts(T.offf[:], T.fl2[:], float(FB), float(ZC), A.add, A.min, d=n)
 
     def mm(bank, o, qb, sbuf, a, n):
         g.tensor.matmul_mx(T.ps[:, 512 * bank:512 * bank + n], T.wq[:, 128 * o:128 * o + 128], T.ws[:, 128 * o:128 * o + 128],
                            qb[:, a:a + n], sbuf[:, a:a + n], True, True).then_inc(s.st, 1)
         cnt["st"] += 1
     g.tensor.wait_ge(s.sv, nwq)
-    for bank, (qb, sbuf, a, n, sem, k) in enumerate(((T.xq, T.xs, 0, 512, None, 0), (T.xwq, T.xws, 512, 256, "aS0", 2 * ncp),
+    for bank, (qb, sbuf, a, n, sem, k) in enumerate(((T.xq, T.xs, 0, 512, None, 0), (T.xwq, T.xws, 0, 256, "aS0", 2 * ncp),
                                                      (T.leq, T.les, 0, EARLY, "aE", 2 * nmf), (T.llq, T.lls, 0, 256, "aL", 2 * nmf))):
         if sem:
             g.tensor.wait_ge(s[sem], k)
         for o in range(2):
             mm(2 * bank + o, o, qb, sbuf, a, n)
     res = (T.res0, T.res1)
-    base = (0, T_, T_ + C0, T_ + C0 + EARLY)
+    base = (0, T_, FB, FB + EARLY)
     width = (512, 256, EARLY, 256)
     for b in range(3):
         for o in range(2):

@@ -28,22 +28,21 @@ SCRATCH = {
     "p0q": sb(256, Q4), "p0s": sb(256, U8),
     "peq": sb(EARLY, Q4), "pes": sb(EARLY, U8), "plq": sb(256, Q4), "pls": sb(256, U8),
     "leq": sb(EARLY, Q4), "les": sb(EARLY, U8), "llq": sb(256, Q4), "lls": sb(256, U8),
-    "zero": sb(512, BF), "one": sb(32, F32), "half": sb(32, F32), "nhalf": sb(32, F32), "hb": sb(1, F32),
+    "zero": sb(512, BF), "one": sb(32, F32), "half": sb(32, F32), "hpm": sb(32, F32), "hb": sb(1, F32), "cb": sb(1, F32),
+    "sgn": sb(1, F32),
     "pi": sb(2, I32), "pint": sb(8, I32), "pf": sb(8, F32),
-    "val0": sb(256, F32), "valb": sb(256, BF), "valx": sb(256, BF), "dd": sb(96, F32), "i480": sb(48, F32), "i48": sb(48, F32),
+    "val0": sb(256, F32), "valb": sb(256, BF), "valx": sb(256, BF), "dd": sb(64, F32), "i480": sb(48, F32), "i48": sb(48, F32),
     "dfl": sb(16, F32),
-    "ta": sb(16, I32), "tb": sb(16, I32), "tc": sb(16, I32), "td": sb(32, I32),
+    "ta": sb(16, I32), "tb": sb(16, I32), "td": sb(32, I32),
     "z0": sb(96, F32), "zt0": sb(64, F32), "car0": sb(1, F32), "pt0": sb(32, F32), "zb0": sb(32, F32), "m0": sb(32, F32),
     "a0": sb(32, F32), "h0": sb(32, F32), "hm": sb(32, F32), "o0": sb(16, U16), "slt": sb(32, F32),
-    "zf": sb(96, F32), "ztf": sb(64, F32), "carf": sb(1, F32), "ptf": sb(32, F32), "zbf": sb(32, F32), "mf": sb(32, F32),
-    "af": sb(32, F32), "hf": sb(32, F32), "of": sb(16, U16),
     "z3": sb(96, F32), "zt3": sb(64, F32), "car3": sb(1, F32), "pt3": sb(32, F32), "zb3": sb(32, F32), "m3": sb(32, F32),
     "x3": sb(32, F32), "a3": sb(32, F32), "h3": sb(32, F32), "o3": sb(16, U16),
-    "win0": sb(512 + FAR, BF), "t0": sb(512, BF), "y0": sb(64, F32), "yt0": sb(64, F32), "yu0": sb(32, F32), "off0": sb(16, U16),
-    "winu": sb(1024 + FAR, BF), "tu": sb(960, BF), "yu": sb(64, F32), "ytu": sb(64, F32), "yuu": sb(32, F32), "offu": sb(32, U16),
+    "winu": sb(1024 + FAR, BF), "tu": sb(960, BF), "yu": sb(64, F32), "ytu": sb(64, F32), "yuu": sb(32, F32),
+    "off0": sb(16, U16), "offu": sb(14, U16),
     "winf": sb(1536 + FAR, BF), "tf": sb(1536, BF), "yf": sb(128, F32), "ytf": sb(128, F32), "yff": sb(64, F32), "sw": sb(48, F32),
     "slu": sb(32, BF), "slin": sb(32, BF),
-    "rexp": sb(64, F32), "ct": sb(64, F32), "rexp3": sb(32, F32), "ct3": sb(32, F32),
+    "rexp": sb(32, F32), "ct": sb(32, F32), "cuv": sb(8, F32), "rexp3": sb(32, F32), "ct3": sb(32, F32),
     "cf": sb(4, F32), "cg": sb(4, F32), "nf2": sb(1, F32),
     "lc": sb(16, F32), "offl": sb(16, U16),
     "sc": sb(16, F32), "lnt": sb(2, F32),
@@ -69,6 +68,7 @@ def rank_program(g, core, T, topo):
     s = T.sem
     cnt = {"sv": 0, "sa": 0, "st": 0, "loc": 0}
     seen = {}
+    L, U = slice(0, 64), slice(64, 128)
 
     def wait(name, eng, sem, n):
         if n > 0 and seen.get((name, sem), 0) < n:
@@ -151,7 +151,7 @@ def rank_program(g, core, T, topo):
     FL = {"allow_small_or_imprecise_dtypes": True}
     g.iota(T.pi[:, 0:1], [[1, 1]], 0, 1).then_inc(s.sg, 1)
     g.iota(T.val0[:], [[32, 16], [1, 16]], -256, 0, **FL).then_inc(s.sg, 1)
-    g.iota(T.dd[:], [[512, 3], [0, 2], [1, 16]], 512, 16, **FL).then_inc(s.sg, 1)
+    g.iota(T.dd[:], [[512, 2], [0, 2], [1, 16]], 1024, 16, **FL).then_inc(s.sg, 1)
     g.wait_ge(s.dml, 128)
     send(cp, T.dmt[:, ob:ob + 31], T.dmt[:, ob:ob + 31], "aDM")
     g.iota(T.i480[:], [[16, 48]], 0, 0, **FL).then_inc(s.sg, 1)
@@ -160,82 +160,83 @@ def rank_program(g, core, T, topo):
     g.vector.wait_ge(s.sg, 1)
     ts(T.pint[:, 0:1], T.pi[:, 0:1], 16, None, A.bitwise_and)
     n = ts(T.pint[:, 1:2], T.pi[:, 0:1], 15, None, A.bitwise_and)
-    nz = fill(T.zf[:], 0.0)
-    npf = cpy(T.pf[:, 0:2], T.pint[:, 0:2], n)
     fill(T.one[:], 1.0)
-    fill(T.z0[:, 31:32], C0 / 16.0)
-    fill(T.zf[:, 31:32], -2.0 / 32, nz)
-    fill(T.z3[:, 31:32], -2.0 / 32)
-    fill(T.half[:], 0.5)
-    fill(T.nhalf[:], -0.5)
-    fill(T.hb[0:64, :], PL)
-    nhb = fill(T.hb[64:128, :], PH)
-    fill(T.y0[:], 0.0)
-    fill(T.hm[:], 0.0)
+    fill(T.z0[L, 31:32], C0 / 16.0)
+    npf = cpy(T.pf[:, 0:2], T.pint[:, 0:2], n)
+    fill(T.z0[U, 31:32], -2.0 / 32)
+    fill(T.z0[U, 48:64], 0.0)
+    fill(T.sgn[L, :], -2.0)
+    nsgn = fill(T.sgn[U, :], 2.0)
+    fill(T.hpm[L, :], -0.5)
+    fill(T.hpm[U, :], 0.5)
+    fill(T.cb[L, :], float(C0))
+    fill(T.cb[U, :], 1.0)
 
-    nw0 = act(T.win0[:, 0:512], T.zero[:], nzero)
+    act(T.winu[:, 0:512], T.zero[:], nzero, bias=-4096.0)
+    act(T.winu[:, 512:960], T.zero[:, 0:448], bias=-4096.0)
     g.scalar.wait_ge(s.sg, 3)
     nvalb = act(T.valb[:], T.val0[:], npf, f=AF.Identity, bias=T.pf[:, 0:1])
 
     g.vector.wait_ge(s.dml, 128)
-    dv = T.dmt[:, ob:ob + 31:2]
-    na = ts(T.ta[:], dv, G, None, A.bitwise_and)
-    nb = ts(T.tb[:], dv, P | G, None, A.bitwise_and)
-    nc = ts(T.tc[:], dv, Fb, None, A.bitwise_and)
-    ts(T.z0[:, 32:48], T.ta[:], 0.0, -2.0, A.is_gt, A.mult, d=na)
-    n = ts(T.z0[:, 48:64], T.tb[:], float(P), -2.0, A.is_equal, A.mult, d=nb)
-    nc = ts(T.zf[:, 32:48], T.tc[:], 0.0, 2.0, A.is_gt, A.mult, d=nc)
+    ts(T.ta[L, :], T.dmt[L, ob:ob + 31:2], G, None, A.bitwise_and)
+    na = ts(T.ta[U, :], T.dmt[U, ob:ob + 31:2], Fb, None, A.bitwise_and)
+    nb = ts(T.tb[L, :], T.dmt[L, ob:ob + 31:2], P | G, None, A.bitwise_and)
+    ts(T.z0[:, 32:48], T.ta[:], 0.0, T.sgn[:], A.is_gt, A.mult, d=max(na, nsgn))
+    n = ts(T.z0[L, 48:64], T.tb[L, :], float(P), -2.0, A.is_equal, A.mult, d=nb)
+    fill(T.half[:], 0.5)
     n = scan(T.z0[:, 64:96], T.z0[:, 31:63], 0.0, n)
-    nc = scan(T.zf[:, 64:96], T.zf[:, 31:63], 0.0, nc)
+    fill(T.z3[:, 31:32], -2.0 / 32)
     n = tr(T.zt0[:], T.z0[:, 32:96], n)
     nzb = act(T.zb0[:], T.zt0[:, 0:32], n, f=AF.Square, scale=128.0)
-    nc = tr(T.ztf[:], T.zf[:, 32:96], nc)
-    nzbf = act(T.zbf[:], T.ztf[:, 0:32], nc, f=AF.Square, scale=128.0)
+    fill(T.hb[L, :], PL)
     n = red(T.car0[:], T.zt0[:, 32:64], n)
-    nc = red(T.carf[:], T.ztf[:, 32:64], nc)
+    nhb = fill(T.hb[U, :], PH)
     np0 = scan(T.pt0[:], T.zt0[:, 0:32], T.car0[:], n)
     g.vector.wait_ge(s.sg, 3)
     vsa(nzb)
-    n = tt(T.m0[:], T.dd[:, 0:32], T.zb0[:], A.subtract)
-    npf_ = scan(T.ptf[:], T.ztf[:, 0:32], T.carf[:], nc)
-    n = tt(T.a0[:], T.pt0[:], T.m0[:], A.max, n)
-    vsa(nzbf)
-    nc = tt(T.mf[:], T.dd[:, 32:64], T.zbf[:], A.subtract)
+    nm = tt(T.m0[:], T.dd[:, 0:32], T.zb0[:], A.subtract)
+    n = tt(T.a0[:], T.pt0[:], T.m0[:], A.max, max(nm, np0))
+    nhm = fill(T.hm[:], 0.0)
     n = tr(T.h0[:], T.a0[:], n)
-    nc = tt(T.af[:], T.ptf[:], T.mf[:], A.max, nc)
-    nhm = tt(T.hm[:, 0:16], T.h0[:, 0:16], T.h0[:, 16:32], A.min, n)
-    nc = tr(T.hf[:], T.af[:], nc)
+    nhm = tt(T.hm[:, 0:16], T.h0[:, 0:16], T.h0[:, 16:32], A.min, max(n, nhm))
     n = cpy(T.o0[:], T.hm[:, 0:16], nhm)
     nslt = tr(T.slt[:], T.hm[:])
-    vsa(max(nw0, nvalb))
-    n = cpy(T.win0[:].indirect(T.o0[:]), T.valb[:], n)
-    act(T.rexp[:, 0:32], T.nhalf[:], np0, scale=T.pt0[:, 31:32], bias=float(C0))
-    nrx = act(T.rexp[:, 32:64], T.half[:], npf_, scale=T.ptf[:, 31:32], bias=1.0)
-    nwf = act(T.winf[:, 0:512], T.zero[:], nhb, f=AF.Identity, bias=T.hb[:])
-    act(T.winu[:, 0:512], T.zero[:], bias=-4096.0)
+    vsa(nvalb)
+    n = cpy(T.winu[:].indirect(T.o0[:]), T.valb[:], n)
+    nrx = act(T.rexp[:], T.hpm[:], np0, f=AF.Identity, scale=T.pt0[:, 31:32], bias=T.cb[:])
+    nyu = act(T.yu[:], T.zero[:, 0:64])
     nslu = act(T.slu[:], T.slt[:], nslt, scale=0.5)
-    nwu = act(T.winu[:, 512:960], T.zero[:, 0:448], bias=-4096.0)
-    act(T.valx[0:64, :], T.valb[0:64, :], 0, nvalb)
-    nvx = act(T.valx[64:128, :], T.zero[64:128, 0:256])
+    nwf = act(T.winf[:, 0:512], T.zero[:], nhb, f=AF.Identity, bias=T.hb[:])
+    act(T.valx[L, :], T.valb[L, :], 0, nvalb)
+    nvx = act(T.valx[U, :], T.zero[U, 0:256])
     g.scalar.wait_ge(s.sg, 4)
     ni48 = act(T.i48[:], T.i480[:], f=AF.Identity, bias=T.pf[:, 1:2])
-    nyu = act(T.yu[:], T.zero[:, 0:64])
+    nyf = act(T.yf[:], T.zero[:, 0:128])
     ndfl = act(T.dfl[:], T.i48[:, 0:16], 0, ni48, bias=-float(T_))
     g.vector.wait_ge(s.xl0, 16)
     nxq0 = V(lambda: g.vector.quantize_mx(T.xq[:, 0:256], T.xs[:, 0:256], T.xt[:, 0:1024]))
-    n = tr(T.t0[:], T.win0[:, 0:512], n)
-    nof = cpy(T.of[:], T.hf[:, 0:16], nc)
-    tt(T.y0[:, 0:16], T.t0[:, 0:512:32], T.t0[:, 16:512:32], A.add, n)
-    n = tt(T.y0[:, 32:48], T.t0[:, 0:512:32], T.t0[:, 16:512:32], A.add)
+    n = tr(T.tu[:], T.winu[:, 0:960], n)
     vsa(nrx)
     nct = tr(T.ct[:], T.rexp[:])
-    n = tr(T.yt0[:], T.y0[:], n)
-    n = tr(T.yu0[:], T.yt0[:, 0:64:2], n)
+    vsa(nyu)
+    tt(T.yu[:, 0:30], T.tu[:, 0:960:32], T.tu[:, 16:960:32], A.max, n)
+    n = tt(T.yu[:, 32:62], T.tu[:, 0:960:32], T.tu[:, 16:960:32], A.max)
+    cpy(T.cuv[L, 0:4], T.ct[L, 15:19], nct)
+    cpy(T.cuv[U, 0:4], T.ct[L, 15:19])
+    n = tr(T.ytu[:], T.yu[:], n)
+    cpy(T.cuv[L, 4:8], T.ct[U, 15:19])
+    nct = cpy(T.cuv[U, 4:8], T.ct[U, 15:19])
+    ny = tr(T.yuu[:], T.ytu[:, 0:64:2], n)
     g.vector.wait_ge(s.xl1, 16)
     nxq = V(lambda: g.vector.quantize_mx(T.xq[:, 256:512], T.xs[:, 256:512], T.xt[:, 1024:2048]))
-    noff0 = ts(T.off0[:], T.yu0[:, 0:16], 256.0, None, A.add, d=n)
+    ts(T.off0[L, :], T.yuu[L, 0:16], 256.0, None, A.add, d=ny)
+    noff0 = ts(T.off0[U, :], T.yuu[L, 0:16], 256.0, None, A.add)
+    ts(T.offu[L, :], T.yuu[U, 0:14], 256.0, None, A.add)
+    noffu = ts(T.offu[U, :], T.yuu[U, 0:14], 256.0, None, A.add)
     nq0 = cpy(b32(T.p0q[:]), b32(T.xq[:]).indirect(T.off0[:]), noff0)
     na0 = SA(lambda: g.scalar.activation(T.p0s[:], T.xs[:].indirect(T.off0[:]), AF.Copy), noff0)
+    npe = cpy(b32(T.peq[:]), b32(T.xq[:]).indirect(T.offu[:]), noffu)
+    nae = SA(lambda: g.scalar.activation(T.pes[:], T.xs[:].indirect(T.offu[:]), AF.Copy), noffu)
 
     wait("s", g.sync, "sa", nwf)
     g.sync.dma_start(T.winf[:, 512:1024], T.winf[:, 0:512]).then_inc(s.wf, 16)
@@ -249,113 +250,112 @@ def rank_program(g, core, T, topo):
     send(cp, T.slin[:], T.slu[:], "aSL")
     wait("g", g, "sv", nct)
     trs = []
-    for dst, land, c, h in ((cf_, T.cf, 47, 0), (cg_, T.cg, 15, 1)):
+    for dst, land, c, h in ((cf_, T.cf, 4, 0), (cg_, T.cg, 0, 1)):
         en = topo.engines(core, dst)
         en = en[:len(en) // 2] if h == 0 else en[len(en) // 2:]
         rid, pid, _se = topo.addr(dst)
         trs.append(RemoteDMATransfer(dst_ids=[DstId(rid=rid, pnc=pid)], dma_engine_mask=sum(1 << e for e in en),
-                                     remote_sem=s.aCNT, src=T.ct[:, c:c + 4], dst=land[:]))
+                                     remote_sem=s.aCNT, src=T.cuv[:, c:c + 4], dst=land[:]))
         cnt["loc"] += len(en)
     g.remote_dma_fused(trs, local_sem=s.loc)
     wait("g", g, "sv", nq0)
     send(cp, b8(T.xwq[:, 0:C0]), b8(T.p0q[:]), "aS0")
     wait("g", g, "sa", na0)
     send(cp, T.xws[:, 0:C0], T.p0s[:], "aS0")
-
-    vsa(nwu)
-    nc = cpy(T.winu[:].indirect(T.of[:]), T.valb[:], nof)
-    g.vector.wait_ge(s.aDM, ncp)
-    n = ts(T.td[:], T.dmt[:, 4:67:2], Qb, None, A.bitwise_and)
-    nc = tr(T.tu[:], T.winu[:, 0:960], nc)
-    n = ts(T.z3[:, 32:64], T.td[:], 0.0, 2.0, A.is_gt, A.mult, d=n)
-    vsa(nyu)
-    tt(T.yu[:, 0:30], T.tu[:, 0:960:32], T.tu[:, 16:960:32], A.max, nc)
-    nc = tt(T.yu[:, 32:62], T.tu[:, 0:960:32], T.tu[:, 16:960:32], A.max)
-    n = scan(T.z3[:, 64:96], T.z3[:, 31:63], 0.0, n)
-    nc = tr(T.ytu[:], T.yu[:], nc)
-    n = tr(T.zt3[:], T.z3[:, 32:96], n)
-    nzb3 = act(T.zb3[:], T.zt3[:, 0:32], n, f=AF.Square, scale=128.0)
-    nc = tr(T.yuu[:], T.ytu[:, 0:64:2], nc)
-    n = red(T.car3[:], T.zt3[:, 32:64], n)
-    noffu = ts(T.offu[:], T.yuu[:], 256.0, None, A.add, d=nc)
-    vsa(ndfl)
-    nc = tt(T.lc[:], T.dfl[:], T.yuu[:, 14:30], A.max)
-    npe = cpy(b32(T.peq[:]), b32(T.xq[:]).indirect(T.offu[:, 0:14]), noffu)
-    noffl = ts(T.offl[:], T.lc[:], float(T_), None, A.add, d=nc)
-    np3 = scan(T.pt3[:], T.zt3[:, 0:32], T.car3[:], n)
-    vsa(nzb3)
-    nm3 = tt(T.m3[:], T.dd[:, 64:96], T.zb3[:], A.subtract)
-
-    nae = SA(lambda: g.scalar.activation(T.pes[:], T.xs[:].indirect(T.offu[:, 0:14]), AF.Copy), noffu)
-    nrx3 = act(T.rexp3[:], T.half[:], np3, scale=T.pt3[:, 31:32], bias=1.0)
-    u, v = T.cf[:, 0:1], T.cg[:, 0:1]
-    local_first = q < rf
-    g.vector.wait_ge(s.xw, 64)
-    g.vector.wait_ge(s.aS0, 2 * ncp)
-    npl = cpy(b32(T.plq[:]), b32(T.xwq[:]).indirect(T.offl[:]), noffl)
-    wait("a", g.scalar, "sv", noffl)
-    g.scalar.wait_ge(s.xw, 64)
-    g.scalar.wait_ge(s.aS0, 2 * ncp)
-    nal = SA(lambda: g.scalar.activation(T.pls[:], T.xws[:].indirect(T.offl[:]), AF.Copy))
-    nyf = act(T.yf[:], T.zero[:, 0:128])
-    act(T.res0[:, ZC:RW], T.zero[:, 0:32])
-    nres = act(T.res1[:, ZC:RW], T.zero[:, 0:32])
-    wait("s", g.sync, "sa", nvx)
-    g.sync.wait_ge(s.aSL, ncp)
-    for k in range(4, 8):
-        a, h = k // 2, k % 2
-        g.sync.dma_start(T.valx[16 * k:16 * k + 1, :], T.slin[32 * a:32 * a + 16, 16 * h:16 * h + 16]).then_inc(s.vps, 16)
-
     wait("g", g, "sv", npe)
     send(cf_, b8(T.leq[:]), b8(T.peq[:]), "aE")
     wait("g", g, "sa", nae)
     send(cf_, T.les[:], T.pes[:], "aE")
-    wait("g", g, "sv", npl)
-    send(cf_, b8(T.llq[:]), b8(T.plq[:]), "aL")
-    wait("g", g, "sa", nal)
-    send(cf_, T.lls[:], T.pls[:], "aL")
 
+    vsa(ndfl)
+    nc = tt(T.lc[U, :], T.dfl[U, :], T.yuu[U, 14:30], A.max)
+    g.vector.wait_ge(s.aDM, ncp)
+    n = ts(T.td[:], T.dmt[:, 4:67:2], Qb, None, A.bitwise_and)
+    ts(T.offl[L, :], T.lc[U, :], float(T_), None, A.add, d=nc)
+    n = ts(T.z3[:, 32:64], T.td[:], 0.0, 2.0, A.is_gt, A.mult, d=n)
+    noffl = ts(T.offl[U, :], T.lc[U, :], float(T_), None, A.add)
+    n = scan(T.z3[:, 64:96], T.z3[:, 31:63], 0.0, n)
+    n = tr(T.zt3[:], T.z3[:, 32:96], n)
+    nzb3 = act(T.zb3[:], T.zt3[:, 0:32], n, f=AF.Square, scale=128.0)
+    n = red(T.car3[:], T.zt3[:, 32:64], n)
+    g.vector.wait_ge(s.wl, 16)
+    nwq = V(lambda: g.vector.quantize_mx(T.wq[:], T.ws[:], T.wt[:]))
+    np3 = scan(T.pt3[:], T.zt3[:, 0:32], T.car3[:], n)
+    nrx3 = act(T.rexp3[:], T.half[:], np3, scale=T.pt3[:, 31:32], bias=1.0)
+    vsa(nzb3)
+    nm3 = tt(T.m3[:], T.dd[:, 32:64], T.zb3[:], A.subtract)
+
+    local_first = q < rf
+    u, v = T.cf[:, 0:1], T.cg[:, 0:1]
     fline = rf < rg
     first = u if fline else v
     nl, fst = T.ct3[:, 31:32], T.ct3[:, 15:16]
     na_, nq = T.lnt[:, 0:1], T.lnt[:, 1:2]
     nf, c1, ba, cz = T.sc[:, 0:1], T.sc[:, 2:3], T.sc[:, 3:4], T.sc[:, 4:5]
-    pt, np_ = T.pt3, np3
-    g.vector.wait_ge(s.wl, 16)
-    if not local_first:
-        g.vector.wait_ge(s.aCNT, nmf)
-        n = ts(T.nf2[:], u, v, 2.0, A.add, A.mult)
-    nwq = V(lambda: g.vector.quantize_mx(T.wq[:], T.ws[:], T.wt[:]))
-    if not local_first:
-        np_ = ts(T.x3[:], T.pt3[:], T.nf2[:], None, A.add, d=max(n, np3))
-        pt = T.x3
-    vsa(nrx3)
-    nc3 = tr(T.ct3[:], T.rexp3[:])
-    n3 = tt(T.a3[:], pt[:], T.m3[:], A.max, max(np_, nm3))
-    g.vector.wait_ge(s.aCNT, nmf)
-    nnf = tt(nf, u, v, A.add)
+    lo, hi = (slice(0, 16), slice(16, 32)) if even else (slice(16, 32), slice(0, 16))
+
+    def pick_late():
+        g.vector.wait_ge(s.xw, 64)
+        g.vector.wait_ge(s.aS0, 2 * ncp)
+        return cpy(b32(T.plq[:]), b32(T.xwq[:]).indirect(T.offl[:]), noffl)
     if local_first:
+        n3 = tt(T.a3[:], T.pt3[:], T.m3[:], A.max, max(np3, nm3))
+        vsa(nrx3)
+        nc3 = tr(T.ct3[:], T.rexp3[:])
+        n3 = tr(T.h3[:], T.a3[:], n3)
+        npl = pick_late()
+        cpy(T.o3[L, :], T.h3[L, lo], n3)
+        no3 = cpy(T.o3[U, :], T.h3[U, hi])
+        g.vector.wait_ge(s.aCNT, nmf)
+        nnf = tt(nf, u, v, A.add)
         cs = T.sc[:, 1:2]
         ncs = tt(cs, nl, first, A.add, nc3)
-    else:
-        cs, ncs = first, 0
-    n3 = tr(T.h3[:], T.a3[:], n3)
-    nna = tt(na_, nl, nf, A.add, max(nnf, nc3))
-    if local_first:
         ts(c1, nl, -1.0 if fline else 1.0, 0.0 if fline else C1 - 1.0, A.mult, A.add)
+        nna = tt(na_, nl, nf, A.add, nnf)
         n1 = ts(ba, cs, nl, C1 - 1.0, A.add, A.add, d=ncs)
     else:
+        cs, ncs = first, 0
         c1 = 0.0 if fline else C1 - 1.0
+        g.vector.wait_ge(s.aCNT, nmf)
+        n = ts(T.nf2[:], u, v, 2.0, A.add, A.mult)
+        nnf = tt(nf, u, v, A.add)
+        vsa(nrx3)
+        nc3 = tr(T.ct3[:], T.rexp3[:])
+        np3 = ts(T.x3[:], T.pt3[:], T.nf2[:], None, A.add, d=max(n, np3))
         n1 = ts(ba, cs, C1 - 1.0, None, A.add)
-    lo, hi = (slice(0, 16), slice(16, 32)) if even else (slice(16, 32), slice(0, 16))
-    cpy(T.o3[0:64, :], T.h3[0:64, lo], n3)
-    no3 = cpy(T.o3[64:128, :], T.h3[64:128, hi])
+        nna = tt(na_, nl, nf, A.add, max(nnf, nc3))
+        n3 = tt(T.a3[:], T.x3[:], T.m3[:], A.max, max(np3, nm3))
+        npl = pick_late()
+        n3 = tr(T.h3[:], T.a3[:], n3)
+        nw = cpy(nq, fst) if even else tt(nq, nl, fst, A.subtract)
     ncz = ts(cz, na_, -4096.0, 4096.0, A.mult, A.add, d=nna)
+    if local_first:
+        nw = cpy(nq, fst) if even else tt(nq, nl, fst, A.subtract)
+    else:
+        cpy(T.o3[L, :], T.h3[L, lo], n3)
+        no3 = cpy(T.o3[U, :], T.h3[U, hi])
+    nln = max(nna, nw)
+    wait("a", g.scalar, "sv", noffl)
+    g.scalar.wait_ge(s.xw, 64)
+    g.scalar.wait_ge(s.aS0, 2 * ncp)
+    nal = SA(lambda: g.scalar.activation(T.pls[:], T.xws[:].indirect(T.offl[:]), AF.Copy))
+    act(T.res0[:, ZC:RW], T.zero[:, 0:32])
+    nres = act(T.res1[:, ZC:RW], T.zero[:, 0:32])
+    wait("s", g.sync, "sa", nvx)
+    g.sync.wait_ge(s.aSL, ncp)
+    for k in range(4, 8):
+        h = k % 2
+        g.sync.dma_start(T.valx[16 * k:16 * k + 1, :], T.slin[0:16, 16 * h:16 * h + 16]).then_inc(s.vps, 16)
+
+    wait("g", g, "sv", npl)
+    send(cf_, b8(T.llq[:]), b8(T.plq[:]), "aL")
+    wait("g", g, "sa", nal)
+    send(cf_, T.lls[:], T.pls[:], "aL")
+
     ii = T.i48[:]
     act(T.fl1[:], ii, n1, f=AF.Identity, scale=1.0 if fline else -1.0, bias=c1)
     act(T.fd[:], ii, f=AF.Identity, scale=-2.0, bias=ba)
     nfz = act(T.fz[:], ii, ncz, f=AF.Relu, scale=4096.0, bias=cz)
-    nln = max(nna, cpy(nq, fst) if even else tt(nq, nl, fst, A.subtract))
     vsa(nvx)
     g.vector.wait_ge(s.vps, 64)
     g.vector.wait_ge(s.wf, 32)
@@ -372,8 +372,8 @@ def rank_program(g, core, T, topo):
     nw = tr(T.ytf[:], T.yf[:], nw)
     nst = tt(T.fm[:], T.ff[:], T.fz[:], A.max, nst)
     nw = tr(T.yff[:], T.ytf[:, 0:128:2], nw)
-    ts(T.sw[0:64, :], T.yff[64:128, 0:48], -LOC - FB, None, A.add, d=nw)
-    n = ts(T.sw[64:128, :], T.yff[0:64, 0:48], -LOC - FB, None, A.add)
+    ts(T.sw[L, :], T.yff[U, 0:48], -LOC - FB, None, A.add, d=nw)
+    n = ts(T.sw[U, :], T.yff[L, 0:48], -LOC - FB, None, A.add)
     n = tt(T.fl[:], T.yff[:, 0:48], T.sw[:], A.add, n)
     n = tt(T.fl2[:], T.fl[:], T.fm[:], A.min, max(n, nst))
     noff = ts(T.offf[:], T.fl2[:], float(FB), float(ZC), A.add, A.min, d=n)
@@ -404,7 +404,7 @@ def rank_program(g, core, T, topo):
     for k in range(len(CUTS) - 1):
         a, b = CUTS[k], CUTS[k + 1]
         of = T.offf[:, a // 16:b // 16]
-        n0 = cpy(T.yt_0[:, a:b], T.res0[:].indirect(of), n)
+        n0 = cpy(T.yt_0[:, a:b], T.res0[:].indirect(of), max(n, noff))
         n1 = SA(lambda: g.scalar.activation(T.yt_1[:, a:b], T.res1[:].indirect(of), AF.Copy), noff, nlast)
         if k == 0:
             wait("s", g.sync, "sv", nln)

@@ -4,13 +4,15 @@ from concourse.mybir import dt, AluOpType, AxisListType, ActivationFunctionType
 
 T_, S_, C0, C1 = 512, 768, 256, 480
 EARLY = C1 - C0
+OWN = T_ - EARLY
 FB = T_ + C0
 RW = FB + C1 + 32
 ZC = FB + C1
-CUTS = (0, 256, 768)
+CUTS = (0, 128, 384, 768)
 FAR = 16 * 127 + 16
-PL, PH = 1280.0, 1024.0
-LOC = PL + 2 * PH - 256.0
+LS = 256.0 + C0 - EARLY
+NONE = 4096.0
+BIG = 8192.0
 
 F32, I32, U16, BF = "float32", "int32", "uint16", "bfloat16"
 Q4, U8 = "float8_e4m3fn_x4", "uint8"
@@ -24,34 +26,35 @@ SCRATCH = {
     "dmt": sb(68, I32),
     "xt": sb(2048, BF), "wt": sb(1024, BF),
     "xq": sb(512, Q4), "xs": sb(512, U8), "wq": sb(256, Q4), "ws": sb(256, U8),
-    "xwq": sb(768, Q4), "xws": sb(768, U8),
+    "xwq": sb(C0 + OWN, Q4), "xws": sb(C0 + OWN, U8),
     "p0q": sb(256, Q4), "p0s": sb(256, U8),
     "peq": sb(EARLY, Q4), "pes": sb(EARLY, U8), "plq": sb(256, Q4), "pls": sb(256, U8),
     "leq": sb(EARLY, Q4), "les": sb(EARLY, U8), "llq": sb(256, Q4), "lls": sb(256, U8),
-    "zero": sb(512, BF), "one": sb(32, F32), "half": sb(32, F32), "hpm": sb(32, F32), "hb": sb(1, F32), "cb": sb(1, F32),
-    "sgn": sb(1, F32),
+    "one": sb(32, F32), "half": sb(32, F32), "hpm": sb(32, F32), "cb": sb(1, F32), "sgn": sb(1, F32),
+    "ho": sb(1, F32), "hf": sb(1, F32),
     "pi": sb(2, I32), "pint": sb(8, I32), "pf": sb(8, F32),
-    "val0": sb(256, F32), "valb": sb(256, BF), "valx": sb(256, BF), "dd": sb(64, F32), "i480": sb(48, F32), "i48": sb(48, F32),
+    "val0": sb(256, BF), "valb": sb(256, BF), "dd0": sb(32, F32), "dd": sb(32, F32), "i480": sb(64, F32), "i48": sb(64, F32),
     "dfl": sb(16, F32),
     "ta": sb(16, I32), "tb": sb(16, I32), "td": sb(32, I32),
     "z0": sb(96, F32), "zt0": sb(64, F32), "car0": sb(1, F32), "pt0": sb(32, F32), "zb0": sb(32, F32), "m0": sb(32, F32),
     "a0": sb(32, F32), "h0": sb(32, F32), "hm": sb(32, F32), "o0": sb(16, U16), "slt": sb(32, F32),
     "z3": sb(96, F32), "zt3": sb(64, F32), "car3": sb(1, F32), "pt3": sb(32, F32), "zb3": sb(32, F32), "m3": sb(32, F32),
-    "x3": sb(32, F32), "a3": sb(32, F32), "h3": sb(32, F32), "o3": sb(16, U16),
-    "winu": sb(1024 + FAR, BF), "tu": sb(960, BF), "yu": sb(64, F32), "ytu": sb(64, F32), "yuu": sb(32, F32),
+    "x3": sb(32, F32), "w3": sb(32, F32), "y3": sb(32, F32), "a3": sb(32, F32), "h3": sb(32, F32), "o3": sb(16, U16),
+    "winu": sb(1024 + FAR, BF), "tu": sb(960, BF), "yu": sb(128, F32), "ytu": sb(128, F32), "yuu": sb(64, F32),
     "off0": sb(16, U16), "offu": sb(14, U16),
-    "winf": sb(1536 + FAR, BF), "tf": sb(1536, BF), "yf": sb(128, F32), "ytf": sb(128, F32), "yff": sb(64, F32), "sw": sb(48, F32),
+    "winf": sb(1024 + FAR, BF), "tf": sb(S_, BF), "yf": sb(64, F32), "ytf": sb(64, F32), "yff": sb(64, F32), "sw": sb(64, F32),
     "slu": sb(32, BF), "slin": sb(32, BF),
     "rexp": sb(32, F32), "ct": sb(32, F32), "cuv": sb(8, F32), "rexp3": sb(32, F32), "ct3": sb(32, F32),
-    "cf": sb(4, F32), "cg": sb(4, F32), "nf2": sb(1, F32),
+    "cf": sb(4, F32), "cg": sb(4, F32),
     "lc": sb(16, F32), "offl": sb(16, U16),
     "sc": sb(16, F32), "lnt": sb(2, F32),
-    "fst": sb(48, F32), "fd": sb(48, F32), "fl1": sb(48, F32), "fz": sb(48, F32), "fsd": sb(48, F32), "ff": sb(48, F32),
-    "fm": sb(48, F32), "fl": sb(48, F32), "fl2": sb(48, F32), "offf": sb(48, U16),
+    "tl": sb(64, F32), "la": sb(64, F32), "wa": sb(64, F32), "lb": sb(64, F32), "wb": sb(64, F32),
+    "ma": sb(64, F32), "mb": sb(64, F32), "fm": sb(64, F32), "fh": sb(64, F32), "fl": sb(64, F32), "fl2": sb(64, F32),
+    "offf": sb(64, U16),
     "res0": sb(RW, F32), "res1": sb(RW, F32), "yt_0": sb(768, F32), "yt_1": sb(768, F32),
     "ps": ("psum", [128, 4096], F32),
 }
-SEMAPHORES = ["sv", "sa", "st", "sg", "dml", "xl0", "xl1", "wl", "xw", "wf", "vps", "yst",
+SEMAPHORES = ["sv", "sa", "st", "sg", "dml", "xl0", "xl1", "wl", "xw", "vps", "yst",
               "aDM", "aS0", "aSL", "aCNT", "aE", "aL", "loc"]
 
 
@@ -144,19 +147,20 @@ def rank_program(g, core, T, topo):
         e = g.sync if k % 2 == 0 else g.scalar
         o = ob - k % 2
         e.dma_start(T.dmt[16 * k:16 * k + 16, o:o + 32], T.dm[:, :]).then_inc(s.dml, 16)
-    g.sync.dma_start(T.xt[:, 0:1024], T.x[:, 0:1024]).then_inc(s.xl0, 16)
-    g.scalar.dma_start(T.xt[:, 1024:2048], T.x[:, 1024:2048]).then_inc(s.xl1, 16)
+    g.sync.dma_start(T.xt[:, 4 * EARLY:2048], T.x[:, 4 * EARLY:2048]).then_inc(s.xl0, 16)
+    g.scalar.dma_start(T.xt[:, 0:4 * EARLY], T.x[:, 0:4 * EARLY]).then_inc(s.xl1, 16)
     g.scalar.dma_start(T.wt[:], T.w[:]).then_inc(s.wl, 16)
 
     FL = {"allow_small_or_imprecise_dtypes": True}
     g.iota(T.pi[:, 0:1], [[1, 1]], 0, 1).then_inc(s.sg, 1)
     g.iota(T.val0[:], [[32, 16], [1, 16]], -256, 0, **FL).then_inc(s.sg, 1)
-    g.iota(T.dd[:], [[512, 2], [0, 2], [1, 16]], 1024, 16, **FL).then_inc(s.sg, 1)
+    g.iota(T.dd0[:], [[0, 2], [16, 16]], 1024, 0, **FL).then_inc(s.sg, 1)
+    g.iota(T.i480[:], [[S_ // 2, 2], [16, 32]], 0, 0, **FL).then_inc(s.sg, 1)
     g.wait_ge(s.dml, 128)
     send(cp, T.dmt[:, ob:ob + 31], T.dmt[:, ob:ob + 31], "aDM")
-    g.iota(T.i480[:], [[16, 48]], 0, 0, **FL).then_inc(s.sg, 1)
+    g.iota(T.yu[:], [[0, 128]], 0, 0, **FL).then_inc(s.sg, 1)
 
-    nzero = fill(T.zero[:], 0.0)
+    nwu = fill(T.winu[:, 0:512], -NONE)
     g.vector.wait_ge(s.sg, 1)
     ts(T.pint[:, 0:1], T.pi[:, 0:1], 16, None, A.bitwise_and)
     n = ts(T.pint[:, 1:2], T.pi[:, 0:1], 15, None, A.bitwise_and)
@@ -167,88 +171,92 @@ def rank_program(g, core, T, topo):
     fill(T.z0[U, 48:64], 0.0)
     fill(T.sgn[L, :], -2.0)
     nsgn = fill(T.sgn[U, :], 2.0)
-    fill(T.hpm[L, :], -0.5)
-    fill(T.hpm[U, :], 0.5)
-    fill(T.cb[L, :], float(C0))
-    fill(T.cb[U, :], 1.0)
+    g.vector.wait_ge(s.sg, 2)
+    ts(T.valb[:], T.val0[:], T.pf[:, 0:1], None, A.add, d=npf)
 
-    act(T.winu[:, 0:512], T.zero[:], nzero, bias=-4096.0)
-    act(T.winu[:, 512:960], T.zero[:, 0:448], bias=-4096.0)
-    g.scalar.wait_ge(s.sg, 3)
-    nvalb = act(T.valb[:], T.val0[:], npf, f=AF.Identity, bias=T.pf[:, 0:1])
+    act(T.winu[:, 512:960], T.winu[:, 0:448], nwu)
+    nwf0 = act(T.winf[:, 0:512], T.winu[:, 0:512], scale=-1.0)
 
     g.vector.wait_ge(s.dml, 128)
     ts(T.ta[L, :], T.dmt[L, ob:ob + 31:2], G, None, A.bitwise_and)
     na = ts(T.ta[U, :], T.dmt[U, ob:ob + 31:2], Fb, None, A.bitwise_and)
     nb = ts(T.tb[L, :], T.dmt[L, ob:ob + 31:2], P | G, None, A.bitwise_and)
+    fill(T.hpm[L, :], -0.5)
     ts(T.z0[:, 32:48], T.ta[:], 0.0, T.sgn[:], A.is_gt, A.mult, d=max(na, nsgn))
-    n = ts(T.z0[L, 48:64], T.tb[L, :], float(P), -2.0, A.is_equal, A.mult, d=nb)
-    fill(T.half[:], 0.5)
-    n = scan(T.z0[:, 64:96], T.z0[:, 31:63], 0.0, n)
-    fill(T.z3[:, 31:32], -2.0 / 32)
-    n = tr(T.zt0[:], T.z0[:, 32:96], n)
-    nzb = act(T.zb0[:], T.zt0[:, 0:32], n, f=AF.Square, scale=128.0)
-    fill(T.hb[L, :], PL)
-    n = red(T.car0[:], T.zt0[:, 32:64], n)
-    nhb = fill(T.hb[U, :], PH)
-    np0 = scan(T.pt0[:], T.zt0[:, 0:32], T.car0[:], n)
+    nz = ts(T.z0[L, 48:64], T.tb[L, :], float(P), -2.0, A.is_equal, A.mult, d=nb)
+    fill(T.hpm[U, :], 0.5)
+    fill(T.cb[L, :], float(C0))
+    n = scan(T.z0[:, 64:96], T.z0[:, 31:63], 0.0, nz)
+    nzb = ts(T.zb0[:], T.z0[:, 32:64], 0.0, 65536.0, A.not_equal, A.mult)
     g.vector.wait_ge(s.sg, 3)
-    vsa(nzb)
-    nm = tt(T.m0[:], T.dd[:, 0:32], T.zb0[:], A.subtract)
-    n = tt(T.a0[:], T.pt0[:], T.m0[:], A.max, max(nm, np0))
-    nhm = fill(T.hm[:], 0.0)
-    n = tr(T.h0[:], T.a0[:], n)
-    nhm = tt(T.hm[:, 0:16], T.h0[:, 0:16], T.h0[:, 16:32], A.min, max(n, nhm))
-    n = cpy(T.o0[:], T.hm[:, 0:16], nhm)
+    ndd = ts(T.dd[:], T.dd0[:], T.pf[:, 1:2], None, A.add)
+    n = tr(T.zt0[:], T.z0[:, 32:96], n)
+    fill(T.cb[U, :], 1.0)
+    fill(T.hm[:], 0.0)
+    n = red(T.car0[:], T.zt0[:, 32:64], n)
+    nm = tt(T.m0[:], T.dd[:], T.zb0[:], A.subtract, max(nzb, ndd))
+    fill(T.half[:], 0.5)
+    np0 = scan(T.pt0[:], T.zt0[:, 0:32], T.car0[:], n)
+    fill(T.z3[:, 31:32], -2.0 / 32)
+    fill(T.ho[L, :], 256.0)
+    n = tr(T.h0[:], T.pt0[:], np0)
+    nrx = ts(T.rexp[:], T.hpm[:], T.pt0[:, 31:32], T.cb[:], A.mult, A.add)
+    fill(T.ho[U, :], 512.0)
+    n = tt(T.a0[:], T.h0[:], T.m0[:], A.max, max(n, nm))
+    nct = tr(T.ct[:], T.rexp[:], nrx)
+    fill(T.hf[L, :], FB - 256.0)
+    n = tt(T.hm[:, 0:16], T.a0[:, 0:16], T.a0[:, 16:32], A.min, n)
+    fill(T.hf[U, :], FB - 512.0)
+    g.vector.wait_ge(s.sg, 4)
+    ni48 = ts(T.i48[:], T.i480[:], T.pf[:, 1:2], None, A.add)
+    n = cpy(T.o0[:], T.hm[:, 0:16], n)
     nslt = tr(T.slt[:], T.hm[:])
-    vsa(nvalb)
-    n = cpy(T.winu[:].indirect(T.o0[:]), T.valb[:], n)
-    nrx = act(T.rexp[:], T.hpm[:], np0, f=AF.Identity, scale=T.pt0[:, 31:32], bias=T.cb[:])
-    nyu = act(T.yu[:], T.zero[:, 0:64])
+    vsa(nwf0)
+    nwin = cpy(T.winu[:].indirect(T.o0[:]), T.valb[:], n)
+    act(T.cuv[L, 0:4], T.ct[L, 15:19], nct)
     nslu = act(T.slu[:], T.slt[:], nslt, scale=0.5)
-    nwf = act(T.winf[:, 0:512], T.zero[:], nhb, f=AF.Identity, bias=T.hb[:])
-    act(T.valx[L, :], T.valb[L, :], 0, nvalb)
-    nvx = act(T.valx[U, :], T.zero[U, 0:256])
-    g.scalar.wait_ge(s.sg, 4)
-    ni48 = act(T.i48[:], T.i480[:], f=AF.Identity, bias=T.pf[:, 1:2])
-    nyf = act(T.yf[:], T.zero[:, 0:128])
-    ndfl = act(T.dfl[:], T.i48[:, 0:16], 0, ni48, bias=-float(T_))
+    act(T.cuv[U, 0:4], T.ct[L, 15:19])
+    act(T.cuv[L, 4:8], T.ct[U, 15:19])
+    ncuv = act(T.cuv[U, 4:8], T.ct[U, 15:19])
+    nwf = act(T.winf[:, 512:S_], T.winf[:, 0:S_ - 512], 0, nwf0)
     g.vector.wait_ge(s.xl0, 16)
-    nxq0 = V(lambda: g.vector.quantize_mx(T.xq[:, 0:256], T.xs[:, 0:256], T.xt[:, 0:1024]))
-    n = tr(T.tu[:], T.winu[:, 0:960], n)
-    vsa(nrx)
-    nct = tr(T.ct[:], T.rexp[:])
-    vsa(nyu)
-    tt(T.yu[:, 0:30], T.tu[:, 0:960:32], T.tu[:, 16:960:32], A.max, n)
-    n = tt(T.yu[:, 32:62], T.tu[:, 0:960:32], T.tu[:, 16:960:32], A.max)
-    cpy(T.cuv[L, 0:4], T.ct[L, 15:19], nct)
-    cpy(T.cuv[U, 0:4], T.ct[L, 15:19])
-    n = tr(T.ytu[:], T.yu[:], n)
-    cpy(T.cuv[L, 4:8], T.ct[U, 15:19])
-    nct = cpy(T.cuv[U, 4:8], T.ct[U, 15:19])
-    ny = tr(T.yuu[:], T.ytu[:, 0:64:2], n)
+    nxq0 = V(lambda: g.vector.quantize_mx(T.xq[:, EARLY:T_], T.xs[:, EARLY:T_], T.xt[:, 4 * EARLY:2048]))
+    n = tr(T.tu[:, 0:512], T.winu[:, 0:512], nwin)
+    ndfl = ts(T.dfl[:], T.i48[:, 0:16], -LS, None, A.add, d=ni48)
+    g.vector.wait_ge(s.aDM, ncp)
+    n3 = ts(T.td[:], T.dmt[:, 4:67:2], Qb, None, A.bitwise_and)
+    g.vector.wait_ge(s.sg, 5)
+    tt(T.yu[:, 0:16], T.tu[:, 0:512:32], T.tu[:, 16:512:32], A.max, n)
+    n = tt(T.yu[:, 32:48], T.tu[:, 0:512:32], T.tu[:, 16:512:32], A.max)
+    n3 = ts(T.z3[:, 32:64], T.td[:], 0.0, 2.0, A.is_gt, A.mult, d=n3)
+    n = tr(T.ytu[:, 0:64], T.yu[:, 0:64], n)
+    n3 = scan(T.z3[:, 64:96], T.z3[:, 31:63], 0.0, n3)
+    ny = tr(T.yuu[:, 0:32], T.ytu[:, 0:64:2], n)
     g.vector.wait_ge(s.xl1, 16)
-    nxq = V(lambda: g.vector.quantize_mx(T.xq[:, 256:512], T.xs[:, 256:512], T.xt[:, 1024:2048]))
+    V(lambda: g.vector.quantize_mx(T.xq[:, 0:EARLY], T.xs[:, 0:EARLY], T.xt[:, 0:4 * EARLY]))
     ts(T.off0[L, :], T.yuu[L, 0:16], 256.0, None, A.add, d=ny)
     noff0 = ts(T.off0[U, :], T.yuu[L, 0:16], 256.0, None, A.add)
     ts(T.offu[L, :], T.yuu[U, 0:14], 256.0, None, A.add)
-    noffu = ts(T.offu[U, :], T.yuu[U, 0:14], 256.0, None, A.add)
+    n3 = tr(T.zt3[:], T.z3[:, 32:96], n3)
     nq0 = cpy(b32(T.p0q[:]), b32(T.xq[:]).indirect(T.off0[:]), noff0)
     na0 = SA(lambda: g.scalar.activation(T.p0s[:], T.xs[:].indirect(T.off0[:]), AF.Copy), noff0)
+    noffu = ts(T.offu[U, :], T.yuu[U, 0:14], 256.0, None, A.add)
+    n3 = red(T.car3[:], T.zt3[:, 32:64], n3)
+    nzb = ts(T.zb3[:], T.z3[:, 32:64], 0.0, 65536.0, A.not_equal, A.mult)
     npe = cpy(b32(T.peq[:]), b32(T.xq[:]).indirect(T.offu[:]), noffu)
     nae = SA(lambda: g.scalar.activation(T.pes[:], T.xs[:].indirect(T.offu[:]), AF.Copy), noffu)
 
-    wait("s", g.sync, "sa", nwf)
-    g.sync.dma_start(T.winf[:, 512:1024], T.winf[:, 0:512]).then_inc(s.wf, 16)
-    g.sync.dma_start(T.winf[:, 1024:1536], T.winf[:, 0:512]).then_inc(s.wf, 16)
-    for n, a in ((nxq0, 0), (nxq, 256)):
-        wait("s", g.sync, "sv", n)
-        g.sync.dma_start(b8(T.xwq[:, C0 + a:C0 + a + 256]), b8(T.xq[:, a:a + 256])).then_inc(s.xw, 16)
-        g.sync.dma_start(T.xws[:, C0 + a:C0 + a + 256], T.xs[:, a:a + 256]).then_inc(s.xw, 16)
+    wait("s", g.sync, "sv", nxq0)
+    g.sync.dma_start(b8(T.xwq[:, C0:C0 + OWN]), b8(T.xq[:, EARLY:T_])).then_inc(s.xw, 16)
+    g.sync.dma_start(T.xws[:, C0:C0 + OWN], T.xs[:, EARLY:T_]).then_inc(s.xw, 16)
+    g.sync.wait_ge(s.aSL, ncp)
+    for k in range(4, 8):
+        h = k % 2
+        g.sync.dma_start(T.valb[16 * k:16 * k + 1, :], T.slin[0:16, 16 * h:16 * h + 16]).then_inc(s.vps, 16)
 
     wait("g", g, "sa", nslu)
     send(cp, T.slin[:], T.slu[:], "aSL")
-    wait("g", g, "sv", nct)
+    wait("g", g, "sa", ncuv)
     trs = []
     for dst, land, c, h in ((cf_, T.cf, 4, 0), (cg_, T.cg, 0, 1)):
         en = topo.engines(core, dst)
@@ -258,6 +266,8 @@ def rank_program(g, core, T, topo):
                                      remote_sem=s.aCNT, src=T.cuv[:, c:c + 4], dst=land[:]))
         cnt["loc"] += len(en)
     g.remote_dma_fused(trs, local_sem=s.loc)
+    for b, a, n in ((T.yf, 0, 64), (T.res0, ZC, 32), (T.res1, ZC, 32)):
+        g.iota(b[:, a:a + n], [[0, n]], 0, 0, **FL).then_inc(s.sg, 1)
     wait("g", g, "sv", nq0)
     send(cp, b8(T.xwq[:, 0:C0]), b8(T.p0q[:]), "aS0")
     wait("g", g, "sa", na0)
@@ -267,116 +277,89 @@ def rank_program(g, core, T, topo):
     wait("g", g, "sa", nae)
     send(cf_, T.les[:], T.pes[:], "aE")
 
-    vsa(ndfl)
-    nc = tt(T.lc[U, :], T.dfl[U, :], T.yuu[U, 14:30], A.max)
-    g.vector.wait_ge(s.aDM, ncp)
-    n = ts(T.td[:], T.dmt[:, 4:67:2], Qb, None, A.bitwise_and)
-    ts(T.offl[L, :], T.lc[U, :], float(T_), None, A.add, d=nc)
-    n = ts(T.z3[:, 32:64], T.td[:], 0.0, 2.0, A.is_gt, A.mult, d=n)
-    noffl = ts(T.offl[U, :], T.lc[U, :], float(T_), None, A.add)
-    n = scan(T.z3[:, 64:96], T.z3[:, 31:63], 0.0, n)
-    n = tr(T.zt3[:], T.z3[:, 32:96], n)
-    nzb3 = act(T.zb3[:], T.zt3[:, 0:32], n, f=AF.Square, scale=128.0)
-    n = red(T.car3[:], T.zt3[:, 32:64], n)
-    g.vector.wait_ge(s.wl, 16)
-    nwq = V(lambda: g.vector.quantize_mx(T.wq[:], T.ws[:], T.wt[:]))
-    np3 = scan(T.pt3[:], T.zt3[:, 0:32], T.car3[:], n)
-    nrx3 = act(T.rexp3[:], T.half[:], np3, scale=T.pt3[:, 31:32], bias=1.0)
-    vsa(nzb3)
-    nm3 = tt(T.m3[:], T.dd[:, 32:64], T.zb3[:], A.subtract)
-
     local_first = q < rf
     u, v = T.cf[:, 0:1], T.cg[:, 0:1]
+    nf2, ba = T.sc[:, 0:1], T.sc[:, 1:2]
     fline = rf < rg
-    first = u if fline else v
     nl, fst = T.ct3[:, 31:32], T.ct3[:, 15:16]
     na_, nq = T.lnt[:, 0:1], T.lnt[:, 1:2]
-    nf, c1, ba, cz = T.sc[:, 0:1], T.sc[:, 2:3], T.sc[:, 3:4], T.sc[:, 4:5]
     lo, hi = (slice(0, 16), slice(16, 32)) if even else (slice(16, 32), slice(0, 16))
-
-    def pick_late():
-        g.vector.wait_ge(s.xw, 64)
-        g.vector.wait_ge(s.aS0, 2 * ncp)
-        return cpy(b32(T.plq[:]), b32(T.xwq[:]).indirect(T.offl[:]), noffl)
+    first, second = (u, v) if fline else (v, u)
+    t = T.tl[:]
+    x3 = T.pt3 if local_first else T.x3
+    nu = tr(T.tu[:, 512:960], T.winu[:, 512:960], nwin)
+    npt = np3 = scan(T.pt3[:], T.zt3[:, 0:32], T.car3[:], n3)
+    nm3 = tt(T.m3[:], T.dd[:], T.zb3[:], A.subtract, nzb)
+    tt(T.yu[:, 64:80], T.tu[:, 448:960:32], T.tu[:, 464:960:32], A.max, nu)
+    nu = tt(T.yu[:, 96:112], T.tu[:, 448:960:32], T.tu[:, 464:960:32], A.max)
+    nrx3 = ts(T.rexp3[:], T.half[:], T.pt3[:, 31:32], 1.0, A.mult, A.add, d=npt)
+    g.vector.wait_ge(s.aCNT, nmf)
+    if not local_first:
+        n = ts(nf2, u, v, 2.0, A.add, A.mult)
+    nba = 0 if fline else ts(ba, v, -1.0, C1 - 1.0, A.mult, A.add)
+    nu = tr(T.ytu[:, 64:128], T.yu[:, 64:128], nu)
+    if not local_first:
+        np3 = ts(T.x3[:], T.pt3[:], nf2, None, A.add, d=n)
+    g.vector.wait_ge(s.wl, 16)
+    nwq = V(lambda: g.vector.quantize_mx(T.wq[:], T.ws[:], T.wt[:]))
+    nu = tr(T.yuu[:, 32:64], T.ytu[:, 64:128:2], nu)
+    n3 = ts(T.w3[:], x3[:], float(S_), 1.0 - S_, A.is_ge, A.mult, d=np3)
+    nc3 = tr(T.ct3[:], T.rexp3[:], nrx3)
+    nc = tt(T.lc[U, :], T.dfl[U, :], T.yuu[U, 32:48], A.max, max(nu, ndfl))
+    n3 = tt(T.y3[:], x3[:], T.w3[:], A.add, n3)
     if local_first:
-        n3 = tt(T.a3[:], T.pt3[:], T.m3[:], A.max, max(np3, nm3))
-        vsa(nrx3)
-        nc3 = tr(T.ct3[:], T.rexp3[:])
-        n3 = tr(T.h3[:], T.a3[:], n3)
-        npl = pick_late()
-        cpy(T.o3[L, :], T.h3[L, lo], n3)
-        no3 = cpy(T.o3[U, :], T.h3[U, hi])
-        g.vector.wait_ge(s.aCNT, nmf)
-        nnf = tt(nf, u, v, A.add)
-        cs = T.sc[:, 1:2]
-        ncs = tt(cs, nl, first, A.add, nc3)
-        ts(c1, nl, -1.0 if fline else 1.0, 0.0 if fline else C1 - 1.0, A.mult, A.add)
-        nna = tt(na_, nl, nf, A.add, nnf)
-        n1 = ts(ba, cs, nl, C1 - 1.0, A.add, A.add, d=ncs)
+        nt = ts(t, T.i48[:], nl, first, A.subtract, A.subtract, d=nc3)
     else:
-        cs, ncs = first, 0
-        c1 = 0.0 if fline else C1 - 1.0
-        g.vector.wait_ge(s.aCNT, nmf)
-        n = ts(T.nf2[:], u, v, 2.0, A.add, A.mult)
-        nnf = tt(nf, u, v, A.add)
-        vsa(nrx3)
-        nc3 = tr(T.ct3[:], T.rexp3[:])
-        np3 = ts(T.x3[:], T.pt3[:], T.nf2[:], None, A.add, d=max(n, np3))
-        n1 = ts(ba, cs, C1 - 1.0, None, A.add)
-        nna = tt(na_, nl, nf, A.add, max(nnf, nc3))
-        n3 = tt(T.a3[:], T.x3[:], T.m3[:], A.max, max(np3, nm3))
-        npl = pick_late()
-        n3 = tr(T.h3[:], T.a3[:], n3)
-        nw = cpy(nq, fst) if even else tt(nq, nl, fst, A.subtract)
-    ncz = ts(cz, na_, -4096.0, 4096.0, A.mult, A.add, d=nna)
-    if local_first:
-        nw = cpy(nq, fst) if even else tt(nq, nl, fst, A.subtract)
-    else:
-        cpy(T.o3[L, :], T.h3[L, lo], n3)
-        no3 = cpy(T.o3[U, :], T.h3[U, hi])
-    nln = max(nna, nw)
+        nt = ts(t, T.i48[:], first, None, A.subtract)
+    ts(T.offl[L, :], T.lc[U, :], LS, None, A.add, d=nc)
+    noffl = ts(T.offl[U, :], T.lc[U, :], LS, None, A.add)
+    n3 = tr(T.h3[:], T.y3[:], n3)
+    g.vector.wait_ge(s.xw, 32)
+    g.vector.wait_ge(s.aS0, 2 * ncp)
+    npl = cpy(b32(T.plq[:]), b32(T.xwq[:]).indirect(T.offl[:]), noffl)
     wait("a", g.scalar, "sv", noffl)
-    g.scalar.wait_ge(s.xw, 64)
+    g.scalar.wait_ge(s.xw, 32)
     g.scalar.wait_ge(s.aS0, 2 * ncp)
     nal = SA(lambda: g.scalar.activation(T.pls[:], T.xws[:].indirect(T.offl[:]), AF.Copy))
-    act(T.res0[:, ZC:RW], T.zero[:, 0:32])
-    nres = act(T.res1[:, ZC:RW], T.zero[:, 0:32])
-    wait("s", g.sync, "sa", nvx)
-    g.sync.wait_ge(s.aSL, ncp)
-    for k in range(4, 8):
-        h = k % 2
-        g.sync.dma_start(T.valx[16 * k:16 * k + 1, :], T.slin[0:16, 16 * h:16 * h + 16]).then_inc(s.vps, 16)
 
     wait("g", g, "sv", npl)
     send(cf_, b8(T.llq[:]), b8(T.plq[:]), "aL")
     wait("g", g, "sa", nal)
     send(cf_, T.lls[:], T.pls[:], "aL")
 
-    ii = T.i48[:]
-    act(T.fl1[:], ii, n1, f=AF.Identity, scale=1.0 if fline else -1.0, bias=c1)
-    act(T.fd[:], ii, f=AF.Identity, scale=-2.0, bias=ba)
-    nfz = act(T.fz[:], ii, ncz, f=AF.Relu, scale=4096.0, bias=cz)
-    vsa(nvx)
+    n3 = tt(T.a3[:], T.h3[:], T.m3[:], A.max, max(n3, nm3))
+    if fline:
+        ts(T.la[:], t, u, 0.0, A.add, A.max, d=nt)
+    else:
+        ts(T.la[:], t, -1.0, ba, A.mult, A.add, d=max(nt, nba))
+    nwa = ts(T.wa[:], t, 0.0, BIG if fline else -BIG, A.is_ge, A.mult)
+    cpy(T.o3[L, :], T.a3[L, lo], n3)
+    no3 = cpy(T.o3[U, :], T.a3[U, hi])
+    nwb = ts(T.wb[:], t, second, BIG, A.is_ge, A.mult)
+    lb, nlb = t, nwb
+    if fline:
+        lb, nlb = T.lb[:], ts(T.lb[:], t, -1.0, C1 - 1.0, A.mult, A.add)
     g.vector.wait_ge(s.vps, 64)
-    g.vector.wait_ge(s.wf, 32)
-    n = cpy(T.winf[:].indirect(T.o3[:]), T.valx[:], no3)
-    nst = ts(T.fst[:], ii, cs, None, A.is_ge, d=ncs)
-    nw = tr(T.tf[:], T.winf[:, 0:1536], n)
-    vsa(nfz)
-    nst = tt(T.fsd[:], T.fst[:], T.fd[:], A.mult, nst)
-    for o in (0, 32):
-        tt(T.yf[:, o:o + 32], T.tf[:, 0:1024:32], T.tf[:, 16:1024:32], A.add, nw)
-    for o in (64, 96):
-        nw = tt(T.yf[:, o:o + 16], T.tf[:, 1024:1536:32], T.tf[:, 1040:1536:32], A.add)
-    nst = tt(T.ff[:], T.fl1[:], T.fsd[:], A.add if fline else A.subtract, nst)
+    vsa(nwf)
+    n = cpy(T.winf[:].indirect(T.o3[:]), T.valb[:], no3)
+    tt(T.ma[:], T.la[:], T.wa[:], A.max if fline else A.add, nwa)
+    nw = tr(T.tf[:], T.winf[:, 0:S_], n)
+    nm = tt(T.mb[:], lb, T.wb[:], A.max, nlb)
+    g.vector.wait_ge(s.sg, 6)
+    tt(T.yf[:, 0:24], T.tf[:, 0:S_:32], T.tf[:, 16:S_:32], A.min, nw)
+    nw = tt(T.yf[:, 32:56], T.tf[:, 0:S_:32], T.tf[:, 16:S_:32], A.min)
+    nm = tt(T.fm[:], T.ma[:], T.mb[:], A.min if fline else A.max, nm)
     nw = tr(T.ytf[:], T.yf[:], nw)
-    nst = tt(T.fm[:], T.ff[:], T.fz[:], A.max, nst)
-    nw = tr(T.yff[:], T.ytf[:, 0:128:2], nw)
-    ts(T.sw[L, :], T.yff[U, 0:48], -LOC - FB, None, A.add, d=nw)
-    n = ts(T.sw[U, :], T.yff[L, 0:48], -LOC - FB, None, A.add)
-    n = tt(T.fl[:], T.yff[:, 0:48], T.sw[:], A.add, n)
-    n = tt(T.fl2[:], T.fl[:], T.fm[:], A.min, max(n, nst))
-    noff = ts(T.offf[:], T.fl2[:], float(FB), float(ZC), A.add, A.min, d=n)
+    nh = ts(T.fh[:], T.fm[:], T.hf[:], None, A.add, d=nm)
+    tr(T.yff[:, 0:32], T.ytf[:, 0:64:2], nw)
+    nw = tr(T.yff[:, 32:64], T.ytf[:, 1:64:2])
+    ts(na_, u, v, nl, A.add, A.add, d=nc3)
+    ts(T.sw[L, :], T.yff[U, :], 256.0, None, A.add, d=nw)
+    ts(T.sw[U, :], T.yff[L, :], -256.0, None, A.add)
+    n = tt(T.fl[:], T.yff[:], T.fh[:], A.min, nh)
+    nln = cpy(nq, fst) if even else tt(nq, nl, fst, A.subtract)
+    n = tt(T.fl2[:], T.fl[:], T.sw[:], A.min, n)
+    noff = ts(T.offf[:], T.fl2[:], T.ho[:], float(ZC), A.add, A.min, d=n)
 
     def mm(bank, o, qb, sbuf, a, n):
         g.tensor.matmul_mx(T.ps[:, 512 * bank:512 * bank + n], T.wq[:, 128 * o:128 * o + 128], T.ws[:, 128 * o:128 * o + 128],
@@ -400,10 +383,13 @@ def rank_program(g, core, T, topo):
     nlast = act(res[1][:, base[3]:base[3] + 256], T.ps[:, 512 * 7:512 * 7 + 256])
     wait("v", g.vector, "st", 7)
     n = cpy(res[0][:, base[3]:base[3] + 256], T.ps[:, 512 * 6:512 * 6 + 256])
-    vsa(max(ncop, nres))
+    g.vector.wait_ge(s.sg, 8)
+    g.scalar.wait_ge(s.sg, 8)
+    vsa(ncop)
     for k in range(len(CUTS) - 1):
         a, b = CUTS[k], CUTS[k + 1]
-        of = T.offf[:, a // 16:b // 16]
+        c = a // 16 + (8 if a >= S_ // 2 else 0)
+        of = T.offf[:, c:c + (b - a) // 16]
         n0 = cpy(T.yt_0[:, a:b], T.res0[:].indirect(of), max(n, noff))
         n1 = SA(lambda: g.scalar.activation(T.yt_1[:, a:b], T.res1[:].indirect(of), AF.Copy), noff, nlast)
         if k == 0:

import numpy as np
from concourse.bass import DstId, RemoteDMATransfer
from concourse.mybir import dt, AluOpType, AxisListType, ActivationFunctionType

T_, S_, C0, C1 = 512, 768, 256, 480
EARLY = C1 - C0
OWN = T_ - EARLY
FB = T_ + C0
RW = FB + C1 + 32
ZC = FB + C1
CUTS = (0, 128, 384, 768)
FAR = 16 * 127 + 16
LS = 256.0 + C0 - EARLY
NONE = 4096.0
BIG = 8192.0

F32, I32, U16, BF = "float32", "int32", "uint16", "bfloat16"
Q4, U8 = "float8_e4m3fn_x4", "uint8"


def sb(n, d):
    return ("sbuf", [128, n], d)


SCRATCH = {
    "dmt": sb(68, I32),
    "xt": sb(2048, BF), "wt": sb(1024, BF),
    "xq": sb(512, Q4), "xs": sb(512, U8), "wq": sb(256, Q4), "ws": sb(256, U8),
    "xwq": sb(C0 + OWN, Q4), "xws": sb(C0 + OWN, U8),
    "p0q": sb(256, Q4), "p0s": sb(256, U8),
    "peq": sb(EARLY, Q4), "pes": sb(EARLY, U8), "plq": sb(256, Q4), "pls": sb(256, U8),
    "leq": sb(EARLY, Q4), "les": sb(EARLY, U8), "llq": sb(256, Q4), "lls": sb(256, U8),
    "one": sb(32, F32), "half": sb(32, F32), "hpm": sb(32, F32), "cb": sb(1, F32), "sgn": sb(1, F32),
    "ho": sb(1, F32), "hf": sb(1, F32),
    "pi": sb(2, I32), "pint": sb(8, I32), "pf": sb(8, F32),
    "val0": sb(256, BF), "valb": sb(256, BF), "dd0": sb(32, F32), "dd": sb(32, F32), "i480": sb(64, F32), "i48": sb(64, F32),
    "dfl": sb(16, F32),
    "ta": sb(16, I32), "tb": sb(16, I32), "td": sb(32, I32),
    "z0": sb(96, F32), "zt0": sb(64, F32), "car0": sb(1, F32), "pt0": sb(32, F32), "zb0": sb(32, F32), "m0": sb(32, F32),
    "a0": sb(32, F32), "h0": sb(32, F32), "hm": sb(32, F32), "o0": sb(16, U16), "slt": sb(32, F32),
    "z3": sb(96, F32), "zt3": sb(64, F32), "car3": sb(1, F32), "pt3": sb(32, F32), "zb3": sb(32, F32), "m3": sb(32, F32),
    "x3": sb(32, F32), "w3": sb(32, F32), "y3": sb(32, F32), "a3": sb(32, F32), "h3": sb(32, F32), "o3": sb(16, U16),
    "winu": sb(1024 + FAR, BF), "tu": sb(960, BF), "yu": sb(128, F32), "ytu": sb(128, F32), "yuu": sb(64, F32),
    "off0": sb(16, U16), "offu": sb(14, U16),
    "winf": sb(1024 + FAR, BF), "tf": sb(S_, BF), "yf": sb(64, F32), "ytf": sb(64, F32), "yff": sb(64, F32), "sw": sb(64, F32),
    "slu": sb(32, BF), "slin": sb(32, BF),
    "rexp": sb(32, F32), "ct": sb(32, F32), "cuv": sb(8, F32), "rexp3": sb(32, F32), "ct3": sb(32, F32),
    "cf": sb(4, F32), "cg": sb(4, F32),
    "lc": sb(16, F32), "offl": sb(16, U16),
    "sc": sb(16, F32), "lnt": sb(2, F32),
    "tl": sb(64, F32), "la": sb(64, F32), "wa": sb(64, F32), "lb": sb(64, F32), "wb": sb(64, F32),
    "ma": sb(64, F32), "mb": sb(64, F32), "fm": sb(64, F32), "fh": sb(64, F32), "fl": sb(64, F32), "fl2": sb(64, F32),
    "offf": sb(64, U16),
    "res0": sb(RW, F32), "res1": sb(RW, F32), "yt_0": sb(768, F32), "yt_1": sb(768, F32),
    "ps": ("psum", [128, 4096], F32),
}
SEMAPHORES = ["sv", "sa", "st", "sg", "dml", "xl0", "xl1", "wl", "xw", "vps", "yst",
              "aDM", "aS0", "aSL", "aCNT", "aE", "aL", "loc"]


def rank_program(g, core, T, topo):
    q = T.rank_of(core)
    if q is None:
        return
    A = AluOpType
    AF = ActivationFunctionType
    X = AxisListType.X
    rp, rf, rg = q ^ 1, q ^ 2, q ^ 3
    cp, cf_, cg_ = T.cores[rp], T.cores[rf], T.cores[rg]
    P, Fb, G, Qb = 1 << rp, 1 << rf, 1 << rg, 1 << q
    s = T.sem
    cnt = {"sv": 0, "sa": 0, "st": 0, "loc": 0}
    seen = {}
    L, U = slice(0, 64), slice(64, 128)

    def wait(name, eng, sem, n):
        if n > 0 and seen.get((name, sem), 0) < n:
            seen[(name, sem)] = n
            eng.wait_ge(s[sem], n)

    def V(ins, d=0):
        wait("v", g.vector, "sv", d)
        r = ins()
        cnt["sv"] += 1
        r.then_inc(s.sv, 1)
        return cnt["sv"]

    def SA(ins, v=0, a=0):
        wait("a", g.scalar, "sv", v)
        wait("a", g.scalar, "sa", a)
        r = ins()
        cnt["sa"] += 1
        r.then_inc(s.sa, 1)
        return cnt["sa"]

    def vsa(n):
        wait("v", g.vector, "sa", n)

    def ts(out, in0, s1, s2, op0, op1=None, d=0):
        if op1 is None:
            return V(lambda: g.vector.tensor_scalar(out, in0, s1, s2, op0), d)
        return V(lambda: g.vector.tensor_scalar(out, in0, s1, s2, op0, op1), d)

    def tt(out, a, b, op, d=0):
        return V(lambda: g.vector.tensor_tensor(out, a, b, op), d)

    def cpy(out, in_, d=0):
        return V(lambda: g.vector.tensor_copy(out, in_), d)

    def tr(out, in_, d=0):
        return V(lambda: g.vector.transpose(out, in_), d)

    def red(out, in_, d=0):
        return V(lambda: g.vector.tensor_reduce(out, in_, X, A.add), d)

    def scan(out, d1, init, d=0):
        return V(lambda: g.vector.tensor_tensor_scan(out, T.one[:], d1, init, A.mult, A.add), d)

    def fill(ap, c, d=0):
        return V(lambda: g.vector.memset(ap, c), d)

    def act(out, in_, v=0, a=0, f=AF.Copy, scale=None, bias=None):
        kw = {}
        if scale is not None:
            kw["scale"] = scale
        if bias is not None:
            kw["bias"] = bias
        return SA(lambda: g.scalar.activation(out, in_, f, **kw), v, a)

    def send(dst, out, in_, rsem):
        rid, pid, _se = topo.addr(dst)
        g.remote_dma(out_ap=out, in_ap=in_, remote_sem=s[rsem], local_sem=s.loc, pid=pid, routing_id=rid,
                     dma_engine_mask=topo.mask(core, dst))
        cnt["loc"] += len(topo.engines(core, dst))

    ncp, nmf = len(topo.engines(core, cp)), len(topo.engines(core, cf_))

    def b8(ap):
        return ap.bitcast(dt.uint8)

    def b32(ap):
        return ap.bitcast(dt.uint32)

    even = q < rp
    ob = 4 if even else 36
    for k in range(8):
        e = g.sync if k % 2 == 0 else g.scalar
        o = ob - k % 2
        e.dma_start(T.dmt[16 * k:16 * k + 16, o:o + 32], T.dm[:, :]).then_inc(s.dml, 16)
    g.sync.dma_start(T.xt[:, 4 * EARLY:2048], T.x[:, 4 * EARLY:2048]).then_inc(s.xl0, 16)
    g.scalar.dma_start(T.xt[:, 0:4 * EARLY], T.x[:, 0:4 * EARLY]).then_inc(s.xl1, 16)
    g.scalar.dma_start(T.wt[:], T.w[:]).then_inc(s.wl, 16)

    FL = {"allow_small_or_imprecise_dtypes": True}
    g.iota(T.pi[:, 0:1], [[1, 1]], 0, 1).then_inc(s.sg, 1)
    g.iota(T.val0[:], [[32, 16], [1, 16]], -256, 0, **FL).then_inc(s.sg, 1)
    g.iota(T.dd0[:], [[0, 2], [16, 16]], 1024, 0, **FL).then_inc(s.sg, 1)
    g.iota(T.i480[:], [[S_ // 2, 2], [16, 32]], 0, 0, **FL).then_inc(s.sg, 1)
    g.wait_ge(s.dml, 128)
    send(cp, T.dmt[:, ob:ob + 31], T.dmt[:, ob:ob + 31], "aDM")
    g.iota(T.yu[:], [[0, 128]], 0, 0, **FL).then_inc(s.sg, 1)

    nwu = fill(T.winu[:, 0:512], -NONE)
    g.vector.wait_ge(s.sg, 1)
    ts(T.pint[:, 0:1], T.pi[:, 0:1], 16, None, A.bitwise_and)
    n = ts(T.pint[:, 1:2], T.pi[:, 0:1], 15, None, A.bitwise_and)
    fill(T.one[:], 1.0)
    fill(T.z0[L, 31:32], C0 / 16.0)
    npf = cpy(T.pf[:, 0:2], T.pint[:, 0:2], n)
    fill(T.z0[U, 31:32], -2.0 / 32)
    fill(T.z0[U, 48:64], 0.0)
    fill(T.sgn[L, :], -2.0)
    nsgn = fill(T.sgn[U, :], 2.0)
    g.vector.wait_ge(s.sg, 2)
    ts(T.valb[:], T.val0[:], T.pf[:, 0:1], None, A.add, d=npf)

    act(T.winu[:, 512:960], T.winu[:, 0:448], nwu)
    nwf0 = act(T.winf[:, 0:512], T.winu[:, 0:512], scale=-1.0)

    g.vector.wait_ge(s.dml, 128)
    ts(T.ta[L, :], T.dmt[L, ob:ob + 31:2], G, None, A.bitwise_and)
    na = ts(T.ta[U, :], T.dmt[U, ob:ob + 31:2], Fb, None, A.bitwise_and)
    nb = ts(T.tb[L, :], T.dmt[L, ob:ob + 31:2], P | G, None, A.bitwise_and)
    fill(T.hpm[L, :], -0.5)
    ts(T.z0[:, 32:48], T.ta[:], 0.0, T.sgn[:], A.is_gt, A.mult, d=max(na, nsgn))
    nz = ts(T.z0[L, 48:64], T.tb[L, :], float(P), -2.0, A.is_equal, A.mult, d=nb)
    fill(T.hpm[U, :], 0.5)
    fill(T.cb[L, :], float(C0))
    n = scan(T.z0[:, 64:96], T.z0[:, 31:63], 0.0, nz)
    nzb = ts(T.zb0[:], T.z0[:, 32:64], 0.0, 65536.0, A.not_equal, A.mult)
    g.vector.wait_ge(s.sg, 3)
    ndd = ts(T.dd[:], T.dd0[:], T.pf[:, 1:2], None, A.add)
    n = tr(T.zt0[:], T.z0[:, 32:96], n)
    fill(T.cb[U, :], 1.0)
    fill(T.hm[:], 0.0)
    n = red(T.car0[:], T.zt0[:, 32:64], n)
    nm = tt(T.m0[:], T.dd[:], T.zb0[:], A.subtract, max(nzb, ndd))
    fill(T.half[:], 0.5)
    np0 = scan(T.pt0[:], T.zt0[:, 0:32], T.car0[:], n)
    fill(T.z3[:, 31:32], -2.0 / 32)
    fill(T.ho[L, :], 256.0)
    n = tr(T.h0[:], T.pt0[:], np0)
    nrx = ts(T.rexp[:], T.hpm[:], T.pt0[:, 31:32], T.cb[:], A.mult, A.add)
    fill(T.ho[U, :], 512.0)
    n = tt(T.a0[:], T.h0[:], T.m0[:], A.max, max(n, nm))
    nct = tr(T.ct[:], T.rexp[:], nrx)
    fill(T.hf[L, :], FB - 256.0)
    n = tt(T.hm[:, 0:16], T.a0[:, 0:16], T.a0[:, 16:32], A.min, n)
    fill(T.hf[U, :], FB - 512.0)
    g.vector.wait_ge(s.sg, 4)
    ni48 = ts(T.i48[:], T.i480[:], T.pf[:, 1:2], None, A.add)
    n = cpy(T.o0[:], T.hm[:, 0:16], n)
    nslt = tr(T.slt[:], T.hm[:])
    vsa(nwf0)
    nwin = cpy(T.winu[:].indirect(T.o0[:]), T.valb[:], n)
    act(T.cuv[L, 0:4], T.ct[L, 15:19], nct)
    nslu = act(T.slu[:], T.slt[:], nslt, scale=0.5)
    act(T.cuv[U, 0:4], T.ct[L, 15:19])
    act(T.cuv[L, 4:8], T.ct[U, 15:19])
    ncuv = act(T.cuv[U, 4:8], T.ct[U, 15:19])
    nwf = act(T.winf[:, 512:S_], T.winf[:, 0:S_ - 512], 0, nwf0)
    g.vector.wait_ge(s.xl0, 16)
    nxq0 = V(lambda: g.vector.quantize_mx(T.xq[:, EARLY:T_], T.xs[:, EARLY:T_], T.xt[:, 4 * EARLY:2048]))
    n = tr(T.tu[:, 0:512], T.winu[:, 0:512], nwin)
    ndfl = ts(T.dfl[:], T.i48[:, 0:16], -LS, None, A.add, d=ni48)
    g.vector.wait_ge(s.aDM, ncp)
    n3 = ts(T.td[:], T.dmt[:, 4:67:2], Qb, None, A.bitwise_and)
    g.vector.wait_ge(s.sg, 5)
    tt(T.yu[:, 0:16], T.tu[:, 0:512:32], T.tu[:, 16:512:32], A.max, n)
    n = tt(T.yu[:, 32:48], T.tu[:, 0:512:32], T.tu[:, 16:512:32], A.max)
    n3 = ts(T.z3[:, 32:64], T.td[:], 0.0, 2.0, A.is_gt, A.mult, d=n3)
    n = tr(T.ytu[:, 0:64], T.yu[:, 0:64], n)
    n3 = scan(T.z3[:, 64:96], T.z3[:, 31:63], 0.0, n3)
    ny = tr(T.yuu[:, 0:32], T.ytu[:, 0:64:2], n)
    g.vector.wait_ge(s.xl1, 16)
    V(lambda: g.vector.quantize_mx(T.xq[:, 0:EARLY], T.xs[:, 0:EARLY], T.xt[:, 0:4 * EARLY]))
    ts(T.off0[L, :], T.yuu[L, 0:16], 256.0, None, A.add, d=ny)
    noff0 = ts(T.off0[U, :], T.yuu[L, 0:16], 256.0, None, A.add)
    ts(T.offu[L, :], T.yuu[U, 0:14], 256.0, None, A.add)
    n3 = tr(T.zt3[:], T.z3[:, 32:96], n3)
    nq0 = cpy(b32(T.p0q[:]), b32(T.xq[:]).indirect(T.off0[:]), noff0)
    na0 = SA(lambda: g.scalar.activation(T.p0s[:], T.xs[:].indirect(T.off0[:]), AF.Copy), noff0)
    noffu = ts(T.offu[U, :], T.yuu[U, 0:14], 256.0, None, A.add)
    n3 = red(T.car3[:], T.zt3[:, 32:64], n3)
    nzb = ts(T.zb3[:], T.z3[:, 32:64], 0.0, 65536.0, A.not_equal, A.mult)
    npe = cpy(b32(T.peq[:]), b32(T.xq[:]).indirect(T.offu[:]), noffu)
    nae = SA(lambda: g.scalar.activation(T.pes[:], T.xs[:].indirect(T.offu[:]), AF.Copy), noffu)

    wait("s", g.sync, "sv", nxq0)
    g.sync.dma_start(b8(T.xwq[:, C0:C0 + OWN]), b8(T.xq[:, EARLY:T_])).then_inc(s.xw, 16)
    g.sync.dma_start(T.xws[:, C0:C0 + OWN], T.xs[:, EARLY:T_]).then_inc(s.xw, 16)
    g.sync.wait_ge(s.aSL, ncp)
    for k in range(4, 8):
        h = k % 2
        g.sync.dma_start(T.valb[16 * k:16 * k + 1, :], T.slin[0:16, 16 * h:16 * h + 16]).then_inc(s.vps, 16)

    wait("g", g, "sa", nslu)
    send(cp, T.slin[:], T.slu[:], "aSL")
    wait("g", g, "sa", ncuv)
    trs = []
    for dst, land, c, h in ((cf_, T.cf, 4, 0), (cg_, T.cg, 0, 1)):
        en = topo.engines(core, dst)
        en = en[:len(en) // 2] if h == 0 else en[len(en) // 2:]
        rid, pid, _se = topo.addr(dst)
        trs.append(RemoteDMATransfer(dst_ids=[DstId(rid=rid, pnc=pid)], dma_engine_mask=sum(1 << e for e in en),
                                     remote_sem=s.aCNT, src=T.cuv[:, c:c + 4], dst=land[:]))
        cnt["loc"] += len(en)
    g.remote_dma_fused(trs, local_sem=s.loc)
    for b, a, n in ((T.yf, 0, 64), (T.res0, ZC, 32), (T.res1, ZC, 32)):
        g.iota(b[:, a:a + n], [[0, n]], 0, 0, **FL).then_inc(s.sg, 1)
    wait("g", g, "sv", nq0)
    send(cp, b8(T.xwq[:, 0:C0]), b8(T.p0q[:]), "aS0")
    wait("g", g, "sa", na0)
    send(cp, T.xws[:, 0:C0], T.p0s[:], "aS0")
    wait("g", g, "sv", npe)
    send(cf_, b8(T.leq[:]), b8(T.peq[:]), "aE")
    wait("g", g, "sa", nae)
    send(cf_, T.les[:], T.pes[:], "aE")

    local_first = q < rf
    u, v = T.cf[:, 0:1], T.cg[:, 0:1]
    nf2, ba = T.sc[:, 0:1], T.sc[:, 1:2]
    fline = rf < rg
    nl, fst = T.ct3[:, 31:32], T.ct3[:, 15:16]
    na_, nq = T.lnt[:, 0:1], T.lnt[:, 1:2]
    lo, hi = (slice(0, 16), slice(16, 32)) if even else (slice(16, 32), slice(0, 16))
    first, second = (u, v) if fline else (v, u)
    t = T.tl[:]
    x3 = T.pt3 if local_first else T.x3
    nu = tr(T.tu[:, 512:960], T.winu[:, 512:960], nwin)
    npt = np3 = scan(T.pt3[:], T.zt3[:, 0:32], T.car3[:], n3)
    nm3 = tt(T.m3[:], T.dd[:], T.zb3[:], A.subtract, nzb)
    tt(T.yu[:, 64:80], T.tu[:, 448:960:32], T.tu[:, 464:960:32], A.max, nu)
    nu = tt(T.yu[:, 96:112], T.tu[:, 448:960:32], T.tu[:, 464:960:32], A.max)
    nrx3 = ts(T.rexp3[:], T.half[:], T.pt3[:, 31:32], 1.0, A.mult, A.add, d=npt)
    g.vector.wait_ge(s.aCNT, nmf)
    if not local_first:
        n = ts(nf2, u, v, 2.0, A.add, A.mult)
    nba = 0 if fline else ts(ba, v, -1.0, C1 - 1.0, A.mult, A.add)
    nu = tr(T.ytu[:, 64:128], T.yu[:, 64:128], nu)
    if not local_first:
        np3 = ts(T.x3[:], T.pt3[:], nf2, None, A.add, d=n)
    g.vector.wait_ge(s.wl, 16)
    nwq = V(lambda: g.vector.quantize_mx(T.wq[:], T.ws[:], T.wt[:]))
    nu = tr(T.yuu[:, 32:64], T.ytu[:, 64:128:2], nu)
    n3 = ts(T.w3[:], x3[:], float(S_), 1.0 - S_, A.is_ge, A.mult, d=np3)
    nc3 = tr(T.ct3[:], T.rexp3[:], nrx3)
    nc = tt(T.lc[U, :], T.dfl[U, :], T.yuu[U, 32:48], A.max, max(nu, ndfl))
    n3 = tt(T.y3[:], x3[:], T.w3[:], A.add, n3)
    if local_first:
        nt = ts(t, T.i48[:], nl, first, A.subtract, A.subtract, d=nc3)
    else:
        nt = ts(t, T.i48[:], first, None, A.subtract)
    ts(T.offl[L, :], T.lc[U, :], LS, None, A.add, d=nc)
    noffl = ts(T.offl[U, :], T.lc[U, :], LS, None, A.add)
    n3 = tr(T.h3[:], T.y3[:], n3)
    g.vector.wait_ge(s.xw, 32)
    g.vector.wait_ge(s.aS0, 2 * ncp)
    npl = cpy(b32(T.plq[:]), b32(T.xwq[:]).indirect(T.offl[:]), noffl)
    wait("a", g.scalar, "sv", noffl)
    g.scalar.wait_ge(s.xw, 32)
    g.scalar.wait_ge(s.aS0, 2 * ncp)
    nal = SA(lambda: g.scalar.activation(T.pls[:], T.xws[:].indirect(T.offl[:]), AF.Copy))

    wait("g", g, "sv", npl)
    send(cf_, b8(T.llq[:]), b8(T.plq[:]), "aL")
    wait("g", g, "sa", nal)
    send(cf_, T.lls[:], T.pls[:], "aL")

    n3 = tt(T.a3[:], T.h3[:], T.m3[:], A.max, max(n3, nm3))
    if fline:
        ts(T.la[:], t, u, 0.0, A.add, A.max, d=nt)
    else:
        ts(T.la[:], t, -1.0, ba, A.mult, A.add, d=max(nt, nba))
    nwa = ts(T.wa[:], t, 0.0, BIG if fline else -BIG, A.is_ge, A.mult)
    cpy(T.o3[L, :], T.a3[L, lo], n3)
    no3 = cpy(T.o3[U, :], T.a3[U, hi])
    nwb = ts(T.wb[:], t, second, BIG, A.is_ge, A.mult)
    lb, nlb = t, nwb
    if fline:
        lb, nlb = T.lb[:], ts(T.lb[:], t, -1.0, C1 - 1.0, A.mult, A.add)
    g.vector.wait_ge(s.vps, 64)
    vsa(nwf)
    n = cpy(T.winf[:].indirect(T.o3[:]), T.valb[:], no3)
    tt(T.ma[:], T.la[:], T.wa[:], A.max if fline else A.add, nwa)
    nw = tr(T.tf[:], T.winf[:, 0:S_], n)
    nm = tt(T.mb[:], lb, T.wb[:], A.max, nlb)
    g.vector.wait_ge(s.sg, 6)
    tt(T.yf[:, 0:24], T.tf[:, 0:S_:32], T.tf[:, 16:S_:32], A.min, nw)
    nw = tt(T.yf[:, 32:56], T.tf[:, 0:S_:32], T.tf[:, 16:S_:32], A.min)
    nm = tt(T.fm[:], T.ma[:], T.mb[:], A.min if fline else A.max, nm)
    nw = tr(T.ytf[:], T.yf[:], nw)
    nh = ts(T.fh[:], T.fm[:], T.hf[:], None, A.add, d=nm)
    tr(T.yff[:, 0:32], T.ytf[:, 0:64:2], nw)
    nw = tr(T.yff[:, 32:64], T.ytf[:, 1:64:2])
    ts(na_, u, v, nl, A.add, A.add, d=nc3)
    ts(T.sw[L, :], T.yff[U, :], 256.0, None, A.add, d=nw)
    ts(T.sw[U, :], T.yff[L, :], -256.0, None, A.add)
    n = tt(T.fl[:], T.yff[:], T.fh[:], A.min, nh)
    nln = cpy(nq, fst) if even else tt(nq, nl, fst, A.subtract)
    n = tt(T.fl2[:], T.fl[:], T.sw[:], A.min, n)
    noff = ts(T.offf[:], T.fl2[:], T.ho[:], float(ZC), A.add, A.min, d=n)

    def mm(bank, o, qb, sbuf, a, n):
        g.tensor.matmul_mx(T.ps[:, 512 * bank:512 * bank + n], T.wq[:, 128 * o:128 * o + 128], T.ws[:, 128 * o:128 * o + 128],
                           qb[:, a:a + n], sbuf[:, a:a + n], True, True).then_inc(s.st, 1)
        cnt["st"] += 1
    g.tensor.wait_ge(s.sv, nwq)
    for bank, (qb, sbuf, a, n, sem, k) in enumerate(((T.xq, T.xs, 0, 512, None, 0), (T.xwq, T.xws, 0, 256, "aS0", 2 * ncp),
                                                     (T.leq, T.les, 0, EARLY, "aE", 2 * nmf), (T.llq, T.lls, 0, 256, "aL", 2 * nmf))):
        if sem:
            g.tensor.wait_ge(s[sem], k)
        for o in range(2):
            mm(2 * bank + o, o, qb, sbuf, a, n)
    res = (T.res0, T.res1)
    base = (0, T_, FB, FB + EARLY)
    width = (512, 256, EARLY, 256)
    for b in range(3):
        for o in range(2):
            wait("a", g.scalar, "st", 2 * b + o + 1)
            ncop = act(res[o][:, base[b]:base[b] + width[b]], T.ps[:, 512 * (2 * b + o):512 * (2 * b + o) + width[b]])
    wait("a", g.scalar, "st", 8)
    nlast = act(res[1][:, base[3]:base[3] + 256], T.ps[:, 512 * 7:512 * 7 + 256])
    wait("v", g.vector, "st", 7)
    n = cpy(res[0][:, base[3]:base[3] + 256], T.ps[:, 512 * 6:512 * 6 + 256])
    g.vector.wait_ge(s.sg, 8)
    g.scalar.wait_ge(s.sg, 8)
    vsa(ncop)
    for k in range(len(CUTS) - 1):
        a, b = CUTS[k], CUTS[k + 1]
        c = a // 16 + (8 if a >= S_ // 2 else 0)
        of = T.offf[:, c:c + (b - a) // 16]
        n0 = cpy(T.yt_0[:, a:b], T.res0[:].indirect(of), max(n, noff))
        n1 = SA(lambda: g.scalar.activation(T.yt_1[:, a:b], T.res1[:].indirect(of), AF.Copy), noff, nlast)
        if k == 0:
            wait("s", g.sync, "sv", nln)
            g.sync.dma_start(T.ln[:, :], T.lnt[0:1, :]).then_inc(s.yst, 16)
        wait("s", g.sync, "sv", n0)
        g.sync.dma_start(T.y[:, a:b], T.yt_0[:, a:b]).then_inc(s.yst, 16)
        wait("s", g.sync, "sa", n1)
        g.sync.dma_start(T.y[:, S_ + a:S_ + b], T.yt_1[:, a:b]).then_inc(s.yst, 16)
    g.sync.wait_ge(s.yst, 16 * (2 * len(CUTS) - 1))
    g.wait_ge(s.loc, cnt["loc"])
